import numpy as np, ml_dtypes
CORES = [23,119,17,113]
N = 4
BF = ml_dtypes.bfloat16
def gentries(a):
    return np.ascontiguousarray(a.reshape(8, 16, -1).transpose(0, 2, 1)).reshape(8, -1)
def gtable(e):
    e = np.asarray(e); return np.ascontiguousarray(e.reshape(8, -1, 16).transpose(0, 2, 1)).reshape(128, -1).astype(np.int32)
W, P, M, L, TV = 4096, 256, 16, 2, 5
def parts(rng):
    X = rng.integers(0, 256, (N, 8, 16, W))
    cen = rng.integers(0, 256, (N, 8, 16, 32)); pick = rng.integers(0, 32, (N, 8, 1, W))
    near = np.clip(np.take_along_axis(cen, pick, 3) + rng.integers(-20, 21, (N, 8, 16, W)), 0, 255)
    X[:, 1::2] = near[:, 1::2]
    Q = rng.integers(0, W, (N, 8, 16, W)); R = rng.integers(0, W, (N, 8, 16, P))
    R = np.where(rng.random((N, 8, 1, P)) < 0.0625, R[:, :, :1], R)
    return X, Q, R, rng.integers(1, 256, (N, 8, 16, 1)), rng.integers(0, 2048, (N, 8, M))
def pack(X, Q, R, w, ka):
    return {"xf": np.ascontiguousarray(X.reshape(N, 128, W)).astype(np.float32).astype(BF), "pa": np.ascontiguousarray(Q.reshape(N, 128, W)).astype(np.int32),
            "rp": np.ascontiguousarray(R.reshape(N, 128, P)).astype(np.int32), "wt": np.ascontiguousarray(w.reshape(N, 128, 1)).astype(np.int32), "kap": np.stack([gtable(a) for a in ka])}
def setup_inputs(rng):
    return pack(*parts(rng))
def setup_inputs_corners(rng):
    X, Q, R, w, ka = parts(rng); n = np.arange(W)[None, :]; k = np.arange(16)[:, None]; turn = int(rng.integers(0, 8))
    for a in range(N):
        for g in range(8):
            kind = (a + g + turn) % 8
            if kind == 0: Q[a, g] = n; w[a, g] = 255
            if kind == 1: Q[a, g] = 0; R[a, g, ::2] = 0
            if kind == 2: Q[a, g] = W - 1; R[a, g, 1::2] = W - 1
            if kind == 3: X[a, g] = int(rng.choice(np.array([0, 255, 100])))
            if kind == 4: ka[a, g] = ka[a, g, :1]
            if kind == 5: w[a, g] = 1; ka[a, g] = 0; ka[a, g, M - 1] = 2047
            if kind == 6: R[a, g] = R[a, g, :, :1]
            if kind == 7:
                R[a, g] = (R[a, g, :1] + k) & (W - 1); Q[a, g] = (n + k - 15) & (W - 1); X[a, g, :, 1::2] = X[a, g, :, ::2]
    q = int(rng.integers(0, N)); R[q] = R[q][:, :1].copy()
    return pack(X, Q, R, w, ka)
def setup_inputs_crowd(rng):
    X, Q, R, w, ka = parts(rng); o = rng.permutation(N); H = W // 4; B = W // P; hit = np.zeros((N, 8, P), bool)
    for a in range(N):
        for g in range(8):
            kind = int(rng.integers(0, 4)); hit[a, g] = (True, True, False, False)[kind]
            if kind == 1: hit[a, g, rng.integers(0, P)] = False
            if kind == 2: hit[a, g] = rng.random(P) < 0.5
    hit[o[0]] = True; hit[o[1]] = True; hit[o[1], rng.integers(0, 8), rng.integers(0, P)] = False
    hit[o[2]] = False; hit[o[3]] = False; hit[o[3], rng.integers(0, 8), rng.integers(0, P)] = True
    many = np.add.reduce(hit.reshape(N, 8 * P).astype(np.int64), axis=1); t = (int(o[2]) + 1) % N
    for g in range(8):
        for d in range(N):
            a = (t + d) % N; v = rng.integers(60, 190, 16); s = v + rng.choice(np.array([-50, 50]), 16); col = rng.permutation(W); plain = col[:H]
            if d == N - 1:
                plain, loc = keep
                X[a, g][:, plain] = v[:, None]; X[a, g][:, loc] = v
                R[a, g] = plain[rng.integers(0, H, (16, P))]; R[a, g, 1] = loc
                continue
            us = int(np.add.reduce(w[a, g, :, 0] * s)) & (W - 1); uv = int(np.add.reduce(w[a, g, :, 0] * v)) & (W - 1)
            z = ((us * us) >> 5) + int(ka[a, g, 0]) * us; c = z & (W - 1); c1 = (z + int(many[a])) & (W - 1)
            rest = col[H:]; rest = rest[(rest % B != us % B) & (rest % B != uv % B) & (rest != c) & (rest != c1)]; loc = int(rest[0])
            if d == 0: keep = (plain, loc)
            X[a, g][:, plain] = v[:, None]; X[a, g][:, c] = v; X[a, g][:, c1] = v; X[a, g][:, loc] = s; Q[a, g, 0, c] = plain[0]; Q[a, g, 0, c1] = plain[0]
            R[a, g] = plain[rng.integers(0, H, (16, P))]; R[a, g, 1] = np.where(hit[a, g], loc, R[a, g, 1])
    return pack(X, Q, R, w, ka)
def setup_inputs_ends(rng):
    X = 255 * rng.integers(0, 2, (N, 8, 16, W)); rec = 255 * rng.integers(0, 2, (N, 8, 1, W)); Q = (W - 1) * rng.integers(0, 2, (N, 8, 16, W))
    w = 1 + 254 * rng.integers(0, 2, (N, 8, 16, 1)); ka = 2047 * rng.integers(0, 2, (N, 8, M)); ka[:, :, 0] = 0; ka[:, :, M - 1] = 2047
    lo = (W - 1) * rng.integers(0, 2, (N, 8, 1, P))
    for a in range(N):
        for g in range(8): lo[a, g, 0, P - 1] = 0 if (a + g + 2) % 4 in (0, 1) else W - 1
    hi = W - 1 - lo; k = np.arange(16)[:, None]
    kind = rng.integers(0, 4, (N, 8, 1, P)); kind[..., P - 1] = 2; q = rng.integers(0, 16, (N, 8, 1, P))
    R = (W - 1) * rng.integers(0, 2, (N, 8, 16, P))
    R = np.where(kind == 1, np.where(k <= q, lo, hi), R); R = np.where(kind == 2, np.where(k == 1, hi, lo), R); R = np.where(kind == 3, rng.integers(0, W, (N, 8, 16, P)), R)
    for a in range(N):
        for g in range(8):
            role = (a + g + 2) % 4
            if role == 0 or role == 2:
                X[a, g] = rec[a, g]; X[a, g, :, 0] = 0 if role == 0 else 255; X[a, g, :, W - 1] = 255 - X[a, g, :, 0]
                if role == 0: w[a, g] = 255
                else:
                    u = (255 * int(np.add.reduce(w[a, g, :, 0]))) & (W - 1)
                    for kk in (0, 2047):
                        c = (((u * u) >> 5) + kk * u) & (W - 1)
                        if 0 < c < W - 1: X[a, g, :, c] = 255; Q[a, g, :, c] = W - 1
            else:
                o = rng.permutation(16); w[a, g, o[0], 0] = 255; w[a, g, o[1], 0] = 1; w[a, g, o[2], 0] = 1; top = W - 1 if role == 1 else 0
                v = np.zeros(16, np.int64); v[o[:3]] = 255; X[a, g, :, top] = v; X[a, g, :, W - 1 - top] = 255 - v
                if role == 1: ka[a, g] = 0; ka[a, g, M - 1] = 2047
                else:
                    f = 2 if g < 4 else 3; u = W - 1
                    ka[a, g, :f] = 0; ka[a, g, f] = 2047; ka[a, g, f + 1] = 1
                    for kk, i in ((0, -1), (2047, int(o[3])), (1, int(o[4]))):
                        c = (((u * u) >> 5) + kk * u) & (W - 1)
                        X[a, g, :, c] = v; Q[a, g, 0, c] = W - 1
                        if i >= 0: X[a, g, i, c] = 255 - v[i]
    return pack(X, Q, R, w, ka)
def setup_inputs_spread(rng):
    X, Q, R, w, ka = parts(rng); e = rng.choice(np.array([1, 2, 4, 8]), (N, 8, 1, 1)); back = rng.random((N, 8, 1, 1)) < 0.5
    X = np.minimum((np.exp2(8 * rng.random((N, 8, 1, W))) * np.exp2(-3 * rng.random((N, 8, 16, 1))) * (0.5 + rng.random((N, 8, 16, W)))).astype(np.int64), 255)
    Q = np.minimum((W * rng.random((N, 8, 16, W)) ** e).astype(np.int64), W - 1); Q = np.where(back, W - 1 - Q, Q)
    R = np.minimum((W * rng.random((N, 8, 16, P)) ** e[:, ::-1]).astype(np.int64), W - 1); R = np.where(back, R, W - 1 - R)
    w = np.minimum(np.exp2(8 * rng.random((N, 8, 16, 1))).astype(np.int64), 255); ka = np.minimum(np.exp2(11 * rng.random((N, 8, M))).astype(np.int64) - 1, 2047)
    return pack(X, Q, R, w, ka)
def brink(rng, X, Q, R, w, ka):
    pl = 4093 & (W - 1); v = rng.integers(60, 190, 16); w[0] = 16; w[1] = 1; ka[0] = 1929; ka[1] = 815
    goal = [4081 & (W - 1), 5]
    cs = [(((goal[m] * goal[m]) >> 5) + int(ka[m]) * goal[m]) & (W - 1) for m in range(2)]
    col = rng.permutation(W); col = col[(col != pl) & (col != cs[0]) & (col != cs[1]) & (col > 0) & (col < W - 1)][:5]
    X[:, pl] = v
    for m in range(2):
        s = v + rng.choice(np.array([-50, 50]), 16); rest = (goal[m] - int(np.add.reduce((w[:, 0] * s)[2:]))) & (W - 1); s[0] = rest >> 4; s[1] = rest & 15
        X[:, col[m]] = s; X[:, cs[m]] = v; Q[0, cs[m]] = pl; R[:, m::4] = pl; R[1, m::4] = col[m]
    X[:, col[2]] = 0; X[:, col[3]] = 255; X[:, col[4]] = 255; X[int(rng.integers(0, 16)), col[4]] = 254
    for j, way in ((2, (4, 2, 2, 3)), (3, (2, 4, 3, 2))):
        for k in range(4): R[k + 1, j::4] = col[way[k]]
def setup_inputs_ties(rng):
    X, Q, R, w, ka = parts(rng); turn = int(rng.integers(0, 8))
    for a in range(N):
        for g in range(8):
            if (a + g + turn) % 8 == 7:
                brink(rng, X[a, g], Q[a, g], R[a, g], w[a, g], ka[a, g])
                continue
            top = int(rng.choice(np.array([1, 2, 3]))); o = rng.permutation(16)[:3]; v = rng.integers(0, 252, 16)
            X[a, g] = v[:, None]; X[a, g, o] = v[o][:, None] + rng.integers(0, top + 1, (3, W))
    return pack(X, Q, R, w, ka)
def check_inputs(d):
    bad = []
    for k, lo, hi in (("xf", 0, 255), ("pa", 0, W - 1), ("rp", 0, W - 1), ("wt", 1, 255), ("kap", 0, 2047)):
        v = np.asarray(d[k]).astype(np.float64)
        if not np.all((v >= lo) & (v <= hi)): bad.append("range of " + k)
        elif not np.all(v == np.floor(v)): bad.append("whole numbers in " + k)
    return bad
def reference(xf, pa, rp, wt, kap):
    X = xf.astype(np.float32).astype(np.int32).reshape(N, 8, 16, W); Q = pa.astype(np.int64).reshape(N, 8, 16, W); R = rp.astype(np.int64).reshape(N, 8, 16, P)
    w = wt.astype(np.int64).reshape(N, 8, 16, 1); ka = np.stack([gentries(a) for a in kap]).astype(np.int64); A = np.zeros(N, np.int64)
    k = np.arange(16)[:, None]; B = W // P
    for v in range(TV):
        S = np.roll(R, v, axis=0)
        x = np.take_along_axis(X, S.reshape(N, 8, 1, 16 * P), 3).reshape(N, 8, 16, 16, P)
        D = np.add.reduce(np.abs(x[:, :, :, 2:16 - L] - x[:, :, :, 1:15 - L]), axis=2)
        p = 1 + np.argmax(D, axis=2)
        xt = [np.take_along_axis(x, (p + j)[:, :, None, None, :], 3)[:, :, :, 0] for j in range(L + 1)]
        u = np.add.reduce(w * xt[0], axis=2) & (W - 1)
        c = (((u * u) >> 5)[:, :, None] + ka[..., None] * u[:, :, None] + A[:, None, None, None]) & (W - 1)
        anc = np.take_along_axis(Q, c.reshape(N, 8, 1, M * P), 3).reshape(N, 8, 16, M, P)
        b = np.take_along_axis(anc, (p - 1)[:, :, None, None, :], 2)[:, :, 0]
        pk = p[:, :, None]
        cc = np.concatenate([np.take_along_axis(S, pk, 2), c], axis=2); bb = np.concatenate([np.take_along_axis(S, pk - 1, 2), b], axis=2)
        Xc = np.take_along_axis(X, cc.reshape(N, 8, 1, -1), 3).reshape(N, 8, 16, M + 1, P); Xb = np.take_along_axis(X, bb.reshape(N, 8, 1, -1), 3).reshape(N, 8, 16, M + 1, P)
        E = np.zeros((N, 8, M + 1, P), np.int64)
        for j in range(1, L + 1):
            E = E + np.add.reduce(np.abs(Xc + j * (Xc - Xb) - xt[j][:, :, :, None, :]), axis=2)
        m = np.argmin(E, axis=2)
        win = np.take_along_axis(cc, m[:, :, None], 2)
        pre = np.take_along_axis(anc, np.maximum(m - 1, 0)[:, :, None, None, :], 3)[:, :, :, 0]
        late = (((S * win) >> 5) + S + 37 * k) & (W - 1)
        new = np.where(k < pk, pre, np.where(k == pk, win, np.where(k > pk + L, late, S)))
        S2 = np.where((m > 0)[:, :, None], new, S)
        mid = (np.take_along_axis(Xc, m[:, :, None, None, :], 3)[:, :, :, 0] + xt[1]) >> 1
        n = np.broadcast_to((B * np.arange(P) + (u & (B - 1)))[:, :, None], (N, 8, 16, P))
        np.put_along_axis(Q, n, S2, 3); np.put_along_axis(X, n, mid, 3)
        A = np.add.reduce((m > 0).astype(np.int64).reshape(N, 8 * P), axis=1)
        R = np.roll(S2, -v, axis=0)
    return {"yr": R.reshape(N, 128, P).astype(np.float32), "yq": np.add.reduce((k + 1) * Q, axis=2).astype(np.float32), "yx": np.add.reduce((k + 1) * X, axis=2).astype(np.float32)}

@@ -1,0 +1,652 @@
+import numpy as np
+from concourse.mybir import AluOpType, ActivationFunctionType
+
+ALU = AluOpType
+AF = ActivationFunctionType
+F32, BF, F16, I32, U16 = "float32", "bfloat16", "float16", "int32", "uint16"
+NV = 5
+BIG = 32768.0
+QSH = 2048.0
+
+SCRATCH = {}
+
+
+def _sb(name, cols, dtype):
+    SCRATCH[name] = ("sbuf", [128] + list(cols), dtype)
+
+
+_sb("X", [4096], BF); _sb("Qw", [4352], F32); _sb("Iw", [4352], F32); _sb("qi", [4096], I32); _sb("ri", [256], I32)
+_sb("r16", [256 * NV], U16); _sb("s16", [256 * (NV - 1)], U16)
+_sb("wti", [1], I32); _sb("kpi", [1], I32)
+for _h in "01":
+    _sb("xs" + _h, [2048], BF); _sb("adD" + _h, [8, 12, 16], BF); _sb("scD" + _h, [96], F32); _sb("vJ" + _h, [48], I32)
+    _sb("off" + _h, [48], U16); _sb("xc" + _h, [2176], BF); _sb("x12" + _h, [384], BF); _sb("mk" + _h, [256], BF)
+    _sb("sq" + _h, [16], I32); _sb("ku" + _h, [128], F32); _sb("cs" + _h, [128], I32); _sb("ct" + _h, [136], I32)
+    _sb("co" + _h, [128], U16); _sb("anc" + _h, [2048], F16); _sb("bo" + _h, [128], U16); _sb("sp" + _h, [2176], F16)
+    _sb("adA" + _h, [2, 8, 8, 16], F16); _sb("adB" + _h, [2, 8, 9, 16], F16); _sb("sc" + _h, [136], F32)
+    _sb("mq" + _h, [8], I32); _sb("wo" + _h, [24], U16); _sb("mid" + _h, [128], I32); _sb("cm" + _h, [256], F32)
+    _sb("nm" + _h, [5, 128], F32); _sb("ni" + _h, [2, 128], I32); _sb("pv" + _h, [48], I32); _sb("po" + _h, [48], U16)
+_sb("ui", [16], I32); _sb("ne", [16], I32); _sb("no", [16], U16); _sb("s2f", [256], F32); _sb("sg", [16], BF)
+_sb("col", [8, 8], F32); _sb("pi", [16], I32); _sb("lst", [32], U16); _sb("Jc", [48], F32); _sb("tf", [128], F32)
+_sb("cD", [96], F16); _sb("rsD", [96], F32); _sb("cE", [136], BF); _sb("rsE", [136], F32); _sb("rs16", [128], F32)
+_sb("MW", [128], BF); _sb("Wa", [64], BF); _sb("Wb", [64], BF); _sb("Kw", [64], F32); _sb("dd", [3, 64], F32)
+_sb("Z", [4, 144], BF); _sb("Qh", [4096], F16); _sb("Id", [6, 128], BF); _sb("one", [128], BF); _sb("BO", [128], BF)
+_sb("kr", [128], F16); _sb("kapE", [128], F32); _sb("nb", [16], F32); _sb("ec", [256], F32); _sb("junk", [16], F32)
+_sb("ei", [16], I32); _sb("eq", [2, 256], F32); _sb("pre", [2, 256], F32); _sb("nw", [2, 256], F16); _sb("n0", [32], F32)
+_sb("nsb", [32], F32); _sb("fin", [2, 256], F32); _sb("yrf", [256], F32)
+for _b in "012":
+    SCRATCH["pb" + _b] = ("psum", [128, 2, 8, 4, 16], F32)
+for _h in "01":
+    SCRATCH["pq" + _h] = ("psum", [128, 512], F32)
+
+SEMAPHORES = ["cv", "ca", "cp", "cg", "lr", "lx", "lq0", "lq1", "lq2", "lq3", "lw", "sent", "o0", "o1", "o2", "o3"] + \
+             ["ar%d%d" % (v, h) for v in range(1, NV) for h in range(2)]
+COUNTER = {"v": "cv", "a": "ca", "p": "cp", "g": "cg"}
+
+CYC, PEC, GAT, SCA = 1.04, 0.52, 1.56, 3.8
+LAT_X, LAT_S, HOP = 120.0, 80.0, 3200.0
+P = {"sp": ["vvvvv", "vvvvv"]}
+PERIOD = 3500
+RANK = [-9012,-9010,-9008,-9006,-9004,-9002,52,-68,162,-242,646,-1980,-272,670,1036,1054,356,-798,-282,916,918,974,-768,734,298,1033,2284,2274,449,1062,928,1342,990,1206,1014,524,686,990,202,1558,76,-66,798,1216,5908,6326,20,150,130,514,1060,1348,1666,2168,480,-800,642,1652,2476,2763,3540,1824,106,-1260,834,-656,2200,2464,4712,7558,7608,7848,-864,1748,1937,3117,3434,3193,3214,1248,819,1220,1283,130,1518,1212,-146,2320,962,1842,980,502,2280,3344,1942,820,1108,2350,1990,3434,3340,2394,3674,3668,3362,1562,1188,438,1810,2612,3678,2886,2334,2768,6418,6555,7426,1772,821,1961,2350,960,2914,2750,2722,3776,3078,3636,3556,3630,1332,3790,3656,4074,4170,3409,590,4839,5250,4374,5034,5016,5368,2786,2572,4172,4595,4895,4918,500,4275,7384,8154,6905,7616,7528,7946,8350,2202,2494,2742,2586,3800,3523,3676,3788,3878,2374,3456,4753,3635,4646,-614,4902,3629,4716,3200,5224,5646,6122,4277,5010,-566,5552,3665,4760,-490,1844,4755,5364,2440,5550,6208,6524,6420,6082,7237,7950,8952,5525,7086,7068,7233,7887,7566,7846,7114,7552,7952,4496,8936,8542,3640,3642,4208,3656,2430,5794,5614,5796,5760,5914,6216,6958,3793,4166,5918,6170,5903,6168,6720,6604,8074,7962,6155,5174,3748,7972,6139,7332,3694,8120,5727,7356,3692,7898,6558,9032,7302,7034,8316,7846,8332,8047,8666,7711,8424,6036,8693,7439,6338,8974,7454,9068,8356,9644,9414,7806,9114,7374,8756,
+2003,1961,2072,2193,1182,2266,2014,2264,1618,1880,2326,2004,2330,3140,2070,2598,1774,2344,2538,3100,2770,2604,1784,3500,3104,3510,2938,2734,910,2348,2930,2732,2142,846,2972,3584,6865,7426,2499,2661,2565,2815,3178,2772,3182,2812,3914,3628,3326,3232,2508,2568,4008,4298,4440,4722,4439,2376,5043,5886,3300,5484,4342,4088,4000,4564,4720,4754,5041,5056,5279,7185,7384,8368,7179,7424,7790,7960,8558,3050,3094,3154,2998,3716,3440,4684,3800,3626,4296,2564,4730,3329,3940,1776,4880,4067,4722,1774,5262,5906,2182,4549,4940,1732,5798,4173,5056,1730,5260,4839,5258,5044,5720,6054,6328,6476,6502,6971,7384,8534,6867,5534,7150,7773,6806,7220,7424,7584,7866,7960,5418,8590,8354,1478,1476,1532,2184,6012,6076,6196,6330,5368,6070,2600,6626,5797,4314,3202,6970,5817,6462,2656,6982,7960,7958,6225,5470,3058,7996,6223,5536,2856,7394,6705,7058,2100,8008,4698,8776,8592,8268,8374,7998,7872,8347,7868,5821,8170,7870,8427,8483,7868,8154,8488,7686,7694,9480,7710,8428,9298,7212,8922,
+2909,3677,1789,1611,1702,1831,1210,1920,1686,456,1002,628,2374,74,960,2528,2520,2212,1876,2048,1446,2700,3412,3572,2404,3596,3586,3280,2544,2132,2580,2742,2670,4024,4279,5300,4320,5224,7487,6928,3293,2401,3465,3587,2866,3678,3188,3758,3950,3868,3796,3714,3836,4016,3840,3670,2420,4164,4471,2408,5101,5200,5226,5616,5618,6072,4178,4748,5476,5555,4201,6084,3479,6187,7538,8544,6609,6728,-1168,5864,6628,7060,7458,2494,1684,1660,1628,3884,3795,4056,3982,3862,3724,-368,4610,3725,3848,1608,5176,4277,4054,4856,4916,5776,6168,4441,5122,4274,5684,4877,5254,4894,4198,4711,5314,4926,4556,4544,6540,6754,6570,8209,8380,8768,2522,2469,2520,3570,4890,7148,8796,8310,5744,7398,7188,7759,7918,8270,6790,7826,8646,8119,7850,8305,5670,6890,8349,9370,8840,-386,140,84,-358,5978,6232,6382,5918,6384,6796,4688,7180,3761,4412,5492,7684,6619,6962,4686,7528,6376,8314,6839,5730,4886,8330,6441,7494,5202,8502,6275,7510,5246,8214,5332,8920,8470,9318,8747,8934,8482,7420,7194,9144,10072,10086,10040,7922,8776,6844,8999,9141,8070,8358,9146,9150,9091,9096,9089,10214,10044,8554,9382,12282]
+_GRID = {}
+
+
+def r(name, *idx):
+    return (name, idx, None)
+
+
+def c(name, a, b, s=1):
+    return (name, (slice(a, b, s),), None)
+
+
+def ind(win, off):
+    return (win[0], win[1], off)
+
+
+def _span(ref):
+    name, idx, _ = ref
+    if name not in _GRID:
+        shp = SCRATCH[name][1][1:]
+        _GRID[name] = np.arange(int(np.prod(shp))).reshape(shp)
+    v = np.asarray(_GRID[name][idx]).ravel()
+    lo, hi = int(v.min()), int(v.max()) + 1
+    if SCRATCH[name][0] == "psum":
+        lo, hi = lo // 512 * 512, (hi + 511) // 512 * 512
+    return lo, hi, int(v.size)
+
+
+def _bits(ref):
+    key = (ref[0], str(ref[1]))
+    if key not in _GRID:
+        _GRID[key] = sum(1 << int(e) for e in np.asarray(_GRID[ref[0]][ref[1]]).ravel())
+    return _GRID[key]
+
+
+def _n(ref):
+    return _span(ref[2])[2] * 16 if ref[2] is not None else _span(ref)[2]
+
+
+def _two(ref):
+    return SCRATCH[ref[0]][2] in (BF, F16, U16)
+
+
+def _psum(ref):
+    return SCRATCH[ref[0]][0] == "psum"
+
+
+def build():
+    ops, seq, phase = [], {}, ["I:", 0]
+
+    def add(kind, args, cost, R, W):
+        rr, ww = [], []
+        for x in R:
+            if isinstance(x, tuple):
+                rr.append(x)
+                if x[2] is not None:
+                    rr.append(x[2])
+        for x in W:
+            ww.append(x)
+            if x[2] is not None:
+                rr.append(x[2])
+        name = phase[0] + ("send" if kind == "send" else ww[0][0].rstrip("012") if ww else "out")
+        seq[name] = seq.get(name, -1) + 1
+        ops.append({"k": kind, "a": args, "c": cost, "R": rr, "W": ww, "key": "%s.%d" % (name, seq[name]), "v": phase[1]})
+        return len(ops) - 1
+
+    def vcost(out, ins, per):
+        n = _n(out)
+        if out[2] is not None:
+            return 50 + n * SCA * CYC
+        if ins[0][2] is not None:
+            return 50 + n * GAT * CYC
+        return 30 + max(64, n * per) * CYC
+
+    def acost(out, in_):
+        return 65 + _n(out) * (GAT if in_[2] is not None else 1) * CYC
+
+    def cp(out, in_, scale=1.0, eng="v"):
+        cost = {}
+        if "v" in eng:
+            cost["v"] = vcost(out, [in_], 0.5 if _two(out) and _two(in_) else 1)
+        if "a" in eng:
+            cost["a"] = acost(out, in_)
+        return add("cp", (out, in_, scale), cost, [in_], [out])
+
+    def tt(out, a, b, op):
+        return add("tt", (out, a, b, op), {"v": vcost(out, [a], 1 if _psum(a) or _psum(b) else 2)}, [a, b], [out])
+
+    def ts(out, a, s1, s2, op0, op1=None):
+        return add("ts", (out, a, s1, s2, op0, op1), {"v": vcost(out, [a], 0.5 if _two(out) and _two(a) else 1)}, [a, s1, s2], [out])
+
+    def aff(out, a, scale, bias):
+        cost = {"v": vcost(out, [a], 0.5 if _two(out) and _two(a) else 1), "a": acost(out, a)}
+        return add("aff", (out, a, scale, bias), cost, [a, bias], [out])
+
+    def scan(out, d0, d1, op0, op1):
+        return add("scan", (out, d0, d1, op0, op1), {"v": vcost(out, [d0], 1)}, [d0, d1], [out])
+
+    def ms(out, val):
+        return add("ms", (out, val), {"v": vcost(out, [out], 0.5 if _two(out) else 1)}, [], [out])
+
+    def act(out, in_, func, bias=0.0, scale=1.0, acc=None):
+        return add("act", (out, in_, func, bias, scale, acc), {"a": acost(out, in_)}, [in_], [out] + ([acc] if acc else []))
+
+    def mms(groups):
+        terms = [x for _, t in groups for x in t]
+        t = sum(max(64, _n(b)) * PEC for _, b in terms)
+        return add("mm", groups, {"p": t}, [x for ab in terms for x in ab], [o for o, _ in groups])
+
+    def mm(out, terms):
+        return mms([(out, terms)])
+
+    def iota(out, pat, base, cm=0):
+        return add("iota", (out, pat, base, cm), {"g": 130 + 2 * _n(out) * CYC}, [], [out])
+
+    def asel(out, in_, pat, op, base, cm):
+        return add("asel", (out, in_, pat, op, base, cm), {"g": 170 + 2 * _n(out) * CYC}, [in_], [out])
+
+    def dma(q, out, in_, sem, val, done):
+        i = add("dma", (out, in_, sem), {q: 1000.0 if q == "g" else 60.0}, [in_], [out] if isinstance(out, tuple) else [])
+        ops[i]["sem"] = (sem, val)
+        ops[i]["done"] = done
+        return i
+
+    S = slice
+    ALL = S(None)
+    zr = lambda z, k: r("Z", z, S(15 - k, 143 - k))
+    idm = lambda j: r("Id", j, ALL)
+    col = lambda j: r("col", j, S(0, 1))
+    RC, R16, R37, WH, KP, K1, AC = (col(j) for j in range(7))
+    REP8, LASTD, REP16 = c("lst", 0, 8), c("lst", 8, 11), c("lst", 16, 32)
+    XW, QW, QX, IX = c("X", 0, 4096), c("Qw", 0, 4096), c("Qw", 0, 4352), c("Iw", 0, 4352)
+    bank = [0]
+
+    def one_bank():
+        b = bank[0] % 6
+        bank[0] += 1
+        return "pb%d" % (b // 2), b % 2
+
+    def two_banks():
+        bank[0] += bank[0] % 2
+        b = bank[0] % 6
+        bank[0] += 2
+        return "pb%d" % (b // 2)
+
+    dma("s", r("ri", ALL), ["rp", None], "lr", 16, 2300)
+    dma("s", XW, ["xf", None], "lx", 16, 5500)
+    for j in range(4):
+        dma("s", c("qi", 1024 * j, 1024 * j + 1024), ["pa", (1024 * j, 1024 * j + 1024)], "lq%d" % j, 16, 7200 + 1700 * j)
+    iota(r("pi", ALL), [[0, 16]], 0, 1)
+    iota(r("ec", ALL), [[0, 16], [1, 16]], 0)
+    ms(r("one", ALL), 1.0)
+    ms(r("Z", 0, ALL), 0.0)
+    ms(r("Z", 0, S(15, 144, 16)), 1.0)
+    asel(idm(0), r("one", ALL), [[-1, 128]], ALU.is_equal, 0, 1)
+    asel(r("Z", 0, ALL), r("Z", 0, ALL), [[-1, 144]], ALU.is_ge, 15, 1)
+    asel(r("Z", 0, ALL), r("Z", 0, ALL), [[1, 144]], ALU.is_ge, 0, -1)
+    ts(c("pi", 8, 16), c("pi", 8, 16), 15, None, ALU.bitwise_and)
+    ts(c("pi", 0, 8), c("pi", 0, 8), 7, None, ALU.bitwise_and)
+    cp(RC, c("pi", 8, 9))
+    ts(R16, c("pi", 8, 9), 16.0, None, ALU.mult)
+    ts(R37, c("pi", 8, 9), 37.0, None, ALU.mult)
+    ts(K1, c("pi", 8, 9), 1.0, None, ALU.add)
+    ms(AC, -0.375)
+    cp(REP8, c("pi", 0, 8))
+    ts(c("lst", 8, 12), c("pi", 0, 4), 12.0, 11.0, ALU.mult, ALU.add)
+    cp(REP16, c("ec", 0, 16))
+    cp(c("r16", 0, 256), r("ri", ALL))
+    for j, f in ((1, -1.0), (2, 2.0), (3, 4.0), (4, -2.0), (5, -3.0)):
+        cp(idm(j), idm(0), f, "va")
+    iota(c("tf", 0, 96), [[-256, 8], [-1, 12]], 2046)
+    ts(r("cD", ALL), c("tf", 0, 96), R16, None, ALU.subtract)
+    ms(r("rsD", ALL), 1.0); ms(c("rsD", 0, 96, 12), 0.0)
+    ms(r("Jc", ALL), 0.0); ms(c("Jc", 8, 16), 1.0); ms(c("Jc", 16, 24), 2.0); ms(c("Jc", 24, 40), -1.0)
+    d0, d1, d2 = (r("dd", j, ALL) for j in range(3))
+    ts(d0, c("ec", 0, 64), RC, None, ALU.subtract)
+    ts(c("MW", 0, 64), d0, 0.0, None, ALU.is_equal)
+    ts(d1, d0, 0.0, 8192.0, ALU.is_ge, ALU.mult)
+    ts(d2, d0, 0.0, BIG - 8192.0, ALU.is_gt, ALU.mult)
+    tt(c("Wa", 0, 64), d1, d2, ALU.add)
+    ts(d1, d0, -2.0, BIG, ALU.is_lt, ALU.mult)
+    ts(d2, d0, 0.0, 32.0, ALU.is_equal, ALU.mult)
+    tt(c("Wb", 0, 64), d1, d2, ALU.add)
+    ts(c("Kw", 0, 64), d0, -2.0, R37, ALU.is_lt, ALU.mult)
+    cp(c("MW", 64, 128), c("MW", 0, 64), 1.0, "va")
+    dma("g", r("wti", ALL), ["wt", None], "lw", 32, 2500)
+    dma("g", r("kpi", ALL), ["kap", None], "lw", 32, 2500)
+    ts(WH, r("wti", ALL), 0.5, None, ALU.mult)
+    cp(KP, r("kpi", ALL))
+    ts(r("Z", 1, ALL), r("Z", 0, ALL), 256.0, None, ALU.mult)
+    ts(r("Z", 2, ALL), r("Z", 0, ALL), WH, None, ALU.mult)
+    asel(r("BO", ALL), r("one", ALL), [[-16, 8], [0, 16]], ALU.is_ge, 0, 1)
+    asel(r("BO", ALL), r("BO", ALL), [[16, 8], [0, 16]], ALU.is_ge, 15, -1)
+    iota(r("kapE", ALL), [[1, 16], [0, 8]], 0)
+    ts(r("kr", ALL), r("kapE", ALL), RC, KP, ALU.is_equal, ALU.mult)
+    mm(c("pq1", 0, 128), [(r("BO", ALL), r("kr", ALL))])
+    cp(r("kapE", ALL), c("pq1", 0, 128), 1.0, "a")
+    iota(c("cE", 0, 64), [[1, 8], [8, 8]], 0)
+    iota(c("cE", 64, 136), [[1, 8], [8, 9]], 64)
+    ms(r("rsE", ALL), 0.0); ms(c("rsE", 0, 64, 8), 1e7); ms(c("rsE", 64, 136, 9), 1e7)
+    ms(r("rs16", ALL), 1.0); ms(c("rs16", 0, 128, 16), 0.0)
+    iota(r("nb", ALL), [[16, 16]], 4096)
+    for h in range(2):
+        ts(c("ct%d" % h, 0, 8), c("nb", 8 * h, 8 * h + 8), RC, None, ALU.add)
+    ts(r("nb", ALL), r("nb", ALL), -4096.0, RC, ALU.add, ALU.add)
+    ts(r("nb", ALL), r("nb", ALL), 16.0, None, ALU.mult)
+    ms(c("Iw", 4096, 4352), 0.0)
+    iota(c("Iw", 0, 4096), [[1, 4096]], 0)
+    for j in range(4):
+        aff(c("Qw", 1024 * j, 1024 * j + 1024), c("qi", 1024 * j, 1024 * j + 1024), 1.0, -QSH)
+    ts(r("Z", 3, ALL), r("Z", 0, ALL), K1, None, ALU.mult)
+
+    def head(v, h):
+        H = str(h)
+        pq = "pq" + H
+        base = 256 * v + 128 * h
+        for j in range(4):
+            cp(c("xs" + H, 512 * j, 512 * j + 512), ind(XW, c("r16", base + 32 * j, base + 32 * j + 32)), 1.0, "va")
+        dif = lambda k, a, b: [(idm(0), c("xs" + H, a + k + 1, b, 16)), (idm(1), c("xs" + H, a + k, b, 16))]
+        for w in range(2):
+            a, tw = 1024 * w, S(4 * w, 4 * w + 4)
+            pb, b = one_bank()
+            mms([(r(pb, b, S(l // 4, 8, 2), l % 4, ALL), dif(1 + l, a, a + 1024)) for l in range(8)])
+            act(r("adD" + H, tw, S(0, 8), ALL), r(pb, b), AF.Abs, scale=2048.0)
+            pb, b = one_bank()
+            mms([(r(pb, b, S(0, 4), l, ALL), dif(9 + l, a, a + 1024)) for l in range(4)])
+            act(r("adD" + H, tw, S(8, 12), ALL), r(pb, b, S(0, 4)), AF.Abs, scale=2048.0)
+            mm(c(pq, 48 * w, 48 * w + 48), [(idm(0), c("cD", 48 * w, 48 * w + 48))] + [(zr(0, k), r("adD" + H, tw, ALL, k)) for k in range(16)])
+        scan(r("scD" + H, ALL), r("rsD", ALL), c(pq, 0, 96), ALU.mult, ALU.max)
+        vJ, off = r("vJ" + H, ALL), "off" + H
+        tt(vJ, ind(r("scD" + H, ALL), LASTD), r("Jc", ALL), ALU.subtract)
+        ts(vJ, vJ, 2047, None, ALU.bitwise_and)
+        aff(r(off, ALL), vJ, -1.0, 2047.0)
+        xs = r("xs" + H, ALL)
+        cp(c("xc" + H, 0, 128), ind(xs, c(off, 0, 8)), 2.0, "va")
+        mm(c(pq, 0, 8), [(zr(2, k), c("xc" + H, k, 128, 16)) for k in range(16)])
+        u = c("ui", 8 * h, 8 * h + 8)
+        aff(u, c(pq, 0, 8), 1.0, 0.0)
+        ts(u, u, 4095, None, ALU.bitwise_and)
+        tt(c("sq" + H, 0, 8), u, u, ALU.mult)
+        aff(c("sq" + H, 8, 16), c("sq" + H, 0, 8), 1.0 / 32, AC)
+        tt(r("ku" + H, ALL), ind(u, REP8), r("kapE", ALL), ALU.mult)
+        tt(r("cs" + H, ALL), ind(c("sq" + H, 8, 16), REP8), r("ku" + H, ALL), ALU.add)
+        ts(c("ct" + H, 8, 136), r("cs" + H, ALL), 4095, None, ALU.bitwise_and)
+        aff(r("co" + H, ALL), c("ct" + H, 8, 136), 1.0, 0.0)
+        po = "po" + H
+        ts(r("pv" + H, ALL), vJ, 15, None, ALU.bitwise_and)
+        aff(r(po, ALL), r("pv" + H, ALL), -1.0, 15.0)
+        cp(r("mk" + H, ALL), ind(c("MW", 0, 16), c(po, 24, 40)), 1.0, "va")
+        cp(r("x12" + H, ALL), ind(xs, c(off, 8, 32)), 2.0, "a")
+        nm = lambda j: r("nm" + H, j, ALL)
+        aff(nm(0), c("r16", base, base + 128), 1.0, 0.0)
+        aff(c("Qw", 4096 + 128 * h, 4224 + 128 * h), nm(0), 1.0, -(8192.0 + QSH))
+        tt(nm(1), ind(c("Wa", 0, 16), c(po, 0, 8)), nm(0), ALU.max)
+        tt(nm(2), ind(c("Kw", 0, 16), c(po, 0, 8)), nm(1), ALU.add)
+        aff(nm(2), nm(2), 32.0, -32 * 8192.0)
+        tt(nm(3), ind(c("Wb", 0, 16), c(po, 0, 8)), nm(1), ALU.min)
+
+    def rivals(v, h):
+        H = str(h)
+        pq = "pq" + H
+        for a in range(2):
+            for j in range(4 * a, 4 * a + 4):
+                tt(c("anc" + H, 256 * j, 256 * j + 256), ind(QW, c("co" + H, 16 * j, 16 * j + 16)), r("mk" + H, ALL), ALU.mult)
+            mm(c(pq, 0, 64), [(zr(0, k), c("anc" + H, 1024 * a + k, 1024 * a + 1024, 16)) for k in range(16)])
+            aff(c("bo" + H, 64 * a, 64 * a + 64), c(pq, 0, 64), 1.0, QSH)
+        for blk, (m0, m1) in enumerate(((0, 4), (4, 8), (8, 12), (12, 16), (16, 17))):
+            lo = max(m0, 1)
+            cp(c("xc" + H, 128 * lo, 128 * m1), ind(XW, c("co" + H, 8 * lo - 8, 8 * m1 - 8)), 2.0, "va")
+            raw = P["sp"][h][blk] == "a"
+            if raw:
+                cp(c("sp" + H, 128 * lo, 128 * m1), ind(XW, c("bo" + H, 8 * lo - 8, 8 * m1 - 8)), 2.0, "a")
+            else:
+                tt(c("sp" + H, 128 * lo, 128 * m1), ind(XW, c("bo" + H, 8 * lo - 8, 8 * m1 - 8)), c("xc" + H, 128 * lo, 128 * m1), ALU.subtract)
+            pb, gs = two_banks(), []
+            for m in range(m0, m1):
+                sp, xc = c("sp" + H, 128 * m, 128 * m + 128), c("xc" + H, 128 * m, 128 * m + 128)
+                x1, x2, xb = (c("x12" + H, 128 * j, 128 * j + 128) for j in range(3))
+                if raw or m == 0:
+                    xb = sp if m else xb
+                    gs.append((r(pb, 0, ALL, m - m0, ALL), [(idm(0), x1), (idm(4), xc), (idm(0), xb)]))
+                    gs.append((r(pb, 1, ALL, m - m0, ALL), [(idm(0), x2), (idm(5), xc), (idm(2), xb)]))
+                else:
+                    gs.append((r(pb, 0, ALL, m - m0, ALL), [(idm(0), x1), (idm(2), sp)]))
+                    gs.append((r(pb, 1, ALL, m - m0, ALL), [(idm(0), x2), (idm(0), xc), (idm(3), sp)]))
+            mms(gs)
+            ad, l0 = ("adA" + H, m0) if m0 < 8 else ("adB" + H, m0 - 8)
+            act(r(ad, ALL, ALL, S(l0, l0 + m1 - m0), ALL), r(pb, ALL, ALL, S(0, m1 - m0), ALL), AF.Abs, scale=0.5)
+            if blk in (1, 4):
+                a, b = (0, 64) if blk == 1 else (64, 136)
+                mm(c(pq, a, b), [(idm(0), c("cE", a, b))] + [(zr(1, k), r(ad, j, ALL, ALL, k)) for j in range(2) for k in range(16)])
+                scan(c("sc" + H, a, b), c("rsE", a, b), c(pq, a, b), ALU.max, ALU.min)
+
+    def winner(v, h):
+        H = str(h)
+        mq = r("mq" + H, ALL)
+        tt(mq, c("sc" + H, 7, 64, 8), c("sc" + H, 72, 136, 9), ALU.min)
+        ts(mq, mq, 255, None, ALU.bitwise_and)
+        aff(c("wo" + H, 0, 8), mq, 16.0, RC)
+        mid = r("mid" + H, ALL)
+        tt(mid, ind(r("xc" + H, ALL), c("wo" + H, 0, 8)), c("x12" + H, 0, 128), ALU.add)
+        aff(mid, mid, 0.25, -0.25)
+
+    def names(v, h):
+        H = str(h)
+        nm = lambda j: r("nm" + H, j, ALL)
+        ni = lambda j: r("ni" + H, j, ALL)
+        aff(c("wo" + H, 8, 16), r("mq" + H, ALL), 1.0, 0.0)
+        tt(c("cm" + H, 0, 128), ind(r("ct" + H, ALL), c("wo" + H, 8, 16)), c("MW", 0, 128), ALU.mult)
+        scan(c("cm" + H, 128, 256), r("rs16", ALL), c("cm" + H, 0, 128), ALU.mult, ALU.add)
+        cw = c("wo" + H, 16, 24)
+        aff(cw, c("cm" + H, 143, 256, 16), 1.0, 0.0)
+        aff(nm(4), ind(QX, cw), 32.0, 32 * QSH)
+        tt(ni(0), ind(IX, cw), nm(3), ALU.mult)
+        tt(nm(4), nm(4), nm(2), ALU.min)
+        tt(ni(1), ni(0), nm(4), ALU.add)
+        ts(ni(1), ni(1), 5, 4095, ALU.arith_shift_right, ALU.bitwise_and)
+        if v < NV - 1:
+            sb = c("s16", 256 * v + 128 * h, 256 * v + 128 * h + 128)
+            aff(sb, ni(1), 1.0, 0.0)
+            land = c("r16", 256 * (v + 1) + 128 * h, 256 * (v + 1) + 128 * h + 128)
+            i = add("send", (land, sb, "ar%d%d" % (v + 1, h)), {"g": 300.0}, [sb], [land])
+            ops[i]["sem"] = ("ar%d%d" % (v + 1, h), None)
+            ops[i]["done"] = None
+            aff(c("s2f", 128 * h, 128 * h + 128), ni(1), 1.0, -QSH)
+            act(c("sg", 8 * h, 8 * h + 8), c("cm" + H, 143, 256, 16), AF.Sign, bias=-4095.5)
+        else:
+            aff(c("yrf", 128 * h, 128 * h + 128), ni(1), 1.0, 0.0)
+            dma("s", ["yr", (128 * h, 128 * h + 128)], c("yrf", 128 * h, 128 * h + 128), "o%d" % h, 16, None)
+
+    def new_sums(h, a):
+        H = str(h)
+        phase[0] = "Y:"
+        src = r("nw", a, S(128 * h, 128 * h + 128))
+        if a == 0:
+            aff(src, r("ni" + H, 1, ALL), 1.0, -QSH)
+        else:
+            aff(src, r("mid" + H, ALL), 1.0, 0.0)
+        out = c("pq" + H, 0, 16)
+        mm(out, [(zr(3, t), r("nw", a, S(16 * t, 16 * t + 16))) for t in range(8 * h, 8 * h + 8)])
+        if h == 0:
+            act(c("n0", 16 * a, 16 * a + 16), out, AF.Identity, bias=136 * QSH if a == 0 else 0.0)
+        else:
+            tt(c("nsb", 16 * a, 16 * a + 16), out, c("n0", 16 * a, 16 * a + 16), ALU.add)
+            f = r("fin", a, ALL)
+            tt(f, ind(c("nsb", 16 * a, 16 * a + 16), REP16), r("eq", 0, ALL), ALU.mult)
+            tt(f, f, r("pre", a, ALL), ALU.add)
+            dma("s", [("yq", "yx")[a], None], f, "o%d" % (2 + a), 16, None)
+        phase[0] = "Z:"
+
+    def old_sums(a):
+        phase[0] = "Y:"
+        if a == 0:
+            for j in range(4):
+                cp(c("Qh", 1024 * j, 1024 * j + 1024), c("Qw", 1024 * j, 1024 * j + 1024), 1.0, "va")
+        out = c("pq%d" % a, 256, 512)
+        mm(out, [(zr(3, t), c(("Qh", "X")[a], 256 * t, 256 * t + 256)) for t in range(16)])
+        act(r("pre", a, ALL), out, AF.Identity, bias=136 * QSH if a == 0 else 0.0)
+        if a == 0:
+            for b in range(2):
+                tt(r("pre", b, ALL), r("pre", b, ALL), r("eq", 1, ALL), ALU.mult)
+        phase[0] = "Z:"
+
+    for v in range(NV):
+        last = v == NV - 1
+        seq.clear()
+        phase[:] = ["A:" if v == 0 else "Z:" if last else "", v]
+        bank[0] = 0
+        if last:
+            old_sums(1)
+        head(v, 0)
+        head(v, 1)
+        if last:
+            phase[0] = "Y:"
+            out = c("pq1", 16, 32)
+            mm(out, [(zr(2, t), c("xc%d" % (t // 8), 16 * (t % 8), 16 * (t % 8) + 16)) for t in range(16)])
+            cp(r("ei", ALL), out)
+            ts(r("ei", ALL), r("ei", ALL), 15, None, ALU.bitwise_and)
+            tt(r("eq", 0, ALL), ind(r("ei", ALL), REP16), r("ec", ALL), ALU.is_equal)
+            act(r("eq", 1, ALL), r("eq", 0, ALL), AF.Identity, bias=1.0, scale=-1.0)
+            phase[0] = "Z:"
+        else:
+            ts(r("ne", ALL), r("ui", ALL), 15, None, ALU.bitwise_and)
+            tt(r("ne", ALL), r("ne", ALL), r("nb", ALL), ALU.add)
+            aff(r("no", ALL), r("ne", ALL), 1.0, 0.0)
+        rivals(v, 0)
+        winner(v, 0)
+        if last:
+            old_sums(0)
+        names(v, 0)
+        if last:
+            new_sums(0, 1)
+            new_sums(0, 0)
+        rivals(v, 1)
+        if not last:
+            cp(ind(XW, c("no", 0, 8)), r("mid0", ALL))
+        winner(v, 1)
+        if not last:
+            cp(ind(XW, c("no", 8, 16)), r("mid1", ALL))
+        else:
+            new_sums(1, 1)
+        names(v, 1)
+        if last:
+            new_sums(1, 0)
+        else:
+            cp(ind(QW, r("no", ALL)), r("s2f", ALL))
+            mm(c("pq1", 0, 16), [(r("one", ALL), r("sg", ALL))])
+            act(r("junk", ALL), c("pq1", 0, 16), AF.Identity, bias=(1024 - 0.375) / 16, scale=-0.5, acc=AC)
+    return ops
+
+
+def depend(ops):
+    hist, deps = {}, []
+    for i, op in enumerate(ops):
+        d = {}
+        acc = [(x, False) for x in op["R"]] + [(x, True) for x in op["W"]]
+        for x, wr in acc:
+            lo, hi, _ = _span(x)
+            ps, m = _psum(x), _bits(x)
+            for (j, a, b, w, m2) in hist.get(x[0], []):
+                if a < hi and lo < b and (wr or w or ps) and j != i:
+                    d[j] = d.get(j, False) or bool((w or wr) and m & m2)
+        for x, wr in acc:
+            lo, hi, _ = _span(x)
+            h, m = hist.setdefault(x[0], []), _bits(x)
+            if wr:
+                h[:] = [e for e in h if e[4] & ~m]
+            h.append((i, lo, hi, wr, m))
+        deps.append(d)
+    return deps
+
+
+def keys(ops):
+    return list(dict.fromkeys(op["key"] for op in ops))
+
+
+def place(ops, deps, succ, rank):
+    n = len(ops)
+    left = [len(d) for d in deps]
+    when = [rank[op["key"]] // 2 + PERIOD * op["v"] for op in ops]
+    ready = [i for i in range(n) if left[i] == 0]
+    free = {e: 0.0 for e in "vapgs"}
+    order = {e: [] for e in "vapgs"}
+    eng, end, start = [None] * n, [0.0] * n, [0.0] * n
+    while ready:
+        i = min(ready, key=lambda x: (when[x], x))
+        ready.remove(i)
+        op = ops[i]
+        e = "va"[rank[op["key"]] % 2] if len(op["c"]) > 1 else next(iter(op["c"]))
+        s = free[e]
+        for j, raw in deps[i].items():
+            if eng[j] != e or "sem" in ops[j]:
+                s = max(s, end[j] + LAT_X)
+            elif raw:
+                s = max(s, end[j] + LAT_S)
+        eng[i], start[i] = e, s
+        free[e] = end[i] = s + op["c"][e]
+        if "sem" in op:
+            end[i] = end[i] + op["done"] if op["k"] == "dma" and e == "g" else op["done"] or end[i] + (HOP if op["k"] == "send" else 2200.0)
+        order[e].append(i)
+        for j in succ[i]:
+            left[j] -= 1
+            if left[j] == 0:
+                ready.append(j)
+    return eng, order, start, end
+
+
+def successors(deps):
+    succ = [[] for _ in deps]
+    for i, d in enumerate(deps):
+        for j in d:
+            succ[j].append(i)
+    return succ
+
+
+def waits(ops, deps, eng, order, start):
+    pos = {i: p for e in order for p, i in enumerate(order[e])}
+    know = {e: {} for e in order}
+    seen, need, marked = {}, {}, set()
+    for i in sorted(range(len(ops)), key=lambda x: (start[x], pos[x])):
+        e, w = eng[i], []
+        kn = know[e]
+        for j in sorted(deps[i], key=lambda x: -start[x]):
+            key, val = (ops[j]["sem"][0], 0) if "sem" in ops[j] else (eng[j], pos[j])
+            if key == e and not deps[i][j]:
+                continue
+            if kn.get(key, -1) >= val:
+                continue
+            w.append(j)
+            marked.add(j)
+            for k2, v2 in ([] if ops[j]["k"] == "send" else list(seen[j].items())) + [(key, val)]:
+                kn[k2] = max(kn.get(k2, -1), v2)
+        need[i] = w
+        seen[i] = dict(kn)
+    count, total = {}, {}
+    for e in COUNTER:
+        m = 0
+        last = [i for i in order[e] if "sem" not in ops[i]][-1]
+        marked.add(last)
+        for i in order[e]:
+            if i in marked and "sem" not in ops[i]:
+                m += 1
+                count[i] = m
+        total[e] = m
+    return need, count, total
+
+
+_PLAN = {}
+
+
+def plan():
+    if not _PLAN:
+        ops = build()
+        deps = depend(ops)
+        eng, order, start, end = place(ops, deps, successors(deps), dict(zip(keys(ops), RANK)))
+        _PLAN["p"] = (ops, eng, order, start, end) + waits(ops, deps, eng, order, start)
+    return _PLAN["p"]
+
+
+def rank_program(g, core, T, topo):
+    rank = T.rank_of(core)
+    if rank is None:
+        return
+    ops, eng, order, start, end, need, count, total = plan()
+    nxt = T.cores[(rank + 1) % len(T.cores)]
+    prv = T.cores[(rank - 1) % len(T.cores)]
+    rid, pid = topo.addr(nxt)[:2]
+    mask = topo.mask(core, nxt)
+    arrive = len(topo.engines(prv, core))
+    Q = {"v": g.vector, "a": g.scalar, "p": g.tensor, "g": g, "s": g.sync}
+
+    def ap(x):
+        if isinstance(x, list):
+            return T[x[0]][:] if x[1] is None else T[x[0]][:, x[1][0]:x[1][1]]
+        if not isinstance(x, tuple):
+            return x
+        a = T[x[0]][(slice(None),) + tuple(x[1])]
+        return a if x[2] is None else a.indirect(ap(x[2]))
+
+    sends = 0
+    for e in "sgvap":
+        q = Q[e]
+        for i in order[e]:
+            op, a = ops[i], ops[i]["a"]
+            for j in need[i]:
+                if "sem" in ops[j]:
+                    q.wait_ge(T.sem[ops[j]["sem"][0]], ops[j]["sem"][1] or arrive)
+                else:
+                    q.wait_ge(T.sem[COUNTER[eng[j]]], count[j])
+            k = op["k"]
+            if k == "cp" and e == "a":
+                ins = q.activation(ap(a[0]), ap(a[1]), AF.Copy, scale=a[2])
+            elif k == "cp" and a[2] == 1.0:
+                ins = q.tensor_copy(ap(a[0]), ap(a[1]))
+            elif k == "cp":
+                ins = q.tensor_scalar(ap(a[0]), ap(a[1]), a[2], None, ALU.mult)
+            elif k == "aff" and e == "a":
+                ins = q.activation(ap(a[0]), ap(a[1]), AF.Identity, bias=ap(a[3]), scale=a[2])
+            elif k == "aff" and a[2] == 1.0 and a[3] == 0.0:
+                ins = q.tensor_copy(ap(a[0]), ap(a[1]))
+            elif k == "aff":
+                ins = q.tensor_scalar(ap(a[0]), ap(a[1]), a[2], ap(a[3]), ALU.mult, ALU.add)
+            elif k == "tt":
+                ins = q.tensor_tensor(ap(a[0]), ap(a[1]), ap(a[2]), a[3])
+            elif k == "ts" and a[5] is None:
+                ins = q.tensor_scalar(ap(a[0]), ap(a[1]), ap(a[2]), None, a[4])
+            elif k == "ts":
+                ins = q.tensor_scalar(ap(a[0]), ap(a[1]), ap(a[2]), ap(a[3]), a[4], a[5])
+            elif k == "scan":
+                ins = q.tensor_tensor_scan(ap(a[0]), ap(a[1]), ap(a[2]), 0.0, a[3], a[4])
+            elif k == "ms":
+                ins = q.memset(ap(a[0]), a[1])
+            elif k == "act" and a[5] is None:
+                ins = q.activation(ap(a[0]), ap(a[1]), a[2], bias=a[3], scale=a[4])
+            elif k == "act":
+                ins = q.activation(ap(a[0]), ap(a[1]), a[2], bias=a[3], scale=a[4], accum_out=ap(a[5]))
+            elif k == "mm":
+                for out, terms in a:
+                    for t, (l, rh) in enumerate(terms):
+                        ins = q.matmul(ap(out), ap(l), ap(rh), t == 0, t == len(terms) - 1)
+            elif k == "iota" and SCRATCH[a[0][0]][2] == I32:
+                ins = q.iota(ap(a[0]), a[1], a[2], a[3])
+            elif k == "iota":
+                ins = q.iota(ap(a[0]), a[1], a[2], a[3], allow_small_or_imprecise_dtypes=True)
+            elif k == "asel":
+                ins = q.affine_select(ap(a[0]), ap(a[1]), a[2], a[3], 0.0, a[4], a[5])
+            elif k == "dma" and e == "g":
+                q.dma_start(ap(a[0]), ap(a[1]), allow_slow_non_contiguous=True).then_inc(T.sem[a[2]], 16)
+            elif k == "dma":
+                q.dma_start(ap(a[0]), ap(a[1])).then_inc(T.sem[a[2]], 16)
+            else:
+                g.remote_dma(ap(a[0]), ap(a[1]), T.sem[a[2]], T.sem.sent, pid, rid, mask)
+                sends += 1
+            if i in count:
+                ins.then_inc(T.sem[COUNTER[e]], 1)
+        if e == "g":
+            g.wait_ge(T.sem.sent, sends * len(topo.engines(core, nxt)))
+            for e2 in "vapg":
+                g.wait_ge(T.sem[COUNTER[e2]], total[e2])
+            for j in range(4):
+                g.wait_ge(T.sem["o%d" % j], 16)

@@ -7,6 +7,7 @@ F32, BF, F16, I32, U16 = "float32", "bfloat16", "float16", "int32", "uint16"
 NV = 5
 BIG = 32768.0
 QSH = 2048.0
+FAR = 1e7
 
 SCRATCH = {}
 
@@ -15,41 +16,47 @@ def _sb(name, cols, dtype):
     SCRATCH[name] = ("sbuf", [128] + list(cols), dtype)
 
 
-_sb("X", [4096], BF); _sb("Qw", [4352], F32); _sb("Iw", [4352], F32); _sb("qi", [4096], I32); _sb("ri", [256], I32)
-_sb("r16", [256 * NV], U16); _sb("s16", [256 * (NV - 1)], U16)
-_sb("wti", [1], I32); _sb("kpi", [1], I32)
+_sb("X", [4096], BF); _sb("Qw", [4352], F32); _sb("Iw", [4352], F32); _sb("qi", [4096], I32); _sb("Qh", [4096], F16)
+_sb("ri", [256], I32); _sb("r16", [256 * NV], U16); _sb("s16", [256 * (NV - 1)], U16); _sb("wk", [2, 4], I32)
+_sb("no", [16], U16); _sb("nw", [2, 256], F16); _sb("ei", [16], I32); _sb("kapE", [128], F32)
+_sb("eq", [2, 256], F32); _sb("pre", [2, 256], F32); _sb("fin", [2, 256], F32); _sb("nsb", [32], F32)
 for _h in "01":
-    _sb("xs" + _h, [2048], BF); _sb("adD" + _h, [8, 12, 16], BF); _sb("scD" + _h, [96], F32); _sb("vJ" + _h, [48], I32)
-    _sb("off" + _h, [48], U16); _sb("xc" + _h, [2176], BF); _sb("x12" + _h, [384], BF); _sb("mk" + _h, [256], BF)
+    _sb("ui" + _h, [8], I32); _sb("ne" + _h, [8], I32)
+    _sb("xs" + _h, [2048], BF); _sb("adD" + _h, [8, 12, 16], BF); _sb("scD" + _h, [96], I32)
+    _sb("off" + _h, [32], U16); _sb("xc" + _h, [2176], BF); _sb("x12" + _h, [256], BF); _sb("mk" + _h, [512], BF)
     _sb("sq" + _h, [16], I32); _sb("ku" + _h, [128], F32); _sb("cs" + _h, [128], I32); _sb("ct" + _h, [136], I32)
     _sb("co" + _h, [128], U16); _sb("anc" + _h, [2048], F16); _sb("bo" + _h, [128], U16); _sb("sp" + _h, [2176], F16)
-    _sb("adA" + _h, [2, 8, 8, 16], F16); _sb("adB" + _h, [2, 8, 9, 16], F16); _sb("sc" + _h, [136], F32)
-    _sb("mq" + _h, [8], I32); _sb("wo" + _h, [24], U16); _sb("mid" + _h, [128], I32); _sb("cm" + _h, [256], F32)
-    _sb("nm" + _h, [5, 128], F32); _sb("ni" + _h, [2, 128], I32); _sb("pv" + _h, [48], I32); _sb("po" + _h, [48], U16)
-_sb("ui", [16], I32); _sb("ne", [16], I32); _sb("no", [16], U16); _sb("s2f", [256], F32); _sb("sg", [16], BF)
-_sb("col", [8, 8], F32); _sb("pi", [16], I32); _sb("lst", [32], U16); _sb("Jc", [48], F32); _sb("tf", [128], F32)
-_sb("cD", [96], F16); _sb("rsD", [96], F32); _sb("cE", [136], BF); _sb("rsE", [136], F32); _sb("rs16", [128], F32)
-_sb("MW", [128], BF); _sb("Wa", [64], BF); _sb("Wb", [64], BF); _sb("Kw", [64], F32); _sb("dd", [3, 64], F32)
-_sb("Z", [4, 144], BF); _sb("Qh", [4096], F16); _sb("Id", [6, 128], BF); _sb("one", [128], BF); _sb("BO", [128], BF)
-_sb("kr", [128], F16); _sb("kapE", [128], F32); _sb("nb", [16], F32); _sb("ec", [256], F32); _sb("junk", [16], F32)
-_sb("ei", [16], I32); _sb("eq", [2, 256], F32); _sb("pre", [2, 256], F32); _sb("nw", [2, 256], F16); _sb("n0", [32], F32)
-_sb("nsb", [32], F32); _sb("fin", [2, 256], F32); _sb("yrf", [256], F32)
-for _b in "012":
-    SCRATCH["pb" + _b] = ("psum", [128, 2, 8, 4, 16], F32)
-for _h in "01":
+    _sb("am" + _h, [2176], F16); _sb("ab" + _h, [2176], F16); _sb("sc" + _h, [144], I32)
+    _sb("mq" + _h, [8], I32); _sb("lw" + _h, [128], BF); _sb("wo" + _h, [24], U16); _sb("mid" + _h, [128], I32)
+    _sb("cm" + _h, [256], F32); _sb("nm" + _h, [4, 128], F32); _sb("ni" + _h, [2, 128], I32)
     SCRATCH["pq" + _h] = ("psum", [128, 512], F32)
+SCRATCH["px"] = ("psum", [128, 512], F32)
+_sb("sg", [16], BF)
+_sb("col", [8, 8], F32); _sb("pi", [16], I32); _sb("lst", [48], U16); _sb("Jc", [32], F32); _sb("tf", [128], F32)
+_sb("cD", [96], F16); _sb("rsD", [96], F32); _sb("dE", [144], F32); _sb("rs16", [128], F32)
+_sb("MW", [2048], BF); _sb("Wa", [128], BF); _sb("Wb", [128], BF); _sb("Kw", [128], F16); _sb("Kc", [128], BF)
+_sb("dd", [4, 128], F32); _sb("B8", [4, 8], BF); _sb("TS", [2, 16], BF)
+_sb("Z", [4, 144], BF); _sb("Id", [6, 128], BF); _sb("one", [128], BF); _sb("BO", [128], BF)
+_sb("kr", [128], F16); _sb("nb", [16], F32); _sb("ec", [256], F32); _sb("junk", [16], F32); _sb("yrf", [256], F32)
+NB = 5
+for _b in range(NB):
+    SCRATCH["pb%d" % _b] = ("psum", [128, 8, 4, 16], F32)
 
-SEMAPHORES = ["cv", "ca", "cp", "cg", "lr", "lx", "lq0", "lq1", "lq2", "lq3", "lw", "sent", "o0", "o1", "o2", "o3"] + \
+OUTS = ["or0", "or1", "oq", "ox"]
+SEMAPHORES = ["cv", "ca", "cp", "cg", "lw", "lr", "lx", "lq0", "lq1", "lq2", "lq3", "sent"] + OUTS + \
              ["ar%d%d" % (v, h) for v in range(1, NV) for h in range(2)]
 COUNTER = {"v": "cv", "a": "ca", "p": "cp", "g": "cg"}
 
-CYC, PEC, GAT, SCA = 1.04, 0.52, 1.56, 3.8
-LAT_X, LAT_S, HOP = 120.0, 80.0, 3200.0
-P = {"sp": ["vvvvv", "vvvvv"]}
-PERIOD = 3500
-RANK = [-9012,-9010,-9008,-9006,-9004,-9002,52,-68,162,-242,646,-1980,-272,670,1036,1054,356,-798,-282,916,918,974,-768,734,298,1033,2284,2274,449,1062,928,1342,990,1206,1014,524,686,990,202,1558,76,-66,798,1216,5908,6326,20,150,130,514,1060,1348,1666,2168,480,-800,642,1652,2476,2763,3540,1824,106,-1260,834,-656,2200,2464,4712,7558,7608,7848,-864,1748,1937,3117,3434,3193,3214,1248,819,1220,1283,130,1518,1212,-146,2320,962,1842,980,502,2280,3344,1942,820,1108,2350,1990,3434,3340,2394,3674,3668,3362,1562,1188,438,1810,2612,3678,2886,2334,2768,6418,6555,7426,1772,821,1961,2350,960,2914,2750,2722,3776,3078,3636,3556,3630,1332,3790,3656,4074,4170,3409,590,4839,5250,4374,5034,5016,5368,2786,2572,4172,4595,4895,4918,500,4275,7384,8154,6905,7616,7528,7946,8350,2202,2494,2742,2586,3800,3523,3676,3788,3878,2374,3456,4753,3635,4646,-614,4902,3629,4716,3200,5224,5646,6122,4277,5010,-566,5552,3665,4760,-490,1844,4755,5364,2440,5550,6208,6524,6420,6082,7237,7950,8952,5525,7086,7068,7233,7887,7566,7846,7114,7552,7952,4496,8936,8542,3640,3642,4208,3656,2430,5794,5614,5796,5760,5914,6216,6958,3793,4166,5918,6170,5903,6168,6720,6604,8074,7962,6155,5174,3748,7972,6139,7332,3694,8120,5727,7356,3692,7898,6558,9032,7302,7034,8316,7846,8332,8047,8666,7711,8424,6036,8693,7439,6338,8974,7454,9068,8356,9644,9414,7806,9114,7374,8756,
-2003,1961,2072,2193,1182,2266,2014,2264,1618,1880,2326,2004,2330,3140,2070,2598,1774,2344,2538,3100,2770,2604,1784,3500,3104,3510,2938,2734,910,2348,2930,2732,2142,846,2972,3584,6865,7426,2499,2661,2565,2815,3178,2772,3182,2812,3914,3628,3326,3232,2508,2568,4008,4298,4440,4722,4439,2376,5043,5886,3300,5484,4342,4088,4000,4564,4720,4754,5041,5056,5279,7185,7384,8368,7179,7424,7790,7960,8558,3050,3094,3154,2998,3716,3440,4684,3800,3626,4296,2564,4730,3329,3940,1776,4880,4067,4722,1774,5262,5906,2182,4549,4940,1732,5798,4173,5056,1730,5260,4839,5258,5044,5720,6054,6328,6476,6502,6971,7384,8534,6867,5534,7150,7773,6806,7220,7424,7584,7866,7960,5418,8590,8354,1478,1476,1532,2184,6012,6076,6196,6330,5368,6070,2600,6626,5797,4314,3202,6970,5817,6462,2656,6982,7960,7958,6225,5470,3058,7996,6223,5536,2856,7394,6705,7058,2100,8008,4698,8776,8592,8268,8374,7998,7872,8347,7868,5821,8170,7870,8427,8483,7868,8154,8488,7686,7694,9480,7710,8428,9298,7212,8922,
-2909,3677,1789,1611,1702,1831,1210,1920,1686,456,1002,628,2374,74,960,2528,2520,2212,1876,2048,1446,2700,3412,3572,2404,3596,3586,3280,2544,2132,2580,2742,2670,4024,4279,5300,4320,5224,7487,6928,3293,2401,3465,3587,2866,3678,3188,3758,3950,3868,3796,3714,3836,4016,3840,3670,2420,4164,4471,2408,5101,5200,5226,5616,5618,6072,4178,4748,5476,5555,4201,6084,3479,6187,7538,8544,6609,6728,-1168,5864,6628,7060,7458,2494,1684,1660,1628,3884,3795,4056,3982,3862,3724,-368,4610,3725,3848,1608,5176,4277,4054,4856,4916,5776,6168,4441,5122,4274,5684,4877,5254,4894,4198,4711,5314,4926,4556,4544,6540,6754,6570,8209,8380,8768,2522,2469,2520,3570,4890,7148,8796,8310,5744,7398,7188,7759,7918,8270,6790,7826,8646,8119,7850,8305,5670,6890,8349,9370,8840,-386,140,84,-358,5978,6232,6382,5918,6384,6796,4688,7180,3761,4412,5492,7684,6619,6962,4686,7528,6376,8314,6839,5730,4886,8330,6441,7494,5202,8502,6275,7510,5246,8214,5332,8920,8470,9318,8747,8934,8482,7420,7194,9144,10072,10086,10040,7922,8776,6844,8999,9141,8070,8358,9146,9150,9091,9096,9089,10214,10044,8554,9382,12282]
+CYC, PEC, GAT, SCA = 0.95, 0.47, 1.56, 3.8
+LAT_X, LAT_S, HOP, SLACK = 200.0, 150.0, 3200.0, 100.0
+P = {"xs": [4, 4], "am": ["aaaaa", "aaaavv"], "b": ((0, 2), (2, 4)), "dsplit": [1, 0],
+     "blocks": [((0, 1), (1, 5), (5, 9), (9, 13), (13, 17)), ((0, 1), (1, 5), (5, 9), (9, 13), (13, 16), (16, 17))]}
+ORDER = """cv00 -qh0 -stx0 -sg1 -cw1 -pre1 -mid1 -nam1 -sg0 -old10 -s21 -stx1 xs01 -cnt1 xs11 cv02 cv03 xs00 xs02 D00 xs03 D01 p0 u0
+-s20 -stq1 mk0 xs10 xs13 xs12 D10 D11 cv01 an01 D12 p1 xc01 xc03 an00 b00 u1 an03 pre0 xc04 sp01 an02 mk1 sp00 an10 x120 xc02 no0 b01
+E01 an11 sp02 sp03 b10 E02 E00 x121 an12 an13 xc12 sp10 no1 E03 sp12 xc14 sp04 E04 xc15 win0 b11 sp15 cw0 xc11 xc13 E10 nam0 sp11 sp13
+px1 sp14 E15 E13 E14 E11 mid0 old11 E12 win1""".split()
+VECTOR = """b01:bo cv02:Qw cw1:wo nam0:pq pre0:Qw s21:nw stx0:nw u0:co u0:sq u0:xc u1:sq win1:wo xc15:xc xs00:xs xs03:xs xs10:xs
+xs13:xs""".split()
 _GRID = {}
 
 
@@ -65,22 +72,24 @@ def ind(win, off):
     return (win[0], win[1], off)
 
 
+def _like(ref):
+    return "pb0" if ref[0][:3] == "pb_" else ref[0]
+
+
 def _span(ref):
-    name, idx, _ = ref
+    name, idx = _like(ref), ref[1]
     if name not in _GRID:
         shp = SCRATCH[name][1][1:]
         _GRID[name] = np.arange(int(np.prod(shp))).reshape(shp)
     v = np.asarray(_GRID[name][idx]).ravel()
-    lo, hi = int(v.min()), int(v.max()) + 1
-    if SCRATCH[name][0] == "psum":
-        lo, hi = lo // 512 * 512, (hi + 511) // 512 * 512
-    return lo, hi, int(v.size)
+    return int(v.min()), int(v.max()) + 1, int(v.size)
 
 
 def _bits(ref):
-    key = (ref[0], str(ref[1]))
+    key = (_like(ref), str(ref[1]))
     if key not in _GRID:
-        _GRID[key] = sum(1 << int(e) for e in np.asarray(_GRID[ref[0]][ref[1]]).ravel())
+        _span(ref)
+        _GRID[key] = sum(1 << int(e) for e in np.asarray(_GRID[key[0]][ref[1]]).ravel())
     return _GRID[key]
 
 
@@ -89,15 +98,15 @@ def _n(ref):
 
 
 def _two(ref):
-    return SCRATCH[ref[0]][2] in (BF, F16, U16)
+    return SCRATCH[_like(ref)][2] in (BF, F16, U16)
 
 
 def _psum(ref):
-    return SCRATCH[ref[0]][0] == "psum"
+    return SCRATCH[_like(ref)][0] == "psum"
 
 
-def build():
-    ops, seq, phase = [], {}, ["I:", 0]
+def build(steps=None):
+    ops, now = [], ["init", 0]
 
     def add(kind, args, cost, R, W):
         rr, ww = [], []
@@ -110,65 +119,67 @@ def build():
             ww.append(x)
             if x[2] is not None:
                 rr.append(x[2])
-        name = phase[0] + ("send" if kind == "send" else ww[0][0].rstrip("012") if ww else "out")
-        seq[name] = seq.get(name, -1) + 1
-        ops.append({"k": kind, "a": args, "c": cost, "R": rr, "W": ww, "key": "%s.%d" % (name, seq[name]), "v": phase[1]})
+        per = {"": 1.0, "g": GAT, "s": SCA}
+        if len(cost) > 1 and VECTOR is not None:
+            e = "v" if now[0] + ":" + ww[0][0].rstrip("01") in VECTOR else "a"
+            cost = {e: cost[e]}
+        ops.append({"k": kind, "a": args, "m": cost, "R": rr, "W": ww, "t": now[0], "v": now[1] // 2, "h": now[1] % 2,
+                    "n": "send" if kind == "send" else ww[0][0] if ww else "out",
+                    "c": {e: f + n * per[k] * (PEC if e == "p" else CYC) for e, (f, n, k) in cost.items()}})
         return len(ops) - 1
 
     def vcost(out, ins, per):
         n = _n(out)
         if out[2] is not None:
-            return 50 + n * SCA * CYC
+            return (50, n, "s")
         if ins[0][2] is not None:
-            return 50 + n * GAT * CYC
-        return 30 + max(64, n * per) * CYC
+            return (50, n, "g")
+        return (30, max(64, n * per), "")
 
-    def acost(out, in_):
-        return 65 + _n(out) * (GAT if in_[2] is not None else 1) * CYC
+    def both(out, in_, eng):
+        cost = {"v": vcost(out, [in_], 0.5 if _two(out) and _two(in_) else 1), "a": (65, _n(out), "g" if in_[2] is not None else "")}
+        return {e: cost[e] for e in eng}
 
     def cp(out, in_, scale=1.0, eng="v"):
-        cost = {}
-        if "v" in eng:
-            cost["v"] = vcost(out, [in_], 0.5 if _two(out) and _two(in_) else 1)
-        if "a" in eng:
-            cost["a"] = acost(out, in_)
-        return add("cp", (out, in_, scale), cost, [in_], [out])
+        return add("cp", (out, in_, scale), both(out, in_, eng), [in_], [out])
+
+    def gcp(out, in_):
+        return add("gcp", (out, in_), {"g": (170, 2 * _n(out), "")}, [in_], [out])
 
     def tt(out, a, b, op):
         return add("tt", (out, a, b, op), {"v": vcost(out, [a], 1 if _psum(a) or _psum(b) else 2)}, [a, b], [out])
 
     def ts(out, a, s1, s2, op0, op1=None):
-        return add("ts", (out, a, s1, s2, op0, op1), {"v": vcost(out, [a], 0.5 if _two(out) and _two(a) else 1)}, [a, s1, s2], [out])
+        return add("ts", (out, a, s1, s2, op0, op1), both(out, a, "v"), [a, s1, s2], [out])
 
-    def aff(out, a, scale, bias):
-        cost = {"v": vcost(out, [a], 0.5 if _two(out) and _two(a) else 1), "a": acost(out, a)}
-        return add("aff", (out, a, scale, bias), cost, [a, bias], [out])
+    def aff(out, a, scale, bias, eng="va"):
+        return add("aff", (out, a, scale, bias), both(out, a, eng), [a, bias], [out])
 
-    def scan(out, d0, d1, op0, op1):
-        return add("scan", (out, d0, d1, op0, op1), {"v": vcost(out, [d0], 1)}, [d0, d1], [out])
+    def scan(out, d0, d1, op0, op1, first=0.0):
+        return add("scan", (out, d0, d1, op0, op1, first), {"v": vcost(out, [d0], 1)}, [d0, d1], [out])
 
     def ms(out, val):
         return add("ms", (out, val), {"v": vcost(out, [out], 0.5 if _two(out) else 1)}, [], [out])
 
     def act(out, in_, func, bias=0.0, scale=1.0, acc=None):
-        return add("act", (out, in_, func, bias, scale, acc), {"a": acost(out, in_)}, [in_], [out] + ([acc] if acc else []))
+        return add("act", (out, in_, func, bias, scale, acc), both(out, in_, "a"), [in_], [out] + ([acc] if acc else []))
 
     def mms(groups):
         terms = [x for _, t in groups for x in t]
-        t = sum(max(64, _n(b)) * PEC for _, b in terms)
-        return add("mm", groups, {"p": t}, [x for ab in terms for x in ab], [o for o, _ in groups])
+        return add("mm", groups, {"p": (0, sum(max(64, _n(b)) for _, b in terms), "")}, [x for ab in terms for x in ab], [o for o, _ in groups])
 
     def mm(out, terms):
         return mms([(out, terms)])
 
     def iota(out, pat, base, cm=0):
-        return add("iota", (out, pat, base, cm), {"g": 130 + 2 * _n(out) * CYC}, [], [out])
+        return add("iota", (out, pat, base, cm), {"g": (130, 2 * _n(out), "")}, [], [out])
 
     def asel(out, in_, pat, op, base, cm):
-        return add("asel", (out, in_, pat, op, base, cm), {"g": 170 + 2 * _n(out) * CYC}, [in_], [out])
+        return add("asel", (out, in_, pat, op, base, cm), {"g": (170, 2 * _n(out), "")}, [in_], [out])
 
-    def dma(q, out, in_, sem, val, done):
-        i = add("dma", (out, in_, sem), {q: 1000.0 if q == "g" else 60.0}, [in_], [out] if isinstance(out, tuple) else [])
+    def dma(q, buf, name, cols, sem, val, done=None):
+        i = add("dma", (buf, name, cols, sem, done), {q: (1000.0 if q == "g" else 60.0, 0, "")},
+                [] if done else [buf], [buf] if done else [])
         ops[i]["sem"] = (sem, val)
         ops[i]["done"] = done
         return i
@@ -176,79 +187,79 @@ def build():
     S = slice
     ALL = S(None)
     zr = lambda z, k: r("Z", z, S(15 - k, 143 - k))
-    idm = lambda j: r("Id", j, ALL)
-    col = lambda j: r("col", j, S(0, 1))
-    RC, R16, R37, WH, KP, K1, AC = (col(j) for j in range(7))
-    REP8, LASTD, REP16 = c("lst", 0, 8), c("lst", 8, 11), c("lst", 16, 32)
-    XW, QW, QX, IX = c("X", 0, 4096), c("Qw", 0, 4096), c("Qw", 0, 4352), c("Iw", 0, 4352)
+    ONE, NEG, TWO, HALF, NHALF, N15 = (r("Id", j, ALL) for j in range(6))
+    G32, G64, GN32, GN16 = (r("B8", j, ALL) for j in range(4))
+    RC, R16, KP, K1, AC, WH = (r("col", j, S(0, 1)) for j in range(6))
+    REP8, REP4, REP16, EXP = c("lst", 0, 8), c("lst", 0, 2), c("lst", 16, 32), c("lst", 32, 40)
+    XW, QW, QX, IX, DIAG = r("X", ALL), c("Qw", 0, 4096), r("Qw", ALL), r("Iw", ALL), c("MW", 0, 128)
     bank = [0]
 
-    def one_bank():
-        b = bank[0] % 6
+    def next_bank():
         bank[0] += 1
-        return "pb%d" % (b // 2), b % 2
+        return "pb_%d" % bank[0]
 
-    def two_banks():
-        bank[0] += bank[0] % 2
-        b = bank[0] % 6
-        bank[0] += 2
-        return "pb%d" % (b // 2)
-
-    dma("s", r("ri", ALL), ["rp", None], "lr", 16, 2300)
-    dma("s", XW, ["xf", None], "lx", 16, 5500)
+    dma("s", r("ri", ALL), "rp", ALL, "lr", 16, 2300)
+    dma("s", XW, "xf", ALL, "lx", 16, 5500)
     for j in range(4):
-        dma("s", c("qi", 1024 * j, 1024 * j + 1024), ["pa", (1024 * j, 1024 * j + 1024)], "lq%d" % j, 16, 7200 + 1700 * j)
+        dma("s", c("qi", 1024 * j, 1024 * j + 1024), "pa", S(1024 * j, 1024 * j + 1024), "lq%d" % j, 16, 7200 + 1700 * j)
     iota(r("pi", ALL), [[0, 16]], 0, 1)
     iota(r("ec", ALL), [[0, 16], [1, 16]], 0)
     ms(r("one", ALL), 1.0)
     ms(r("Z", 0, ALL), 0.0)
     ms(r("Z", 0, S(15, 144, 16)), 1.0)
-    asel(idm(0), r("one", ALL), [[-1, 128]], ALU.is_equal, 0, 1)
+    asel(ONE, r("one", ALL), [[-1, 128]], ALU.is_equal, 0, 1)
     asel(r("Z", 0, ALL), r("Z", 0, ALL), [[-1, 144]], ALU.is_ge, 15, 1)
     asel(r("Z", 0, ALL), r("Z", 0, ALL), [[1, 144]], ALU.is_ge, 0, -1)
+    iota(c("tf", 0, 96), [[256, 8], [1, 12]], 1 - 2048)
+    dma("g", r("wk", 0, S(0, 1)), "wt", ALL, "lw", 32, 2500)
+    dma("g", r("wk", 1, S(0, 1)), "kap", ALL, "lw", 32, 2500)
     ts(c("pi", 8, 16), c("pi", 8, 16), 15, None, ALU.bitwise_and)
     ts(c("pi", 0, 8), c("pi", 0, 8), 7, None, ALU.bitwise_and)
+    cp(c("r16", 0, 256), r("ri", ALL))
     cp(RC, c("pi", 8, 9))
     ts(R16, c("pi", 8, 9), 16.0, None, ALU.mult)
-    ts(R37, c("pi", 8, 9), 37.0, None, ALU.mult)
     ts(K1, c("pi", 8, 9), 1.0, None, ALU.add)
     ms(AC, -0.375)
     cp(REP8, c("pi", 0, 8))
-    ts(c("lst", 8, 12), c("pi", 0, 4), 12.0, 11.0, ALU.mult, ALU.add)
     cp(REP16, c("ec", 0, 16))
-    cp(c("r16", 0, 256), r("ri", ALL))
-    for j, f in ((1, -1.0), (2, 2.0), (3, 4.0), (4, -2.0), (5, -3.0)):
-        cp(idm(j), idm(0), f, "va")
-    iota(c("tf", 0, 96), [[-256, 8], [-1, 12]], 2046)
-    ts(r("cD", ALL), c("tf", 0, 96), R16, None, ALU.subtract)
+    cp(EXP, c("ec", 0, 8))
+    for m, f in ((NEG, -1.0), (TWO, 2.0), (HALF, 0.5), (NHALF, -0.5), (N15, -1.5)):
+        cp(m, ONE, f, "a")
+    cp(r("Z", 1, ALL), r("Z", 0, ALL), -1.0, "a")
+    for m, f in ((G32, 32.0), (G64, 64.0), (GN32, -32.0), (GN16, -16.0), (r("TS", 0, S(0, 8)), 128.0), (r("TS", 0, S(8, 16)), 8.0)):
+        cp(m, r("Z", 0, S(15, 143, 16)), f, "a")
+    ts(r("cD", ALL), c("tf", 0, 96), R16, None, ALU.add)
     ms(r("rsD", ALL), 1.0); ms(c("rsD", 0, 96, 12), 0.0)
-    ms(r("Jc", ALL), 0.0); ms(c("Jc", 8, 16), 1.0); ms(c("Jc", 16, 24), 2.0); ms(c("Jc", 24, 40), -1.0)
-    d0, d1, d2 = (r("dd", j, ALL) for j in range(3))
-    ts(d0, c("ec", 0, 64), RC, None, ALU.subtract)
-    ts(c("MW", 0, 64), d0, 0.0, None, ALU.is_equal)
-    ts(d1, d0, 0.0, 8192.0, ALU.is_ge, ALU.mult)
-    ts(d2, d0, 0.0, BIG - 8192.0, ALU.is_gt, ALU.mult)
-    tt(c("Wa", 0, 64), d1, d2, ALU.add)
-    ts(d1, d0, -2.0, BIG, ALU.is_lt, ALU.mult)
-    ts(d2, d0, 0.0, 32.0, ALU.is_equal, ALU.mult)
-    tt(c("Wb", 0, 64), d1, d2, ALU.add)
-    ts(c("Kw", 0, 64), d0, -2.0, R37, ALU.is_lt, ALU.mult)
-    cp(c("MW", 64, 128), c("MW", 0, 64), 1.0, "va")
-    dma("g", r("wti", ALL), ["wt", None], "lw", 32, 2500)
-    dma("g", r("kpi", ALL), ["kap", None], "lw", 32, 2500)
-    ts(WH, r("wti", ALL), 0.5, None, ALU.mult)
-    cp(KP, r("kpi", ALL))
-    ts(r("Z", 1, ALL), r("Z", 0, ALL), 256.0, None, ALU.mult)
-    ts(r("Z", 2, ALL), r("Z", 0, ALL), WH, None, ALU.mult)
-    asel(r("BO", ALL), r("one", ALL), [[-16, 8], [0, 16]], ALU.is_ge, 0, 1)
-    asel(r("BO", ALL), r("BO", ALL), [[16, 8], [0, 16]], ALU.is_ge, 15, -1)
+    ms(r("Jc", ALL), 0.0); ms(c("Jc", 8, 16), 1.0); ms(c("Jc", 16, 24), 2.0); ms(c("Jc", 24, 32), -1.0)
+    ts(c("MW", 0, 256), r("ec", ALL), RC, None, ALU.is_equal)
+    for n in (256, 512, 1024):
+        cp(c("MW", n, 2 * n), c("MW", 0, n))
+    ts(r("TS", 1, S(0, 8)), c("ec", 0, 8), 16.0, RC, ALU.mult, ALU.add)
+    cp(r("TS", 1, S(8, 16)), c("ec", 0, 8))
+    ts(WH, r("wk", 0, S(0, 1)), 0.5, None, ALU.mult)
+    cp(KP, r("wk", 1, S(0, 1)))
+    ts(r("Z", 3, ALL), r("Z", 0, ALL), WH, None, ALU.mult)
+    inside = lambda out, in_: (asel(out, in_, [[-16, 8], [0, 16]], ALU.is_ge, 0, 1), asel(out, out, [[16, 8], [0, 16]], ALU.is_ge, 15, -1))
+    inside(r("BO", ALL), r("one", ALL))
     iota(r("kapE", ALL), [[1, 16], [0, 8]], 0)
     ts(r("kr", ALL), r("kapE", ALL), RC, KP, ALU.is_equal, ALU.mult)
     mm(c("pq1", 0, 128), [(r("BO", ALL), r("kr", ALL))])
     cp(r("kapE", ALL), c("pq1", 0, 128), 1.0, "a")
-    iota(c("cE", 0, 64), [[1, 8], [8, 8]], 0)
-    iota(c("cE", 64, 136), [[1, 8], [8, 9]], 64)
-    ms(r("rsE", ALL), 0.0); ms(c("rsE", 0, 64, 8), 1e7); ms(c("rsE", 64, 136, 9), 1e7)
+    for h in range(2):
+        ms(c("pq%d" % h, 145, 272, 18), 0.0)
+    cp(r("Kc", ALL), r("BO", ALL), -(8192.0 + QSH), "a")
+    d0, d1, d2, d3 = (r("dd", j, ALL) for j in range(4))
+    ts(d0, c("ec", 0, 128), K1, -1.0, ALU.subtract, ALU.add)
+    inside(d0, d0)
+    ts(d1, d0, -1.0, 8192.0, ALU.is_le, ALU.mult)
+    ts(d2, d0, -1.0, BIG - 8192.0, ALU.is_lt, ALU.mult)
+    tt(r("Wa", ALL), d1, d2, ALU.add)
+    ts(d1, d0, 1.0, BIG, ALU.is_gt, ALU.mult)
+    ts(d2, d0, -1.0, 32.0, ALU.is_equal, ALU.mult)
+    tt(r("Wb", ALL), d1, d2, ALU.add)
+    ts(d3, d0, 1.0, 37.0, ALU.is_gt, ALU.mult)
+    tt(r("Kw", ALL), d3, c("ec", 0, 128), ALU.mult)
+    ms(r("dE", ALL), -1.0); ms(c("dE", 16, 144, 18), 16.0); ms(c("dE", 17, 144, 18), FAR)
     ms(r("rs16", ALL), 1.0); ms(c("rs16", 0, 128, 16), 0.0)
     iota(r("nb", ALL), [[16, 16]], 4096)
     for h in range(2):
@@ -256,207 +267,254 @@ def build():
     ts(r("nb", ALL), r("nb", ALL), -4096.0, RC, ALU.add, ALU.add)
     ts(r("nb", ALL), r("nb", ALL), 16.0, None, ALU.mult)
     ms(c("Iw", 4096, 4352), 0.0)
-    iota(c("Iw", 0, 4096), [[1, 4096]], 0)
-    for j in range(4):
-        aff(c("Qw", 1024 * j, 1024 * j + 1024), c("qi", 1024 * j, 1024 * j + 1024), 1.0, -QSH)
-    ts(r("Z", 3, ALL), r("Z", 0, ALL), K1, None, ALU.mult)
+    ts(r("Z", 2, ALL), r("Z", 0, ALL), K1, None, ALU.mult)
 
-    def head(v, h):
+    def old_names(v, h, a=0, b=128):
+        return c("r16", 256 * v + 128 * h + a, 256 * v + 128 * h + b)
+
+    def cand(name, h, a, b):
+        return c(name + str(h), 128 * a, 128 * b)
+
+    def nm(h, j):
+        return r("nm%d" % h, j, ALL)
+
+    def ni(h, j):
+        return r("ni%d" % h, j, ALL)
+
+    def s_cv(v, h, j):
+        if v == 0:
+            aff(c("Qw", 1024 * j, 1024 * j + 1024), c("qi", 1024 * j, 1024 * j + 1024), 1.0, -QSH)
+            iota(c("Iw", 1024 * j, 1024 * j + 1024), [[1, 1024]], 1024 * j)
+
+    def s_xs(v, h, j):
+        a, b = 128 * j // P["xs"][h], 128 * (j + 1) // P["xs"][h]
+        cp(c("xs%d" % h, 16 * a, 16 * b), ind(XW, old_names(v, h, a, b)), 1.0, "va")
+
+    def s_D(v, h, w):
         H = str(h)
-        pq = "pq" + H
-        base = 256 * v + 128 * h
-        for j in range(4):
-            cp(c("xs" + H, 512 * j, 512 * j + 512), ind(XW, c("r16", base + 32 * j, base + 32 * j + 32)), 1.0, "va")
-        dif = lambda k, a, b: [(idm(0), c("xs" + H, a + k + 1, b, 16)), (idm(1), c("xs" + H, a + k, b, 16))]
-        for w in range(2):
+        dif = lambda k, a, b: [(ONE, c("xs" + H, a + k + 1, b, 16)), (NEG, c("xs" + H, a + k, b, 16))]
+        keys = lambda a, b, t: mm(c("pq" + H, a, b), [(ONE, c("cD", a, b))] + [(zr(1, k), r("adD" + H, t, ALL, k)) for k in range(16)])
+        pb = next_bank()
+        if P["dsplit"][h]:
             a, tw = 1024 * w, S(4 * w, 4 * w + 4)
-            pb, b = one_bank()
-            mms([(r(pb, b, S(l // 4, 8, 2), l % 4, ALL), dif(1 + l, a, a + 1024)) for l in range(8)])
-            act(r("adD" + H, tw, S(0, 8), ALL), r(pb, b), AF.Abs, scale=2048.0)
-            pb, b = one_bank()
-            mms([(r(pb, b, S(0, 4), l, ALL), dif(9 + l, a, a + 1024)) for l in range(4)])
-            act(r("adD" + H, tw, S(8, 12), ALL), r(pb, b, S(0, 4)), AF.Abs, scale=2048.0)
-            mm(c(pq, 48 * w, 48 * w + 48), [(idm(0), c("cD", 48 * w, 48 * w + 48))] + [(zr(0, k), r("adD" + H, tw, ALL, k)) for k in range(16)])
-        scan(r("scD" + H, ALL), r("rsD", ALL), c(pq, 0, 96), ALU.mult, ALU.max)
-        vJ, off = r("vJ" + H, ALL), "off" + H
-        tt(vJ, ind(r("scD" + H, ALL), LASTD), r("Jc", ALL), ALU.subtract)
-        ts(vJ, vJ, 2047, None, ALU.bitwise_and)
-        aff(r(off, ALL), vJ, -1.0, 2047.0)
-        xs = r("xs" + H, ALL)
-        cp(c("xc" + H, 0, 128), ind(xs, c(off, 0, 8)), 2.0, "va")
-        mm(c(pq, 0, 8), [(zr(2, k), c("xc" + H, k, 128, 16)) for k in range(16)])
-        u = c("ui", 8 * h, 8 * h + 8)
-        aff(u, c(pq, 0, 8), 1.0, 0.0)
+            mms([(r(pb, S(l // 4, 8, 2), l % 4, ALL), dif(1 + l, a, a + 1024)) for l in range(8)])
+            act(r("adD" + H, tw, S(0, 8), ALL), r(pb, ALL), AF.Abs, scale=2048.0)
+            pb = next_bank()
+            mms([(r(pb, S(0, 4), l, ALL), dif(9 + l, a, a + 1024)) for l in range(4)])
+            act(r("adD" + H, tw, S(8, 12), ALL), r(pb, S(0, 4)), AF.Abs, scale=2048.0)
+            keys(48 * w, 48 * w + 48, tw)
+        else:
+            mms([(r(pb, ALL, l, ALL), dif(4 * w + 1 + l, 0, 2048)) for l in range(4)])
+            act(r("adD" + H, ALL, S(4 * w, 4 * w + 4), ALL), r(pb, ALL), AF.Abs, scale=2048.0)
+            if w == 2:
+                keys(0, 96, ALL)
+
+    def s_p(v, h, j):
+        H = str(h)
+        scan(r("scD" + H, ALL), r("rsD", ALL), c("pq" + H, 0, 96), ALU.mult, ALU.min)
+        ts(c("mq" + H, 0, 8), c("scD" + H, 11, 96, 12), 2047, None, ALU.bitwise_and)
+        tt(r("off" + H, ALL), ind(c("mq" + H, 0, 8), REP4), r("Jc", ALL), ALU.add)
+
+    def s_u(v, h, j):
+        H = str(h)
+        cp(cand("xc", h, 0, 1), ind(r("xs" + H, ALL), c("off" + H, 0, 8)), 2.0, "va")
+        mm(c("pq" + H, 96, 104), [(zr(3, k), c("xc" + H, k, 128, 16)) for k in range(16)])
+        u = r("ui" + H, ALL)
+        aff(u, c("pq" + H, 96, 104), 1.0, 0.0)
         ts(u, u, 4095, None, ALU.bitwise_and)
         tt(c("sq" + H, 0, 8), u, u, ALU.mult)
-        aff(c("sq" + H, 8, 16), c("sq" + H, 0, 8), 1.0 / 32, AC)
         tt(r("ku" + H, ALL), ind(u, REP8), r("kapE", ALL), ALU.mult)
+        aff(c("sq" + H, 8, 16), c("sq" + H, 0, 8), 1.0 / 32, AC)
         tt(r("cs" + H, ALL), ind(c("sq" + H, 8, 16), REP8), r("ku" + H, ALL), ALU.add)
         ts(c("ct" + H, 8, 136), r("cs" + H, ALL), 4095, None, ALU.bitwise_and)
         aff(r("co" + H, ALL), c("ct" + H, 8, 136), 1.0, 0.0)
-        po = "po" + H
-        ts(r("pv" + H, ALL), vJ, 15, None, ALU.bitwise_and)
-        aff(r(po, ALL), r("pv" + H, ALL), -1.0, 15.0)
-        cp(r("mk" + H, ALL), ind(c("MW", 0, 16), c(po, 24, 40)), 1.0, "va")
-        cp(r("x12" + H, ALL), ind(xs, c(off, 8, 32)), 2.0, "a")
-        nm = lambda j: r("nm" + H, j, ALL)
-        aff(nm(0), c("r16", base, base + 128), 1.0, 0.0)
-        aff(c("Qw", 4096 + 128 * h, 4224 + 128 * h), nm(0), 1.0, -(8192.0 + QSH))
-        tt(nm(1), ind(c("Wa", 0, 16), c(po, 0, 8)), nm(0), ALU.max)
-        tt(nm(2), ind(c("Kw", 0, 16), c(po, 0, 8)), nm(1), ALU.add)
-        aff(nm(2), nm(2), 32.0, -32 * 8192.0)
-        tt(nm(3), ind(c("Wb", 0, 16), c(po, 0, 8)), nm(1), ALU.min)
 
-    def rivals(v, h):
+    def s_mk(v, h, j):
         H = str(h)
-        pq = "pq" + H
-        for a in range(2):
-            for j in range(4 * a, 4 * a + 4):
-                tt(c("anc" + H, 256 * j, 256 * j + 256), ind(QW, c("co" + H, 16 * j, 16 * j + 16)), r("mk" + H, ALL), ALU.mult)
-            mm(c(pq, 0, 64), [(zr(0, k), c("anc" + H, 1024 * a + k, 1024 * a + 1024, 16)) for k in range(16)])
-            aff(c("bo" + H, 64 * a, 64 * a + 64), c(pq, 0, 64), 1.0, QSH)
-        for blk, (m0, m1) in enumerate(((0, 4), (4, 8), (8, 12), (12, 16), (16, 17))):
-            lo = max(m0, 1)
-            cp(c("xc" + H, 128 * lo, 128 * m1), ind(XW, c("co" + H, 8 * lo - 8, 8 * m1 - 8)), 2.0, "va")
-            raw = P["sp"][h][blk] == "a"
-            if raw:
-                cp(c("sp" + H, 128 * lo, 128 * m1), ind(XW, c("bo" + H, 8 * lo - 8, 8 * m1 - 8)), 2.0, "a")
-            else:
-                tt(c("sp" + H, 128 * lo, 128 * m1), ind(XW, c("bo" + H, 8 * lo - 8, 8 * m1 - 8)), c("xc" + H, 128 * lo, 128 * m1), ALU.subtract)
-            pb, gs = two_banks(), []
-            for m in range(m0, m1):
-                sp, xc = c("sp" + H, 128 * m, 128 * m + 128), c("xc" + H, 128 * m, 128 * m + 128)
-                x1, x2, xb = (c("x12" + H, 128 * j, 128 * j + 128) for j in range(3))
-                if raw or m == 0:
-                    xb = sp if m else xb
-                    gs.append((r(pb, 0, ALL, m - m0, ALL), [(idm(0), x1), (idm(4), xc), (idm(0), xb)]))
-                    gs.append((r(pb, 1, ALL, m - m0, ALL), [(idm(0), x2), (idm(5), xc), (idm(2), xb)]))
-                else:
-                    gs.append((r(pb, 0, ALL, m - m0, ALL), [(idm(0), x1), (idm(2), sp)]))
-                    gs.append((r(pb, 1, ALL, m - m0, ALL), [(idm(0), x2), (idm(0), xc), (idm(3), sp)]))
-            mms(gs)
-            ad, l0 = ("adA" + H, m0) if m0 < 8 else ("adB" + H, m0 - 8)
-            act(r(ad, ALL, ALL, S(l0, l0 + m1 - m0), ALL), r(pb, ALL, ALL, S(0, m1 - m0), ALL), AF.Abs, scale=0.5)
-            if blk in (1, 4):
-                a, b = (0, 64) if blk == 1 else (64, 136)
-                mm(c(pq, a, b), [(idm(0), c("cE", a, b))] + [(zr(1, k), r(ad, j, ALL, ALL, k)) for j in range(2) for k in range(16)])
-                scan(c("sc" + H, a, b), c("rsE", a, b), c(pq, a, b), ALU.max, ALU.min)
+        cp(c("mk" + H, 0, 128), ind(r("MW", ALL), c("off" + H, 24, 32)), 1.0, "a")
+        gcp(c("mk" + H, 128, 256), c("mk" + H, 0, 128))
+        gcp(c("mk" + H, 256, 512), c("mk" + H, 0, 256))
 
-    def winner(v, h):
+    def s_x12(v, h, j):
+        cp(r("x12%d" % h, ALL), ind(r("xs%d" % h, ALL), c("off%d" % h, 8, 24)), 2.0, "a")
+
+    def s_an(v, h, j):
+        H = str(h)
+        tt(c("anc" + H, 512 * j, 512 * j + 512), ind(QW, c("co" + H, 32 * j, 32 * j + 32)), r("mk" + H, ALL), ALU.mult)
+
+    def s_b(v, h, a):
+        H = str(h)
+        lo, hi = (32 * x for x in P["b"][a])
+        out = c("pq" + H, lo, hi)
+        mm(out, [(zr(0, k), c("anc" + H, 16 * lo + k, 16 * hi, 16)) for k in range(16)])
+        aff(c("bo" + H, lo, hi), out, 1.0, QSH)
+
+    def s_pre(v, h, j):
+        pb, mk = next_bank(), c("mk%d" % h, 0, 128)
+        w = lambda j: r(pb, S(2 * j, 2 * j + 2), ALL, ALL)
+        aff(c("Qw", 4096 + 128 * h, 4224 + 128 * h), old_names(v, h), 1.0, -(16384.0 + QSH))
+        mms([(w(0), [(r("Wa", ALL), mk)]), (w(1), [(r("Kw", ALL), mk), (r("Kc", ALL), mk)]), (w(2), [(r("Wb", ALL), mk)])])
+        tt(nm(h, 0), w(0), old_names(v, h), ALU.max)
+        tt(nm(h, 1), w(1), nm(h, 0), ALU.add)
+        tt(nm(h, 2), w(2), nm(h, 0), ALU.min)
+
+    def s_xc(v, h, j):
+        m0, m1 = P["blocks"][h][j]
+        cp(cand("xc", h, m0, m1), ind(XW, c("co%d" % h, 8 * m0 - 8, 8 * m1 - 8)), 2.0, "va")
+
+    def s_sp(v, h, j):
+        m0, m1 = P["blocks"][h][j]
+        xb = ind(XW, c("bo%d" % h, 8 * m0 - 8, 8 * m1 - 8)) if j else ind(r("xs%d" % h, ALL), c("off%d" % h, 24, 32))
+        if P["am"][h][j] == "r":
+            cp(cand("sp", h, m0, m1), xb, 1.0, "a")
+        else:
+            tt(cand("sp", h, m0, m1), xb, cand("xc", h, m0, m1), ALU.subtract)
+
+    def s_px(v, h, j):
+        if "v" in P["am"][h]:
+            mms([(c("px", 128 * m, 128 * m + 128), [(NHALF, cand("x12", h, 0, 1))]) for m in range(4)])
+
+    def s_E(v, h, j):
+        m0, m1 = P["blocks"][h][j]
+        x1, x2 = cand("x12", h, 0, 1), cand("x12", h, 1, 2)
+        one, raw = lambda name, m: cand(name, h, m, m + 1), P["am"][h][j] == "r"
+        part = lambda pb, a, b: r(pb, S(2 * (a - m0), 2 * (b - m0)), ALL, ALL)
+        if P["am"][h][j] == "v":
+            tt(cand("am", h, m0, m1), c("px", 0, 128 * (m1 - m0)), cand("sp", h, m0, m1), ALU.max)
+            first = lambda m: [(one("am", m), G64), (one("sp", m), GN32)]
+        else:
+            pb = next_bank()
+            mms([(part(pb, m, m + 1), [(HALF, x1), (ONE, one("sp", m))] + [(NEG, one("xc", m))] * raw) for m in range(m0, m1)])
+            act(cand("am", h, m0, m1), part(pb, m0, m1), AF.Abs)
+            first = lambda m: [(one("am", m), G32)] + [(x1, GN16)] * ("v" in P["am"][h])
+        pb = next_bank()
+        mms([(part(pb, m, m + 1), [(HALF, x2), (N15 if raw else HALF, one("xc", m)), (TWO, one("sp", m))]) for m in range(m0, m1)])
+        act(cand("ab", h, m0, m1), part(pb, m0, m1), AF.Abs)
+        mms([(c("pq%d" % h, 128 + m, 272, 18), first(m) + [(one("ab", m), G32)]) for m in range(m0, m1)])
+
+    def s_win(v, h, j):
         H = str(h)
         mq = r("mq" + H, ALL)
-        tt(mq, c("sc" + H, 7, 64, 8), c("sc" + H, 72, 136, 9), ALU.min)
-        ts(mq, mq, 255, None, ALU.bitwise_and)
-        aff(c("wo" + H, 0, 8), mq, 16.0, RC)
-        mid = r("mid" + H, ALL)
-        tt(mid, ind(r("xc" + H, ALL), c("wo" + H, 0, 8)), c("x12" + H, 0, 128), ALU.add)
-        aff(mid, mid, 0.25, -0.25)
+        scan(r("sc" + H, ALL), c("pq" + H, 128, 272), r("dE", ALL), ALU.min, ALU.add, FAR)
+        ts(mq, c("sc" + H, 16, 144, 18), 31, None, ALU.bitwise_and)
+        tt(r("lw" + H, ALL), ind(mq, EXP), DIAG, ALU.mult)
+        mm(c("pq" + H, 0, 16), [(r("lw" + H, ALL), r("TS", 0, ALL)), (ONE, r("TS", 1, ALL))])
+        aff(c("wo" + H, 0, 16), c("pq" + H, 0, 16), 1.0, 0.0)
 
-    def names(v, h):
+    def s_mid(v, h, j):
         H = str(h)
-        nm = lambda j: r("nm" + H, j, ALL)
-        ni = lambda j: r("ni" + H, j, ALL)
-        aff(c("wo" + H, 8, 16), r("mq" + H, ALL), 1.0, 0.0)
-        tt(c("cm" + H, 0, 128), ind(r("ct" + H, ALL), c("wo" + H, 8, 16)), c("MW", 0, 128), ALU.mult)
+        tt(r("mid" + H, ALL), ind(r("xc" + H, ALL), c("wo" + H, 0, 8)), cand("x12", h, 0, 1), ALU.add)
+        aff(r("mid" + H, ALL), r("mid" + H, ALL), 0.25, -0.25)
+
+    def s_cw(v, h, j):
+        H = str(h)
+        tt(c("cm" + H, 0, 128), ind(r("ct" + H, ALL), c("wo" + H, 8, 16)), DIAG, ALU.mult)
         scan(c("cm" + H, 128, 256), r("rs16", ALL), c("cm" + H, 0, 128), ALU.mult, ALU.add)
+        aff(c("wo" + H, 16, 24), c("cm" + H, 143, 256, 16), 1.0, 0.0)
+
+    def s_nam(v, h, j):
+        H = str(h)
         cw = c("wo" + H, 16, 24)
-        aff(cw, c("cm" + H, 143, 256, 16), 1.0, 0.0)
-        aff(nm(4), ind(QX, cw), 32.0, 32 * QSH)
-        tt(ni(0), ind(IX, cw), nm(3), ALU.mult)
-        tt(nm(4), nm(4), nm(2), ALU.min)
-        tt(ni(1), ni(0), nm(4), ALU.add)
-        ts(ni(1), ni(1), 5, 4095, ALU.arith_shift_right, ALU.bitwise_and)
+        tt(nm(h, 3), ind(QX, cw), nm(h, 1), ALU.min)
+        aff(c("pq" + H, 272, 400), nm(h, 3), 32.0, 32 * QSH)
+        tt(ni(h, 0), ind(IX, cw), nm(h, 2), ALU.mult)
+        tt(ni(h, 1), c("pq" + H, 272, 400), ni(h, 0), ALU.add)
+        ts(ni(h, 1), ni(h, 1), 5, 4095, ALU.arith_shift_right, ALU.bitwise_and)
         if v < NV - 1:
             sb = c("s16", 256 * v + 128 * h, 256 * v + 128 * h + 128)
-            aff(sb, ni(1), 1.0, 0.0)
-            land = c("r16", 256 * (v + 1) + 128 * h, 256 * (v + 1) + 128 * h + 128)
-            i = add("send", (land, sb, "ar%d%d" % (v + 1, h)), {"g": 300.0}, [sb], [land])
-            ops[i]["sem"] = ("ar%d%d" % (v + 1, h), None)
+            aff(sb, ni(h, 1), 1.0, 0.0)
+            land, sem = old_names(v + 1, h), "ar%d%d" % (v + 1, h)
+            i = add("send", (land, sb, sem), {"g": (300.0, 0, "")}, [sb], [land])
+            ops[i]["sem"] = (sem, None)
             ops[i]["done"] = None
-            aff(c("s2f", 128 * h, 128 * h + 128), ni(1), 1.0, -QSH)
-            act(c("sg", 8 * h, 8 * h + 8), c("cm" + H, 143, 256, 16), AF.Sign, bias=-4095.5)
         else:
-            aff(c("yrf", 128 * h, 128 * h + 128), ni(1), 1.0, 0.0)
-            dma("s", ["yr", (128 * h, 128 * h + 128)], c("yrf", 128 * h, 128 * h + 128), "o%d" % h, 16, None)
+            aff(c("yrf", 128 * h, 128 * h + 128), ni(h, 1), 1.0, 0.0)
+            dma("s", c("yrf", 128 * h, 128 * h + 128), "yr", S(128 * h, 128 * h + 128), "or" + H, 16)
 
-    def new_sums(h, a):
+    def s_no(v, h, j):
         H = str(h)
-        phase[0] = "Y:"
-        src = r("nw", a, S(128 * h, 128 * h + 128))
-        if a == 0:
-            aff(src, r("ni" + H, 1, ALL), 1.0, -QSH)
-        else:
-            aff(src, r("mid" + H, ALL), 1.0, 0.0)
-        out = c("pq" + H, 0, 16)
-        mm(out, [(zr(3, t), r("nw", a, S(16 * t, 16 * t + 16))) for t in range(8 * h, 8 * h + 8)])
-        if h == 0:
-            act(c("n0", 16 * a, 16 * a + 16), out, AF.Identity, bias=136 * QSH if a == 0 else 0.0)
-        else:
-            tt(c("nsb", 16 * a, 16 * a + 16), out, c("n0", 16 * a, 16 * a + 16), ALU.add)
-            f = r("fin", a, ALL)
-            tt(f, ind(c("nsb", 16 * a, 16 * a + 16), REP16), r("eq", 0, ALL), ALU.mult)
-            tt(f, f, r("pre", a, ALL), ALU.add)
-            dma("s", [("yq", "yx")[a], None], f, "o%d" % (2 + a), 16, None)
-        phase[0] = "Z:"
-
-    def old_sums(a):
-        phase[0] = "Y:"
-        if a == 0:
-            for j in range(4):
-                cp(c("Qh", 1024 * j, 1024 * j + 1024), c("Qw", 1024 * j, 1024 * j + 1024), 1.0, "va")
-        out = c("pq%d" % a, 256, 512)
-        mm(out, [(zr(3, t), c(("Qh", "X")[a], 256 * t, 256 * t + 256)) for t in range(16)])
-        act(r("pre", a, ALL), out, AF.Identity, bias=136 * QSH if a == 0 else 0.0)
-        if a == 0:
-            for b in range(2):
-                tt(r("pre", b, ALL), r("pre", b, ALL), r("eq", 1, ALL), ALU.mult)
-        phase[0] = "Z:"
-
-    for v in range(NV):
-        last = v == NV - 1
-        seq.clear()
-        phase[:] = ["A:" if v == 0 else "Z:" if last else "", v]
-        bank[0] = 0
-        if last:
-            old_sums(1)
-        head(v, 0)
-        head(v, 1)
-        if last:
-            phase[0] = "Y:"
-            out = c("pq1", 16, 32)
-            mm(out, [(zr(2, t), c("xc%d" % (t // 8), 16 * (t % 8), 16 * (t % 8) + 16)) for t in range(16)])
-            cp(r("ei", ALL), out)
-            ts(r("ei", ALL), r("ei", ALL), 15, None, ALU.bitwise_and)
-            tt(r("eq", 0, ALL), ind(r("ei", ALL), REP16), r("ec", ALL), ALU.is_equal)
+        if v < NV - 1:
+            ts(r("ne" + H, ALL), r("ui" + H, ALL), 15, None, ALU.bitwise_and)
+            tt(c("no", 8 * h, 8 * h + 8), r("ne" + H, ALL), c("nb", 8 * h, 8 * h + 8), ALU.add)
+        elif h == 1:
+            out, ei = r(next_bank(), 0, 0, ALL), r("ei", ALL)
+            mm(out, [(zr(3, t), c("xc%d" % (t // 8), 16 * (t % 8), 16 * (t % 8) + 16)) for t in range(16)])
+            cp(ei, out)
+            ts(ei, ei, 15, None, ALU.bitwise_and)
+            tt(r("eq", 0, ALL), ind(ei, REP16), r("ec", ALL), ALU.is_equal)
             act(r("eq", 1, ALL), r("eq", 0, ALL), AF.Identity, bias=1.0, scale=-1.0)
-            phase[0] = "Z:"
+
+    def s_stx(v, h, j):
+        if v < NV - 1:
+            cp(ind(XW, c("no", 8 * h, 8 * h + 8)), r("mid%d" % h, ALL))
         else:
-            ts(r("ne", ALL), r("ui", ALL), 15, None, ALU.bitwise_and)
-            tt(r("ne", ALL), r("ne", ALL), r("nb", ALL), ALU.add)
-            aff(r("no", ALL), r("ne", ALL), 1.0, 0.0)
-        rivals(v, 0)
-        winner(v, 0)
-        if last:
-            old_sums(0)
-        names(v, 0)
-        if last:
-            new_sums(0, 1)
-            new_sums(0, 0)
-        rivals(v, 1)
-        if not last:
-            cp(ind(XW, c("no", 0, 8)), r("mid0", ALL))
-        winner(v, 1)
-        if not last:
-            cp(ind(XW, c("no", 8, 16)), r("mid1", ALL))
+            aff(r("nw", 1, S(128 * h, 128 * h + 128)), r("mid%d" % h, ALL), 1.0, 0.0)
+            if h == 1:
+                new_sums(1)
+
+    def s_s2(v, h, j):
+        src = c("s16", 256 * v + 128 * h, 256 * v + 128 * h + 128) if v < NV - 1 else ni(h, 1)
+        aff(r("nw", 0, S(128 * h, 128 * h + 128)), src, 1.0, -QSH)
+
+    def s_stq(v, h, j):
+        if v < NV - 1:
+            cp(ind(QW, r("no", ALL)), r("nw", 0, ALL))
         else:
-            new_sums(1, 1)
-        names(v, 1)
-        if last:
-            new_sums(1, 0)
-        else:
-            cp(ind(QW, r("no", ALL)), r("s2f", ALL))
-            mm(c("pq1", 0, 16), [(r("one", ALL), r("sg", ALL))])
-            act(r("junk", ALL), c("pq1", 0, 16), AF.Identity, bias=(1024 - 0.375) / 16, scale=-0.5, acc=AC)
+            new_sums(0)
+
+    def s_sg(v, h, j):
+        if v < NV - 1:
+            act(c("sg", 8 * h, 8 * h + 8), r("mq%d" % h, ALL), AF.Sign)
+
+    def s_cnt(v, h, j):
+        if v < NV - 1 and h == 1:
+            out = r(next_bank(), 0, 0, ALL)
+            mm(out, [(r("one", ALL), r("sg", ALL))])
+            act(r("junk", ALL), out, AF.Identity, bias=-0.375 / 16, acc=AC)
+
+    def new_sums(a):
+        out, new, f = r(next_bank(), 0, 0, ALL), c("nsb", 16 * a, 16 * a + 16), r("fin", a, ALL)
+        mm(out, [(zr(2, t), r("nw", a, S(16 * t, 16 * t + 16))) for t in range(16)])
+        aff(new, out, 1.0, 136 * QSH if a == 0 else 0.0)
+        tt(f, ind(new, REP16), r("eq", 0, ALL), ALU.mult)
+        tt(f, f, r("pre", a, ALL), ALU.add)
+        dma("s", f, ("yq", "yx")[a], ALL, ("oq", "ox")[a], 16)
+
+    def s_qh(v, h, j):
+        if v == NV - 1:
+            for a in range(0, 4096, 512):
+                gcp(c("Qh", a, a + 512), c("Qw", a, a + 512))
+
+    def s_old(v, h, a):
+        if v == NV - 1:
+            out, pre = r(next_bank(), S(0, 4), ALL, ALL), r("pre", a, ALL)
+            mm(out, [(zr(2, t), c(("Qh", "X")[a], 256 * t, 256 * t + 256)) for t in range(16)])
+            act(pre, out, AF.Identity, bias=136 * QSH if a == 0 else 0.0)
+            tt(pre, pre, r("eq", 1, ALL), ALU.mult)
+
+    table = {"cv": s_cv, "xs": s_xs, "D": s_D, "p": s_p, "u": s_u, "mk": s_mk, "x12": s_x12, "an": s_an, "b": s_b,
+             "pre": s_pre, "xc": s_xc, "sp": s_sp, "px": s_px, "E": s_E, "win": s_win, "mid": s_mid, "cw": s_cw, "nam": s_nam,
+             "no": s_no, "stx": s_stx, "s2": s_s2, "stq": s_stq, "sg": s_sg, "cnt": s_cnt, "qh": s_qh, "old": s_old}
+    steps = steps or ORDER
+    names = [step.lstrip("-") for step in steps]
+    held = {}
+    for turn in range(NV + 2):
+        for step, name in zip(steps, names):
+            v = turn - (len(step) - len(name))
+            if not 0 <= v < NV:
+                continue
+            if (name, v) not in held:
+                key = max((k for k in table if name.startswith(k)), key=len)
+                h, j = (int(x) for x in (name[len(key):] + "0")[:2])
+                now[:] = [name, 2 * v + h]
+                n = len(ops)
+                table[key](v, h, j)
+                held[name, v] = [names.count(name), ops[n:]]
+                del ops[n:]
+            left, calls = held[name, v]
+            n = 1 if left > 1 else len(calls)
+            ops.extend(calls[:n])
+            held[name, v] = [left - 1, calls[n:]]
     return ops
 
 
@@ -465,12 +523,13 @@ def depend(ops):
     for i, op in enumerate(ops):
         d = {}
         acc = [(x, False) for x in op["R"]] + [(x, True) for x in op["W"]]
+        op["B"] = sorted({x[0] for x, _ in acc if _psum(x)})
         for x, wr in acc:
             lo, hi, _ = _span(x)
             ps, m = _psum(x), _bits(x)
             for (j, a, b, w, m2) in hist.get(x[0], []):
-                if a < hi and lo < b and (wr or w or ps) and j != i:
-                    d[j] = d.get(j, False) or bool((w or wr) and m & m2)
+                if a < hi and lo < b and (wr or w) and j != i and (m & m2 or not ps):
+                    d[j] = d.get(j, False) or bool(m & m2)
         for x, wr in acc:
             lo, hi, _ = _span(x)
             h, m = hist.setdefault(x[0], []), _bits(x)
@@ -481,47 +540,62 @@ def depend(ops):
     return deps
 
 
-def keys(ops):
-    return list(dict.fromkeys(op["key"] for op in ops))
+def _lag(op):
+    return {"send": HOP, "dma": 2200.0}.get(op["k"], 0.0)
 
 
-def place(ops, deps, succ, rank):
+def place(ops, deps, rank=None, eng=None):
     n = len(ops)
-    left = [len(d) for d in deps]
-    when = [rank[op["key"]] // 2 + PERIOD * op["v"] for op in ops]
-    ready = [i for i in range(n) if left[i] == 0]
-    free = {e: 0.0 for e in "vapgs"}
-    order = {e: [] for e in "vapgs"}
-    eng, end, start = [None] * n, [0.0] * n, [0.0] * n
-    while ready:
-        i = min(ready, key=lambda x: (when[x], x))
-        ready.remove(i)
-        op = ops[i]
-        e = "va"[rank[op["key"]] % 2] if len(op["c"]) > 1 else next(iter(op["c"]))
-        s = free[e]
-        for j, raw in deps[i].items():
-            if eng[j] != e or "sem" in ops[j]:
-                s = max(s, end[j] + LAT_X)
-            elif raw:
-                s = max(s, end[j] + LAT_S)
-        eng[i], start[i] = e, s
-        free[e] = end[i] = s + op["c"][e]
-        if "sem" in op:
-            end[i] = end[i] + op["done"] if op["k"] == "dma" and e == "g" else op["done"] or end[i] + (HOP if op["k"] == "send" else 2200.0)
-        order[e].append(i)
-        for j in succ[i]:
-            left[j] -= 1
-            if left[j] == 0:
-                ready.append(j)
-    return eng, order, start, end
-
-
-def successors(deps):
-    succ = [[] for _ in deps]
+    rank = rank or range(n)
+    eng = eng or [next(iter(op["c"])) for op in ops]
+    succ, left = [[] for _ in ops], [len(d) for d in deps]
     for i, d in enumerate(deps):
         for j in d:
             succ[j].append(i)
-    return succ
+    uses = {}
+    for op in ops:
+        for b in op["B"]:
+            uses[b] = uses.get(b, 0) + 1
+    lent, idle, last = {}, ["pb%d" % b for b in range(NB)], {}
+    free, order = {e: 0.0 for e in "vapgs"}, {e: [] for e in "vapgs"}
+    start, end = [0.0] * n, [0.0] * n
+    ready = {i: 0.0 for i in range(n) if not left[i]}
+
+    def after(j, e, raw):
+        return end[j] + (LAT_X if eng[j] != e or "sem" in ops[j] else LAT_S if raw else 0.0)
+
+    while ready:
+        can = {}
+        for i, s in ready.items():
+            for b in ops[i]["B"]:
+                b = lent.get(b) or (b if b[:2] != "pb" else idle[0] if idle else None)
+                s = max(s, after(last[b], eng[i], False) if b in last else 0.0) if b else 1e18
+            can[i] = max(s, free[eng[i]])
+        first = min(can, key=can.get)
+        e = eng[first]
+        i = min((x for x in can if eng[x] == e and can[x] <= can[first] + SLACK), key=lambda x: rank[x])
+        del ready[i]
+        op = ops[i]
+        for b in op["B"]:
+            if b[:2] == "pb" and b not in lent:
+                lent[b] = idle.pop(0)
+            real = lent.get(b, b)
+            if real in last:
+                deps[i].setdefault(last[real], False)
+            last[real] = i
+            uses[b] -= 1
+            if b[:2] == "pb" and not uses[b]:
+                idle.append(real)
+        start[i] = can[i]
+        free[e] = end[i] = can[i] + op["c"][e]
+        if "sem" in op:
+            end[i] = end[i] + op["done"] if op["k"] == "dma" and e == "g" else op["done"] or end[i] + _lag(op)
+        order[e].append(i)
+        for j in succ[i]:
+            left[j] -= 1
+            if not left[j]:
+                ready[j] = max(after(x, eng[j], raw) for x, raw in deps[j].items())
+    return eng, order, start, end, lent
 
 
 def waits(ops, deps, eng, order, start):
@@ -563,8 +637,8 @@ def plan():
     if not _PLAN:
         ops = build()
         deps = depend(ops)
-        eng, order, start, end = place(ops, deps, successors(deps), dict(zip(keys(ops), RANK)))
-        _PLAN["p"] = (ops, eng, order, start, end) + waits(ops, deps, eng, order, start)
+        eng, order, start, end, lent = place(ops, deps)
+        _PLAN["p"] = (ops, eng, order, lent) + waits(ops, deps, eng, order, start)
     return _PLAN["p"]
 
 
@@ -572,7 +646,7 @@ def rank_program(g, core, T, topo):
     rank = T.rank_of(core)
     if rank is None:
         return
-    ops, eng, order, start, end, need, count, total = plan()
+    ops, eng, order, lent, need, count, total = plan()
     nxt = T.cores[(rank + 1) % len(T.cores)]
     prv = T.cores[(rank - 1) % len(T.cores)]
     rid, pid = topo.addr(nxt)[:2]
@@ -581,11 +655,9 @@ def rank_program(g, core, T, topo):
     Q = {"v": g.vector, "a": g.scalar, "p": g.tensor, "g": g, "s": g.sync}
 
     def ap(x):
-        if isinstance(x, list):
-            return T[x[0]][:] if x[1] is None else T[x[0]][:, x[1][0]:x[1][1]]
         if not isinstance(x, tuple):
             return x
-        a = T[x[0]][(slice(None),) + tuple(x[1])]
+        a = T[lent.get(x[0], x[0])][(slice(None),) + tuple(x[1])]
         return a if x[2] is None else a.indirect(ap(x[2]))
 
     sends = 0
@@ -605,6 +677,8 @@ def rank_program(g, core, T, topo):
                 ins = q.tensor_copy(ap(a[0]), ap(a[1]))
             elif k == "cp":
                 ins = q.tensor_scalar(ap(a[0]), ap(a[1]), a[2], None, ALU.mult)
+            elif k == "gcp":
+                ins = q.affine_select(ap(a[0]), ap(a[1]), [[0, _n(a[0])]], ALU.is_ge, 0.0, 0, 0)
             elif k == "aff" and e == "a":
                 ins = q.activation(ap(a[0]), ap(a[1]), AF.Identity, bias=ap(a[3]), scale=a[2])
             elif k == "aff" and a[2] == 1.0 and a[3] == 0.0:
@@ -618,7 +692,7 @@ def rank_program(g, core, T, topo):
             elif k == "ts":
                 ins = q.tensor_scalar(ap(a[0]), ap(a[1]), ap(a[2]), ap(a[3]), a[4], a[5])
             elif k == "scan":
-                ins = q.tensor_tensor_scan(ap(a[0]), ap(a[1]), ap(a[2]), 0.0, a[3], a[4])
+                ins = q.tensor_tensor_scan(ap(a[0]), ap(a[1]), ap(a[2]), a[5], a[3], a[4])
             elif k == "ms":
                 ins = q.memset(ap(a[0]), a[1])
             elif k == "act" and a[5] is None:
@@ -636,9 +710,11 @@ def rank_program(g, core, T, topo):
             elif k == "asel":
                 ins = q.affine_select(ap(a[0]), ap(a[1]), a[2], a[3], 0.0, a[4], a[5])
             elif k == "dma" and e == "g":
-                q.dma_start(ap(a[0]), ap(a[1]), allow_slow_non_contiguous=True).then_inc(T.sem[a[2]], 16)
+                q.dma_start(ap(a[0]), T[a[1]][:], allow_slow_non_contiguous=True).then_inc(T.sem[a[3]], 16)
+            elif k == "dma" and a[4]:
+                q.dma_start(ap(a[0]), T[a[1]][:, a[2]]).then_inc(T.sem[a[3]], 16)
             elif k == "dma":
-                q.dma_start(ap(a[0]), ap(a[1])).then_inc(T.sem[a[2]], 16)
+                q.dma_start(T[a[1]][:, a[2]], ap(a[0])).then_inc(T.sem[a[3]], 16)
             else:
                 g.remote_dma(ap(a[0]), ap(a[1]), T.sem[a[2]], T.sem.sent, pid, rid, mask)
                 sends += 1
@@ -648,5 +724,5 @@ def rank_program(g, core, T, topo):
             g.wait_ge(T.sem.sent, sends * len(topo.engines(core, nxt)))
             for e2 in "vapg":
                 g.wait_ge(T.sem[COUNTER[e2]], total[e2])
-            for j in range(4):
-                g.wait_ge(T.sem["o%d" % j], 16)
+            for name in OUTS:
+                g.wait_ge(T.sem[name], 16)

@@ -20,10 +20,10 @@ _sb("X", [4096], BF); _sb("Qw", [4352], F32); _sb("Iw", [4352], F32); _sb("qi", 
 _sb("ri", [256], I32); _sb("r16", [256 * NV], U16); _sb("s16", [256 * (NV - 1)], U16); _sb("wk", [2, 4], I32)
 _sb("no", [16], U16); _sb("nw", [2, 256], F16); _sb("ei", [16], I32); _sb("kapE", [128], F32)
 _sb("eq", [2, 256], F32); _sb("pre", [2, 256], F32); _sb("fin", [2, 256], F32); _sb("nsb", [32], F32)
+_sb("ui", [16], I32); _sb("ne", [16], I32); _sb("won", [16], I32)
 for _h in "01":
-    _sb("ui" + _h, [8], I32); _sb("ne" + _h, [8], I32)
-    _sb("xs" + _h, [2048], BF); _sb("adD" + _h, [8, 12, 16], BF); _sb("scD" + _h, [96], I32)
-    _sb("off" + _h, [32], U16); _sb("xc" + _h, [2176], BF); _sb("x12" + _h, [256], BF); _sb("mk" + _h, [512], BF)
+    _sb("xw" + _h, [2048], BF); _sb("adD" + _h, [8, 12, 16], BF); _sb("scD" + _h, [104], I32)
+    _sb("off" + _h, [32], U16); _sb("xc" + _h, [2432], BF); _sb("own" + _h, [256], F16); _sb("mk" + _h, [512], BF)
     _sb("sq" + _h, [16], I32); _sb("ku" + _h, [128], F32); _sb("cs" + _h, [128], I32); _sb("ct" + _h, [136], I32)
     _sb("co" + _h, [128], U16); _sb("anc" + _h, [2048], F16); _sb("bo" + _h, [128], U16); _sb("sp" + _h, [2176], F16)
     _sb("am" + _h, [2176], F16); _sb("ab" + _h, [2176], F16); _sb("sc" + _h, [144], I32)
@@ -31,12 +31,12 @@ for _h in "01":
     _sb("cm" + _h, [256], F32); _sb("nm" + _h, [4, 128], F32); _sb("ni" + _h, [2, 128], I32)
     SCRATCH["pq" + _h] = ("psum", [128, 512], F32)
 SCRATCH["px"] = ("psum", [128, 512], F32)
-_sb("sg", [16], BF)
+_sb("sg", [16], BF); _sb("xs0", [8, 256], BF); _sb("hold", [96], F32); _sb("us", [96], I32); _sb("ends", [104], I32)
 _sb("col", [8, 8], F32); _sb("pi", [16], I32); _sb("lst", [48], U16); _sb("Jc", [32], F32); _sb("tf", [128], F32)
 _sb("cD", [96], F16); _sb("rsD", [96], F32); _sb("dE", [144], F32); _sb("rs16", [128], F32)
 _sb("MW", [2048], BF); _sb("Wa", [128], BF); _sb("Wb", [128], BF); _sb("Kw", [128], F16); _sb("Kc", [128], BF)
 _sb("dd", [4, 128], F32); _sb("B8", [4, 8], BF); _sb("TS", [2, 16], BF)
-_sb("Z", [4, 144], BF); _sb("Id", [6, 128], BF); _sb("one", [128], BF); _sb("BO", [128], BF)
+_sb("cU", [96], BF); _sb("Z", [5, 144], BF); _sb("Id", [6, 128], BF); _sb("one", [128], BF); _sb("BO", [128], BF)
 _sb("kr", [128], F16); _sb("nb", [16], F32); _sb("ec", [256], F32); _sb("junk", [16], F32); _sb("yrf", [256], F32)
 NB = 5
 for _b in range(NB):
@@ -44,19 +44,20 @@ for _b in range(NB):
 
 OUTS = ["or0", "or1", "oq", "ox"]
 SEMAPHORES = ["cv", "ca", "cp", "cg", "lw", "lr", "lx", "lq0", "lq1", "lq2", "lq3", "sent"] + OUTS + \
-             ["ar%d%d" % (v, h) for v in range(1, NV) for h in range(2)]
+             ["ar%d%d" % (v, h) for v in range(1, NV) for h in range(2)] + ["mv%d0" % v for v in range(NV)]
 COUNTER = {"v": "cv", "a": "ca", "p": "cp", "g": "cg"}
 
 CYC, PEC, GAT, SCA = 0.95, 0.47, 1.56, 3.8
-LAT_X, LAT_S, HOP, SLACK = 200.0, 150.0, 3200.0, 100.0
-P = {"xs": [4, 4], "am": ["aaaaa", "aaaavv"], "b": ((0, 2), (2, 4)), "dsplit": [1, 0],
+LAT_X, LAT_S, HOP, SLACK = 200.0, 150.0, 3600.0, 100.0
+P = {"am": ["aaaaa", "aaavvv"], "b": [((0, 2), (2, 4))] * 2, "dsplit": [1, 0], "mk": "vg", "s16": "gv", "co": "vg",
+     "runs": [((0, 1), (1, 5), (5, 9), (9, 13), (13, 17)), ((0, 1), (1, 5), (5, 9), (9, 13), (13, 16), (16, 17))],
      "blocks": [((0, 1), (1, 5), (5, 9), (9, 13), (13, 17)), ((0, 1), (1, 5), (5, 9), (9, 13), (13, 16), (16, 17))]}
-ORDER = """cv00 -qh0 -stx0 -sg1 -cw1 -pre1 -mid1 -nam1 -sg0 -old10 -s21 -stx1 xs01 -cnt1 xs11 cv02 cv03 xs00 xs02 D00 xs03 D01 p0 u0
--s20 -stq1 mk0 xs10 xs13 xs12 D10 D11 cv01 an01 D12 p1 xc01 xc03 an00 b00 u1 an03 pre0 xc04 sp01 an02 mk1 sp00 an10 x120 xc02 no0 b01
-E01 an11 sp02 sp03 b10 E02 E00 x121 an12 an13 xc12 sp10 no1 E03 sp12 xc14 sp04 E04 xc15 win0 b11 sp15 cw0 xc11 xc13 E10 nam0 sp11 sp13
-px1 sp14 E15 E13 E14 E11 mid0 old11 E12 win1""".split()
-VECTOR = """b01:bo cv02:Qw cw1:wo nam0:pq pre0:Qw s21:nw stx0:nw u0:co u0:sq u0:xc u1:sq win1:wo xc15:xc xs00:xs xs03:xs xs10:xs
-xs13:xs""".split()
+ORDER = """-mid1 -stx1 xs02 xs03 xs00 -stq1 set00 D01 xs01 in0 D00 xs10 xs12 xs13 xs11 ws0 D10 cv01 p00 p01 cv00 D11 D12 p10 u0 p11
+mk0 xw0 cv02 cv03 x120 xc02 xc10 -old10 pre0 an02 an03 old11 b01 sp00 xc03 x121 xc04 px1 u1 an01 an00 mk1 sp04 xc01 b00 E04 an10 xc12
+an11 sp01 sp03 -clr10 b10 sp12 E00 sp10 E01 E03 sp02 set01 E02 win0 xc11 qh0 sp11 xc13 an12 E10 xc15 xc14 -s21 an13 b11 sp13 cw0 sp14
+E12 E11 E13 nam0 sp15 E14 E15 no1 mid0 win1 cw1 s20 stx0 pre1 cnt1 nam1 clr11""".split()
+VECTOR = "b11:bo cv01:Qw cw1:wo in0:r16 mk0:mk nam0:pq s20:nw stq1:nw stx0:nw u0:co u0:sq xs00:xs xs03:xs xs12:xw xs13:xw".split()
+FIRM = ["D11p", "E15p", "win1p", "x121a", "xs03v"]
 _GRID = {}
 
 
@@ -187,10 +188,10 @@ def build(steps=None):
     S = slice
     ALL = S(None)
     zr = lambda z, k: r("Z", z, S(15 - k, 143 - k))
-    ONE, NEG, TWO, HALF, NHALF, N15 = (r("Id", j, ALL) for j in range(6))
+    ONE, NEG, TWO, HALF, NHALF = (r("Id", j, ALL) for j in range(5))
     G32, G64, GN32, GN16 = (r("B8", j, ALL) for j in range(4))
     RC, R16, KP, K1, AC, WH = (r("col", j, S(0, 1)) for j in range(6))
-    REP8, REP4, REP16, EXP = c("lst", 0, 8), c("lst", 0, 2), c("lst", 16, 32), c("lst", 32, 40)
+    REP8, REP4, LAST, REP16, EXP = c("lst", 0, 8), c("lst", 0, 2), c("lst", 8, 14), c("lst", 16, 32), c("lst", 32, 40)
     XW, QW, QX, IX, DIAG = r("X", ALL), c("Qw", 0, 4096), r("Qw", ALL), r("Iw", ALL), c("MW", 0, 128)
     bank = [0]
 
@@ -210,12 +211,12 @@ def build(steps=None):
     asel(ONE, r("one", ALL), [[-1, 128]], ALU.is_equal, 0, 1)
     asel(r("Z", 0, ALL), r("Z", 0, ALL), [[-1, 144]], ALU.is_ge, 15, 1)
     asel(r("Z", 0, ALL), r("Z", 0, ALL), [[1, 144]], ALU.is_ge, 0, -1)
-    iota(c("tf", 0, 96), [[256, 8], [1, 12]], 1 - 2048)
     dma("g", r("wk", 0, S(0, 1)), "wt", ALL, "lw", 32, 2500)
     dma("g", r("wk", 1, S(0, 1)), "kap", ALL, "lw", 32, 2500)
+    iota(c("tf", 0, 96), [[256, 8], [1, 12]], 1 - 2048)
     ts(c("pi", 8, 16), c("pi", 8, 16), 15, None, ALU.bitwise_and)
     ts(c("pi", 0, 8), c("pi", 0, 8), 7, None, ALU.bitwise_and)
-    cp(c("r16", 0, 256), r("ri", ALL))
+    cp(c("r16", 0, 128), c("ri", 0, 128), 1.0, "a")
     cp(RC, c("pi", 8, 9))
     ts(R16, c("pi", 8, 9), 16.0, None, ALU.mult)
     ts(K1, c("pi", 8, 9), 1.0, None, ALU.add)
@@ -223,22 +224,28 @@ def build(steps=None):
     cp(REP8, c("pi", 0, 8))
     cp(REP16, c("ec", 0, 16))
     cp(EXP, c("ec", 0, 8))
-    for m, f in ((NEG, -1.0), (TWO, 2.0), (HALF, 0.5), (NHALF, -0.5), (N15, -1.5)):
-        cp(m, ONE, f, "a")
+    for m, f in ((NEG, -1.0), (TWO, 2.0), (HALF, 0.5), (NHALF, -0.5)):
+        cp(m, ONE, f)
     cp(r("Z", 1, ALL), r("Z", 0, ALL), -1.0, "a")
     for m, f in ((G32, 32.0), (G64, 64.0), (GN32, -32.0), (GN16, -16.0), (r("TS", 0, S(0, 8)), 128.0), (r("TS", 0, S(8, 16)), 8.0)):
-        cp(m, r("Z", 0, S(15, 143, 16)), f, "a")
+        cp(m, r("Z", 0, S(15, 143, 16)), f)
     ts(r("cD", ALL), c("tf", 0, 96), R16, None, ALU.add)
     ms(r("rsD", ALL), 1.0); ms(c("rsD", 0, 96, 12), 0.0)
-    ms(r("Jc", ALL), 0.0); ms(c("Jc", 8, 16), 1.0); ms(c("Jc", 16, 24), 2.0); ms(c("Jc", 24, 32), -1.0)
+    ms(r("Jc", ALL), 0.0); ms(c("Jc", 0, 8), 1.0); ms(c("Jc", 8, 16), 2.0); ms(c("Jc", 24, 32), -1.0)
     ts(c("MW", 0, 256), r("ec", ALL), RC, None, ALU.is_equal)
     for n in (256, 512, 1024):
-        cp(c("MW", n, 2 * n), c("MW", 0, n))
+        cp(c("MW", n, 2 * n), c("MW", 0, n), 1.0, "a")
     ts(r("TS", 1, S(0, 8)), c("ec", 0, 8), 16.0, RC, ALU.mult, ALU.add)
     cp(r("TS", 1, S(8, 16)), c("ec", 0, 8))
     ts(WH, r("wk", 0, S(0, 1)), 0.5, None, ALU.mult)
     cp(KP, r("wk", 1, S(0, 1)))
     ts(r("Z", 3, ALL), r("Z", 0, ALL), WH, None, ALU.mult)
+    cp(r("Z", 4, ALL), r("Z", 3, ALL), 2.0, "a")
+    iota(r("cU", ALL), [[0, 8], [-1, 12]], 12)
+    cp(r("cU", ALL), r("cU", ALL), 2.0 ** 20, "a")
+    ts(c("us", 0, 6), r("TS", 1, S(0, 6)), 1.0 / 12, -5.5 / 12, ALU.mult, ALU.add)
+    ts(LAST, c("us", 0, 6), 12.0, 11.0, ALU.mult, ALU.add)
+    ms(c("scD0", 0, 8), 0)
     inside = lambda out, in_: (asel(out, in_, [[-16, 8], [0, 16]], ALU.is_ge, 0, 1), asel(out, out, [[16, 8], [0, 16]], ALU.is_ge, 15, -1))
     inside(r("BO", ALL), r("one", ALL))
     iota(r("kapE", ALL), [[1, 16], [0, 8]], 0)
@@ -247,33 +254,42 @@ def build(steps=None):
     cp(r("kapE", ALL), c("pq1", 0, 128), 1.0, "a")
     for h in range(2):
         ms(c("pq%d" % h, 145, 272, 18), 0.0)
-    cp(r("Kc", ALL), r("BO", ALL), -(8192.0 + QSH), "a")
-    d0, d1, d2, d3 = (r("dd", j, ALL) for j in range(4))
-    ts(d0, c("ec", 0, 128), K1, -1.0, ALU.subtract, ALU.add)
-    inside(d0, d0)
-    ts(d1, d0, -1.0, 8192.0, ALU.is_le, ALU.mult)
-    ts(d2, d0, -1.0, BIG - 8192.0, ALU.is_lt, ALU.mult)
-    tt(r("Wa", ALL), d1, d2, ALU.add)
-    ts(d1, d0, 1.0, BIG, ALU.is_gt, ALU.mult)
-    ts(d2, d0, -1.0, 32.0, ALU.is_equal, ALU.mult)
-    tt(r("Wb", ALL), d1, d2, ALU.add)
-    ts(d3, d0, 1.0, 37.0, ALU.is_gt, ALU.mult)
-    tt(r("Kw", ALL), d3, c("ec", 0, 128), ALU.mult)
     ms(r("dE", ALL), -1.0); ms(c("dE", 16, 144, 18), 16.0); ms(c("dE", 17, 144, 18), FAR)
     ms(r("rs16", ALL), 1.0); ms(c("rs16", 0, 128, 16), 0.0)
-    iota(r("nb", ALL), [[16, 16]], 4096)
-    for h in range(2):
-        ts(c("ct%d" % h, 0, 8), c("nb", 8 * h, 8 * h + 8), RC, None, ALU.add)
-    ts(r("nb", ALL), r("nb", ALL), -4096.0, RC, ALU.add, ALU.add)
-    ts(r("nb", ALL), r("nb", ALL), 16.0, None, ALU.mult)
     ms(c("Iw", 4096, 4352), 0.0)
-    ts(r("Z", 2, ALL), r("Z", 0, ALL), K1, None, ALU.mult)
+
+    def s_set(v, h, j):
+        if v > 0:
+            return
+        if j == 1:
+            for a in range(0, 4096, 512):
+                iota(c("Iw", a, a + 512), [[1, 512]], a)
+            return
+        d0, d1, d2, d3 = (r("dd", j, ALL) for j in range(4))
+        cp(r("Kc", ALL), r("BO", ALL), -(8192.0 + QSH), "a")
+        ts(d0, c("ec", 0, 128), K1, -1.0, ALU.subtract, ALU.add)
+        inside(d0, d0)
+        ts(d1, d0, -1.0, 8192.0, ALU.is_le, ALU.mult)
+        ts(d2, d0, -1.0, BIG - 8192.0, ALU.is_lt, ALU.mult)
+        tt(r("Wa", ALL), d1, d2, ALU.add)
+        ts(d1, d0, 1.0, BIG, ALU.is_gt, ALU.mult)
+        ts(d2, d0, -1.0, 32.0, ALU.is_equal, ALU.mult)
+        tt(r("Wb", ALL), d1, d2, ALU.add)
+        ts(d3, d0, 1.0, 37.0, ALU.is_gt, ALU.mult)
+        tt(r("Kw", ALL), d3, c("ec", 0, 128), ALU.mult)
+        iota(r("nb", ALL), [[16, 16]], 4096)
+        for h in range(2):
+            ts(c("ct%d" % h, 0, 8), c("nb", 8 * h, 8 * h + 8), RC, None, ALU.add)
+        ts(r("nb", ALL), r("nb", ALL), -4096.0, RC, ALU.add, ALU.add)
+        ts(r("nb", ALL), r("nb", ALL), 16.0, None, ALU.mult)
+        ts(r("Z", 2, ALL), r("Z", 0, ALL), K1, None, ALU.mult)
 
     def old_names(v, h, a=0, b=128):
         return c("r16", 256 * v + 128 * h + a, 256 * v + 128 * h + b)
 
     def cand(name, h, a, b):
-        return c(name + str(h), 128 * a, 128 * b)
+        at = 256 * (name == "xc")
+        return c(name + str(h), 128 * a + at, 128 * b + at)
 
     def nm(h, j):
         return r("nm%d" % h, j, ALL)
@@ -284,59 +300,87 @@ def build(steps=None):
     def s_cv(v, h, j):
         if v == 0:
             aff(c("Qw", 1024 * j, 1024 * j + 1024), c("qi", 1024 * j, 1024 * j + 1024), 1.0, -QSH)
-            iota(c("Iw", 1024 * j, 1024 * j + 1024), [[1, 1024]], 1024 * j)
 
     def s_xs(v, h, j):
-        a, b = 128 * j // P["xs"][h], 128 * (j + 1) // P["xs"][h]
-        cp(c("xs%d" % h, 16 * a, 16 * b), ind(XW, old_names(v, h, a, b)), 1.0, "va")
+        if h:
+            cp(c("xw1", 512 * j, 512 * j + 512), ind(XW, old_names(v, h, 32 * j, 32 * j + 32)), 1.0, "va")
+            return
+        for t in (2 * j, 2 * j + 1):
+            cp(r("xs0", t, ALL), ind(XW, old_names(v, h, 16 * t, 16 * t + 16)), 1.0, "va")
+
+    def s_in(v, h, j):
+        if v == 0:
+            ops[cp(old_names(0, 1), c("ri", 128, 256), 1.0, "va")]["R"].append(r("xs0", ALL, ALL))
+
+    def s_xw(v, h, j):
+        out, in_ = r("xw%d" % h, ALL), r("xs%d" % h, ALL, ALL)
+        i = add("move", (out, in_), {"s": (60.0, 0, "")}, [in_], [out])
+        ops[i]["sem"], ops[i]["done"] = ("mv%d%d" % (v, h), 16), None
 
     def s_D(v, h, w):
         H = str(h)
-        dif = lambda k, a, b: [(ONE, c("xs" + H, a + k + 1, b, 16)), (NEG, c("xs" + H, a + k, b, 16))]
+        at = lambda k, t: c("xw1", k, 2048, 16) if h else r("xs0", t, S(k, 256, 16))
+        dif = lambda k, t: [(ONE, at(k + 1, t)), (NEG, at(k, t))]
         keys = lambda a, b, t: mm(c("pq" + H, a, b), [(ONE, c("cD", a, b))] + [(zr(1, k), r("adD" + H, t, ALL, k)) for k in range(16)])
         pb = next_bank()
         if P["dsplit"][h]:
-            a, tw = 1024 * w, S(4 * w, 4 * w + 4)
-            mms([(r(pb, S(l // 4, 8, 2), l % 4, ALL), dif(1 + l, a, a + 1024)) for l in range(8)])
+            tw = S(4 * w, 4 * w + 4)
+            mms([(r(pb, S(l // 4, 8, 2), l % 4, ALL), dif(1 + l, tw)) for l in range(8)])
             act(r("adD" + H, tw, S(0, 8), ALL), r(pb, ALL), AF.Abs, scale=2048.0)
             pb = next_bank()
-            mms([(r(pb, S(0, 4), l, ALL), dif(9 + l, a, a + 1024)) for l in range(4)])
+            mms([(r(pb, S(0, 4), l, ALL), dif(9 + l, tw)) for l in range(4)])
             act(r("adD" + H, tw, S(8, 12), ALL), r(pb, S(0, 4)), AF.Abs, scale=2048.0)
             keys(48 * w, 48 * w + 48, tw)
         else:
-            mms([(r(pb, ALL, l, ALL), dif(4 * w + 1 + l, 0, 2048)) for l in range(4)])
+            mms([(r(pb, ALL, l, ALL), dif(4 * w + 1 + l, ALL)) for l in range(4)])
             act(r("adD" + H, ALL, S(4 * w, 4 * w + 4), ALL), r(pb, ALL), AF.Abs, scale=2048.0)
             if w == 2:
                 keys(0, 96, ALL)
 
     def s_p(v, h, j):
         H = str(h)
-        scan(r("scD" + H, ALL), r("rsD", ALL), c("pq" + H, 0, 96), ALU.mult, ALU.min)
-        ts(c("mq" + H, 0, 8), c("scD" + H, 11, 96, 12), 2047, None, ALU.bitwise_and)
-        tt(r("off" + H, ALL), ind(c("mq" + H, 0, 8), REP4), r("Jc", ALL), ALU.add)
+        if j == 0:
+            for out in ["scD" + H] + ["ends"] * (1 - h):
+                scan(c(out, 8, 104), r("rsD", ALL), c("pq" + H, 0, 96), ALU.mult, ALU.min)
+        else:
+            ts(c("mq" + H, 0, 8), c("scD" + H, 19, 104, 12), 2047, None, ALU.bitwise_and)
+            tt(r("off" + H, ALL), ind(c("mq" + H, 0, 8), REP4), r("Jc", ALL), ALU.add)
+
+    def s_ws(v, h, j):
+        mm(c("pq%d" % h, 400, 496), [(ONE, r("cU", ALL))] + [(zr(4, k), r("xs%d" % h, ALL, S(16 * k + 1, 16 * k + 13))) for k in range(16)])
 
     def s_u(v, h, j):
         H = str(h)
-        cp(cand("xc", h, 0, 1), ind(r("xs" + H, ALL), c("off" + H, 0, 8)), 2.0, "va")
-        mm(c("pq" + H, 96, 104), [(zr(3, k), c("xc" + H, k, 128, 16)) for k in range(16)])
-        u = r("ui" + H, ALL)
-        aff(u, c("pq" + H, 96, 104), 1.0, 0.0)
-        ts(u, u, 4095, None, ALU.bitwise_and)
+        u = c("ui", 8 * h, 8 * h + 8)
+        if h == 0:
+            tt(r("hold", ALL), ind(c("ends", 8, 104), LAST), c("scD0", 7, 103), ALU.is_equal)
+            scan(r("us", ALL), r("hold", ALL), c("pq0", 400, 496), ALU.mult, ALU.max)
+            ts(u, c("us", 11, 96, 12), 4095, None, ALU.bitwise_and)
+        else:
+            mm(c("pq1", 96, 104), [(zr(3, k), c("xc1", 256 + k, 384, 16)) for k in range(16)])
+            aff(u, c("pq1", 96, 104), 1.0, 0.0)
+            ts(u, u, 4095, None, ALU.bitwise_and)
         tt(c("sq" + H, 0, 8), u, u, ALU.mult)
         tt(r("ku" + H, ALL), ind(u, REP8), r("kapE", ALL), ALU.mult)
         aff(c("sq" + H, 8, 16), c("sq" + H, 0, 8), 1.0 / 32, AC)
         tt(r("cs" + H, ALL), ind(c("sq" + H, 8, 16), REP8), r("ku" + H, ALL), ALU.add)
         ts(c("ct" + H, 8, 136), r("cs" + H, ALL), 4095, None, ALU.bitwise_and)
-        aff(r("co" + H, ALL), c("ct" + H, 8, 136), 1.0, 0.0)
+        if P["co"][h] == "g":
+            gcp(r("co" + H, ALL), c("ct" + H, 8, 136))
+        else:
+            aff(r("co" + H, ALL), c("ct" + H, 8, 136), 1.0, 0.0)
 
     def s_mk(v, h, j):
         H = str(h)
-        cp(c("mk" + H, 0, 128), ind(r("MW", ALL), c("off" + H, 24, 32)), 1.0, "a")
-        gcp(c("mk" + H, 128, 256), c("mk" + H, 0, 128))
-        gcp(c("mk" + H, 256, 512), c("mk" + H, 0, 256))
+        cp(c("mk" + H, 0, 128), ind(r("MW", ALL), c("off" + H, 24, 32)), 1.0, "va")
+        for n in (128, 256):
+            if P["mk"][h] == "g":
+                gcp(c("mk" + H, n, 2 * n), c("mk" + H, 0, n))
+            else:
+                cp(c("mk" + H, n, 2 * n), c("mk" + H, 0, n))
 
     def s_x12(v, h, j):
-        cp(r("x12%d" % h, ALL), ind(r("xs%d" % h, ALL), c("off%d" % h, 8, 24)), 2.0, "a")
+        cp(cand("xc", h, -2, 1 - h), ind(r("xw%d" % h, ALL), c("off%d" % h, 0, 24 - 8 * h)), 2.0, "a")
 
     def s_an(v, h, j):
         H = str(h)
@@ -344,7 +388,7 @@ def build(steps=None):
 
     def s_b(v, h, a):
         H = str(h)
-        lo, hi = (32 * x for x in P["b"][a])
+        lo, hi = (32 * x for x in P["b"][h][a])
         out = c("pq" + H, lo, hi)
         mm(out, [(zr(0, k), c("anc" + H, 16 * lo + k, 16 * hi, 16)) for k in range(16)])
         aff(c("bo" + H, lo, hi), out, 1.0, QSH)
@@ -352,49 +396,54 @@ def build(steps=None):
     def s_pre(v, h, j):
         pb, mk = next_bank(), c("mk%d" % h, 0, 128)
         w = lambda j: r(pb, S(2 * j, 2 * j + 2), ALL, ALL)
-        aff(c("Qw", 4096 + 128 * h, 4224 + 128 * h), old_names(v, h), 1.0, -(16384.0 + QSH))
+        if h == 0:
+            aff(c("Qw", 4096, 4352), old_names(v, 0, 0, 256), 1.0, -(16384.0 + QSH))
         mms([(w(0), [(r("Wa", ALL), mk)]), (w(1), [(r("Kw", ALL), mk), (r("Kc", ALL), mk)]), (w(2), [(r("Wb", ALL), mk)])])
         tt(nm(h, 0), w(0), old_names(v, h), ALU.max)
         tt(nm(h, 1), w(1), nm(h, 0), ALU.add)
         tt(nm(h, 2), w(2), nm(h, 0), ALU.min)
 
     def s_xc(v, h, j):
-        m0, m1 = P["blocks"][h][j]
-        cp(cand("xc", h, m0, m1), ind(XW, c("co%d" % h, 8 * m0 - 8, 8 * m1 - 8)), 2.0, "va")
+        m0, m1 = P["runs"][h][j]
+        x = ind(XW, c("co%d" % h, 8 * m0 - 8, 8 * m1 - 8)) if j else ind(r("xw%d" % h, ALL), c("off%d" % h, 16, 24))
+        cp(cand("xc", h, m0, m1), x, 2.0, "va")
 
     def s_sp(v, h, j):
-        m0, m1 = P["blocks"][h][j]
-        xb = ind(XW, c("bo%d" % h, 8 * m0 - 8, 8 * m1 - 8)) if j else ind(r("xs%d" % h, ALL), c("off%d" % h, 24, 32))
-        if P["am"][h][j] == "r":
-            cp(cand("sp", h, m0, m1), xb, 1.0, "a")
-        else:
-            tt(cand("sp", h, m0, m1), xb, cand("xc", h, m0, m1), ALU.subtract)
+        m0, m1 = P["runs"][h][j]
+        xb = ind(XW, c("bo%d" % h, 8 * m0 - 8, 8 * m1 - 8)) if j else ind(r("xw%d" % h, ALL), c("off%d" % h, 24, 32))
+        tt(cand("sp", h, m0, m1), xb, cand("xc", h, m0, m1), ALU.subtract)
 
     def s_px(v, h, j):
         if "v" in P["am"][h]:
-            mms([(c("px", 128 * m, 128 * m + 128), [(NHALF, cand("x12", h, 0, 1))]) for m in range(4)])
+            mms([(c("px", 128 * m, 128 * m + 128), [(NHALF, cand("xc", h, -2, -1))]) for m in range(4)])
 
     def s_E(v, h, j):
         m0, m1 = P["blocks"][h][j]
-        x1, x2 = cand("x12", h, 0, 1), cand("x12", h, 1, 2)
-        one, raw = lambda name, m: cand(name, h, m, m + 1), P["am"][h][j] == "r"
+        x1, x2 = cand("xc", h, -2, -1), cand("xc", h, -1, 0)
+        one = lambda name, m: cand(name, h, m, m + 1)
         part = lambda pb, a, b: r(pb, S(2 * (a - m0), 2 * (b - m0)), ALL, ALL)
+        if j == 0:
+            pb = next_bank()
+            mms([(part(pb, 0, 1), [(HALF, x1), (ONE, one("sp", 0))]), (part(pb, 1, 2), [(HALF, x2), (HALF, one("xc", 0)), (TWO, one("sp", 0))])])
+            act(cand("own", h, 0, 2), part(pb, 0, 2), AF.Abs)
+            mm(c("pq%d" % h, 128, 272, 18), [(one("own", 0), G32), (one("own", 1), G32)] + [(x1, GN16)] * ("v" in P["am"][h]))
+            return
         if P["am"][h][j] == "v":
             tt(cand("am", h, m0, m1), c("px", 0, 128 * (m1 - m0)), cand("sp", h, m0, m1), ALU.max)
             first = lambda m: [(one("am", m), G64), (one("sp", m), GN32)]
         else:
             pb = next_bank()
-            mms([(part(pb, m, m + 1), [(HALF, x1), (ONE, one("sp", m))] + [(NEG, one("xc", m))] * raw) for m in range(m0, m1)])
+            mms([(part(pb, m, m + 1), [(HALF, x1), (ONE, one("sp", m))]) for m in range(m0, m1)])
             act(cand("am", h, m0, m1), part(pb, m0, m1), AF.Abs)
             first = lambda m: [(one("am", m), G32)] + [(x1, GN16)] * ("v" in P["am"][h])
         pb = next_bank()
-        mms([(part(pb, m, m + 1), [(HALF, x2), (N15 if raw else HALF, one("xc", m)), (TWO, one("sp", m))]) for m in range(m0, m1)])
+        mms([(part(pb, m, m + 1), [(HALF, x2), (HALF, one("xc", m)), (TWO, one("sp", m))]) for m in range(m0, m1)])
         act(cand("ab", h, m0, m1), part(pb, m0, m1), AF.Abs)
         mms([(c("pq%d" % h, 128 + m, 272, 18), first(m) + [(one("ab", m), G32)]) for m in range(m0, m1)])
 
     def s_win(v, h, j):
         H = str(h)
-        mq = r("mq" + H, ALL)
+        mq = c("won", 8 * h, 8 * h + 8)
         scan(r("sc" + H, ALL), c("pq" + H, 128, 272), r("dE", ALL), ALU.min, ALU.add, FAR)
         ts(mq, c("sc" + H, 16, 144, 18), 31, None, ALU.bitwise_and)
         tt(r("lw" + H, ALL), ind(mq, EXP), DIAG, ALU.mult)
@@ -403,7 +452,7 @@ def build(steps=None):
 
     def s_mid(v, h, j):
         H = str(h)
-        tt(r("mid" + H, ALL), ind(r("xc" + H, ALL), c("wo" + H, 0, 8)), cand("x12", h, 0, 1), ALU.add)
+        tt(r("mid" + H, ALL), ind(cand("xc", h, 0, 17), c("wo" + H, 0, 8)), cand("xc", h, -2, -1), ALU.add)
         aff(r("mid" + H, ALL), r("mid" + H, ALL), 0.25, -0.25)
 
     def s_cw(v, h, j):
@@ -422,23 +471,25 @@ def build(steps=None):
         ts(ni(h, 1), ni(h, 1), 5, 4095, ALU.arith_shift_right, ALU.bitwise_and)
         if v < NV - 1:
             sb = c("s16", 256 * v + 128 * h, 256 * v + 128 * h + 128)
-            aff(sb, ni(h, 1), 1.0, 0.0)
+            if P["s16"][h] == "g":
+                gcp(sb, ni(h, 1))
+            else:
+                aff(sb, ni(h, 1), 1.0, 0.0)
             land, sem = old_names(v + 1, h), "ar%d%d" % (v + 1, h)
             i = add("send", (land, sb, sem), {"g": (300.0, 0, "")}, [sb], [land])
             ops[i]["sem"] = (sem, None)
             ops[i]["done"] = None
         else:
-            aff(c("yrf", 128 * h, 128 * h + 128), ni(h, 1), 1.0, 0.0)
+            gcp(c("yrf", 128 * h, 128 * h + 128), ni(h, 1))
             dma("s", c("yrf", 128 * h, 128 * h + 128), "yr", S(128 * h, 128 * h + 128), "or" + H, 16)
 
     def s_no(v, h, j):
-        H = str(h)
         if v < NV - 1:
-            ts(r("ne" + H, ALL), r("ui" + H, ALL), 15, None, ALU.bitwise_and)
-            tt(c("no", 8 * h, 8 * h + 8), r("ne" + H, ALL), c("nb", 8 * h, 8 * h + 8), ALU.add)
-        elif h == 1:
+            ts(r("ne", ALL), r("ui", ALL), 15, None, ALU.bitwise_and)
+            tt(r("no", ALL), r("ne", ALL), r("nb", ALL), ALU.add)
+        else:
             out, ei = r(next_bank(), 0, 0, ALL), r("ei", ALL)
-            mm(out, [(zr(3, t), c("xc%d" % (t // 8), 16 * (t % 8), 16 * (t % 8) + 16)) for t in range(16)])
+            mm(out, [(zr(3, t), c("xc%d" % (t // 8), 256 + 16 * (t % 8), 272 + 16 * (t % 8))) for t in range(16)])
             cp(ei, out)
             ts(ei, ei, 15, None, ALU.bitwise_and)
             tt(r("eq", 0, ALL), ind(ei, REP16), r("ec", ALL), ALU.is_equal)
@@ -449,52 +500,55 @@ def build(steps=None):
             cp(ind(XW, c("no", 8 * h, 8 * h + 8)), r("mid%d" % h, ALL))
         else:
             aff(r("nw", 1, S(128 * h, 128 * h + 128)), r("mid%d" % h, ALL), 1.0, 0.0)
-            if h == 1:
-                new_sums(1)
+            new_sums(h, 1)
 
     def s_s2(v, h, j):
-        src = c("s16", 256 * v + 128 * h, 256 * v + 128 * h + 128) if v < NV - 1 else ni(h, 1)
-        aff(r("nw", 0, S(128 * h, 128 * h + 128)), src, 1.0, -QSH)
+        if v == NV - 1:
+            aff(r("nw", 0, S(128 * h, 128 * h + 128)), ni(h, 1), 1.0, -QSH)
+            new_sums(h, 0)
 
     def s_stq(v, h, j):
         if v < NV - 1:
+            aff(r("nw", 0, ALL), c("s16", 256 * v, 256 * v + 256), 1.0, -QSH)
             cp(ind(QW, r("no", ALL)), r("nw", 0, ALL))
-        else:
-            new_sums(0)
-
-    def s_sg(v, h, j):
-        if v < NV - 1:
-            act(c("sg", 8 * h, 8 * h + 8), r("mq%d" % h, ALL), AF.Sign)
 
     def s_cnt(v, h, j):
-        if v < NV - 1 and h == 1:
+        if v < NV - 1:
             out = r(next_bank(), 0, 0, ALL)
+            act(r("sg", ALL), r("won", ALL), AF.Sign)
             mm(out, [(r("one", ALL), r("sg", ALL))])
             act(r("junk", ALL), out, AF.Identity, bias=-0.375 / 16, acc=AC)
 
-    def new_sums(a):
+    def new_sums(h, a):
         out, new, f = r(next_bank(), 0, 0, ALL), c("nsb", 16 * a, 16 * a + 16), r("fin", a, ALL)
-        mm(out, [(zr(2, t), r("nw", a, S(16 * t, 16 * t + 16))) for t in range(16)])
-        aff(new, out, 1.0, 136 * QSH if a == 0 else 0.0)
+        mm(out, [(zr(2, t), r("nw", a, S(16 * t, 16 * t + 16))) for t in range(8 * h, 8 * h + 8)])
+        if h == 0:
+            aff(new, out, 1.0, 136 * QSH if a == 0 else 0.0)
+            return
+        tt(new, out, new, ALU.add)
         tt(f, ind(new, REP16), r("eq", 0, ALL), ALU.mult)
-        tt(f, f, r("pre", a, ALL), ALU.add)
+        tt(f, c("pq0", 256 * a, 256 * a + 256), f, ALU.add)
         dma("s", f, ("yq", "yx")[a], ALL, ("oq", "ox")[a], 16)
 
     def s_qh(v, h, j):
         if v == NV - 1:
-            for a in range(0, 4096, 512):
-                gcp(c("Qh", a, a + 512), c("Qw", a, a + 512))
+            for a in range(0, 4096, 256):
+                gcp(c("Qh", a, a + 256), c("Qw", a, a + 256))
 
     def s_old(v, h, a):
         if v == NV - 1:
-            out, pre = r(next_bank(), S(0, 4), ALL, ALL), r("pre", a, ALL)
-            mm(out, [(zr(2, t), c(("Qh", "X")[a], 256 * t, 256 * t + 256)) for t in range(16)])
-            act(pre, out, AF.Identity, bias=136 * QSH if a == 0 else 0.0)
-            tt(pre, pre, r("eq", 1, ALL), ALU.mult)
+            pb = next_bank()
+            for q in range(4):
+                mm(r(pb, q, ALL, ALL), [(zr(2, t), c(("Qh", "X")[a], 256 * t + 64 * q, 256 * t + 64 * q + 64)) for t in range(16)])
+            act(r("pre", a, ALL), r(pb, S(0, 4), ALL, ALL), AF.Identity, bias=136 * QSH if a == 0 else 0.0)
 
-    table = {"cv": s_cv, "xs": s_xs, "D": s_D, "p": s_p, "u": s_u, "mk": s_mk, "x12": s_x12, "an": s_an, "b": s_b,
+    def s_clr(v, h, a):
+        if v == NV - 1:
+            tt(c("pq0", 256 * a, 256 * a + 256), r("pre", a, ALL), r("eq", 1, ALL), ALU.mult)
+
+    table = {"cv": s_cv, "xs": s_xs, "D": s_D, "p": s_p, "ws": s_ws, "xw": s_xw, "in": s_in, "u": s_u, "mk": s_mk, "x12": s_x12, "an": s_an, "b": s_b,
              "pre": s_pre, "xc": s_xc, "sp": s_sp, "px": s_px, "E": s_E, "win": s_win, "mid": s_mid, "cw": s_cw, "nam": s_nam,
-             "no": s_no, "stx": s_stx, "s2": s_s2, "stq": s_stq, "sg": s_sg, "cnt": s_cnt, "qh": s_qh, "old": s_old}
+             "no": s_no, "stx": s_stx, "s2": s_s2, "stq": s_stq, "cnt": s_cnt, "qh": s_qh, "old": s_old, "clr": s_clr, "set": s_set}
     steps = steps or ORDER
     names = [step.lstrip("-") for step in steps]
     held = {}
@@ -541,7 +595,7 @@ def depend(ops):
 
 
 def _lag(op):
-    return {"send": HOP, "dma": 2200.0}.get(op["k"], 0.0)
+    return {"send": HOP, "dma": 2200.0, "move": 4500.0}.get(op["k"], 0.0)
 
 
 def place(ops, deps, rank=None, eng=None):
@@ -560,6 +614,8 @@ def place(ops, deps, rank=None, eng=None):
     free, order = {e: 0.0 for e in "vapgs"}, {e: [] for e in "vapgs"}
     start, end = [0.0] * n, [0.0] * n
     ready = {i: 0.0 for i in range(n) if not left[i]}
+    firm = {e: sorted((i for i in range(n) if eng[i] == e and ops[i]["t"] + e in FIRM),
+                      key=lambda x: rank[x], reverse=True) for e in free}
 
     def after(j, e, raw):
         return end[j] + (LAT_X if eng[j] != e or "sem" in ops[j] else LAT_S if raw else 0.0)
@@ -567,6 +623,8 @@ def place(ops, deps, rank=None, eng=None):
     while ready:
         can = {}
         for i, s in ready.items():
+            if firm[eng[i]] and rank[firm[eng[i]][-1]] < rank[i]:
+                continue
             for b in ops[i]["B"]:
                 b = lent.get(b) or (b if b[:2] != "pb" else idle[0] if idle else None)
                 s = max(s, after(last[b], eng[i], False) if b in last else 0.0) if b else 1e18
@@ -575,6 +633,8 @@ def place(ops, deps, rank=None, eng=None):
         e = eng[first]
         i = min((x for x in can if eng[x] == e and can[x] <= can[first] + SLACK), key=lambda x: rank[x])
         del ready[i]
+        if i in firm[e][-1:]:
+            firm[e].pop()
         op = ops[i]
         for b in op["B"]:
             if b[:2] == "pb" and b not in lent:
@@ -679,6 +739,8 @@ def rank_program(g, core, T, topo):
                 ins = q.tensor_scalar(ap(a[0]), ap(a[1]), a[2], None, ALU.mult)
             elif k == "gcp":
                 ins = q.affine_select(ap(a[0]), ap(a[1]), [[0, _n(a[0])]], ALU.is_ge, 0.0, 0, 0)
+            elif k == "move":
+                q.dma_start(ap(a[0]), ap(a[1])).then_inc(T.sem[op["sem"][0]], 16)
             elif k == "aff" and e == "a":
                 ins = q.activation(ap(a[0]), ap(a[1]), AF.Identity, bias=ap(a[3]), scale=a[2])
             elif k == "aff" and a[2] == 1.0 and a[3] == 0.0:

import numpy as np
from concourse.mybir import AluOpType, ActivationFunctionType

ALU = AluOpType
AF = ActivationFunctionType
F32, BF, F16, I32, U16 = "float32", "bfloat16", "float16", "int32", "uint16"
NV = 5
BIG = 32768.0
QSH = 2048.0
FAR = 1e7

SCRATCH = {}


def _sb(name, cols, dtype):
    SCRATCH[name] = ("sbuf", [128] + list(cols), dtype)


_sb("X", [4096], BF); _sb("Qw", [4352], F32); _sb("Iw", [4352], F32); _sb("qi", [4096], I32); _sb("Qh", [4096], F16)
_sb("ri", [256], I32); _sb("r16", [256 * NV], U16); _sb("s16", [256 * (NV - 1)], U16); _sb("wk", [2, 4], I32)
_sb("no", [16], U16); _sb("nw", [2, 256], F16); _sb("ei", [16], I32); _sb("kapE", [128], F32)
_sb("eq", [2, 256], F32); _sb("pre", [2, 256], F32); _sb("fin", [2, 256], F32); _sb("nsb", [32], F32)
_sb("ui", [16], I32); _sb("ne", [16], I32); _sb("won", [16], I32)
for _h in "01":
    _sb("xw" + _h, [2048], BF); _sb("adD" + _h, [8, 12, 16], BF); _sb("scD" + _h, [104], I32)
    _sb("off" + _h, [32], U16); _sb("xc" + _h, [2432], BF); _sb("own" + _h, [256], F16); _sb("mk" + _h, [512], BF)
    _sb("sq" + _h, [16], I32); _sb("ku" + _h, [128], F32); _sb("cs" + _h, [128], I32); _sb("ct" + _h, [136], I32)
    _sb("co" + _h, [128], U16); _sb("anc" + _h, [2048], F16); _sb("bo" + _h, [128], U16); _sb("sp" + _h, [2176], F16)
    _sb("am" + _h, [2176], F16); _sb("ab" + _h, [2176], F16); _sb("sc" + _h, [144], I32)
    _sb("mq" + _h, [8], I32); _sb("lw" + _h, [128], BF); _sb("wo" + _h, [24], U16); _sb("mid" + _h, [128], I32)
    _sb("cm" + _h, [256], F32); _sb("nm" + _h, [4, 128], F32); _sb("ni" + _h, [2, 128], I32)
    SCRATCH["pq" + _h] = ("psum", [128, 512], F32)
SCRATCH["px"] = ("psum", [128, 512], F32)
_sb("sg", [16], BF); _sb("xs0", [8, 256], BF); _sb("hold", [96], F32); _sb("us", [96], I32); _sb("ends", [104], I32)
_sb("col", [8, 8], F32); _sb("pi", [16], I32); _sb("lst", [48], U16); _sb("Jc", [32], F32); _sb("tf", [128], F32)
_sb("cD", [96], F16); _sb("rsD", [96], F32); _sb("dE", [144], F32); _sb("rs16", [128], F32)
_sb("MW", [2048], BF); _sb("Wa", [128], BF); _sb("Wb", [128], BF); _sb("Kw", [128], F16); _sb("Kc", [128], BF)
_sb("dd", [4, 128], F32); _sb("B8", [4, 8], BF); _sb("TS", [2, 16], BF)
_sb("cU", [96], BF); _sb("Z", [5, 144], BF); _sb("Id", [6, 128], BF); _sb("one", [128], BF); _sb("BO", [128], BF)
_sb("kr", [128], F16); _sb("nb", [16], F32); _sb("ec", [256], F32); _sb("junk", [16], F32); _sb("yrf", [256], F32)
NB = 5
for _b in range(NB):
    SCRATCH["pb%d" % _b] = ("psum", [128, 8, 4, 16], F32)

OUTS = ["or0", "or1", "oq", "ox"]
SEMAPHORES = ["cv", "ca", "cp", "cg", "lw", "lr", "lx", "lq0", "lq1", "lq2", "lq3", "sent"] + OUTS + \
             ["ar%d%d" % (v, h) for v in range(1, NV) for h in range(2)] + ["mv%d0" % v for v in range(NV)]
COUNTER = {"v": "cv", "a": "ca", "p": "cp", "g": "cg"}

CYC, PEC, GAT, SCA = 0.95, 0.47, 1.56, 3.8
LAT_X, LAT_S, HOP, SLACK = 200.0, 150.0, 3600.0, 100.0
P = {"am": ["aaaaa", "aaavvv"], "b": [((0, 2), (2, 4))] * 2, "dsplit": [1, 0], "mk": "vg", "s16": "gv", "co": "vg",
     "runs": [((0, 1), (1, 5), (5, 9), (9, 13), (13, 17)), ((0, 1), (1, 5), (5, 9), (9, 13), (13, 16), (16, 17))],
     "blocks": [((0, 1), (1, 5), (5, 9), (9, 13), (13, 17)), ((0, 1), (1, 5), (5, 9), (9, 13), (13, 16), (16, 17))]}
ORDER = """-mid1 -stx1 xs02 xs03 xs00 -stq1 set00 D01 xs01 in0 D00 xs10 xs12 xs13 xs11 ws0 D10 cv01 p00 p01 cv00 D11 D12 p10 u0 p11
mk0 xw0 cv02 cv03 x120 xc02 xc10 -old10 pre0 an02 an03 old11 b01 sp00 xc03 x121 xc04 px1 u1 an01 an00 mk1 sp04 xc01 b00 E04 an10 xc12
an11 sp01 sp03 -clr10 b10 sp12 E00 sp10 E01 E03 sp02 set01 E02 win0 xc11 qh0 sp11 xc13 an12 E10 xc15 xc14 -s21 an13 b11 sp13 cw0 sp14
E12 E11 E13 nam0 sp15 E14 E15 no1 mid0 win1 cw1 s20 stx0 pre1 cnt1 nam1 clr11""".split()
VECTOR = "b11:bo cv01:Qw cw1:wo in0:r16 mk0:mk nam0:pq s20:nw stq1:nw stx0:nw u0:co u0:sq xs00:xs xs03:xs xs12:xw xs13:xw".split()
FIRM = ["D11p", "E15p", "win1p", "x121a", "xs03v"]
_GRID = {}


def r(name, *idx):
    return (name, idx, None)


def c(name, a, b, s=1):
    return (name, (slice(a, b, s),), None)


def ind(win, off):
    return (win[0], win[1], off)


def _like(ref):
    return "pb0" if ref[0][:3] == "pb_" else ref[0]


def _span(ref):
    name, idx = _like(ref), ref[1]
    if name not in _GRID:
        shp = SCRATCH[name][1][1:]
        _GRID[name] = np.arange(int(np.prod(shp))).reshape(shp)
    v = np.asarray(_GRID[name][idx]).ravel()
    return int(v.min()), int(v.max()) + 1, int(v.size)


def _bits(ref):
    key = (_like(ref), str(ref[1]))
    if key not in _GRID:
        _span(ref)
        _GRID[key] = sum(1 << int(e) for e in np.asarray(_GRID[key[0]][ref[1]]).ravel())
    return _GRID[key]


def _n(ref):
    return _span(ref[2])[2] * 16 if ref[2] is not None else _span(ref)[2]


def _two(ref):
    return SCRATCH[_like(ref)][2] in (BF, F16, U16)


def _psum(ref):
    return SCRATCH[_like(ref)][0] == "psum"


def build(steps=None):
    ops, now = [], ["init", 0]

    def add(kind, args, cost, R, W):
        rr, ww = [], []
        for x in R:
            if isinstance(x, tuple):
                rr.append(x)
                if x[2] is not None:
                    rr.append(x[2])
        for x in W:
            ww.append(x)
            if x[2] is not None:
                rr.append(x[2])
        per = {"": 1.0, "g": GAT, "s": SCA}
        if len(cost) > 1 and VECTOR is not None:
            e = "v" if now[0] + ":" + ww[0][0].rstrip("01") in VECTOR else "a"
            cost = {e: cost[e]}
        ops.append({"k": kind, "a": args, "m": cost, "R": rr, "W": ww, "t": now[0], "v": now[1] // 2, "h": now[1] % 2,
                    "n": "send" if kind == "send" else ww[0][0] if ww else "out",
                    "c": {e: f + n * per[k] * (PEC if e == "p" else CYC) for e, (f, n, k) in cost.items()}})
        return len(ops) - 1

    def vcost(out, ins, per):
        n = _n(out)
        if out[2] is not None:
            return (50, n, "s")
        if ins[0][2] is not None:
            return (50, n, "g")
        return (30, max(64, n * per), "")

    def both(out, in_, eng):
        cost = {"v": vcost(out, [in_], 0.5 if _two(out) and _two(in_) else 1), "a": (65, _n(out), "g" if in_[2] is not None else "")}
        return {e: cost[e] for e in eng}

    def cp(out, in_, scale=1.0, eng="v"):
        return add("cp", (out, in_, scale), both(out, in_, eng), [in_], [out])

    def gcp(out, in_):
        return add("gcp", (out, in_), {"g": (170, 2 * _n(out), "")}, [in_], [out])

    def tt(out, a, b, op):
        return add("tt", (out, a, b, op), {"v": vcost(out, [a], 1 if _psum(a) or _psum(b) else 2)}, [a, b], [out])

    def ts(out, a, s1, s2, op0, op1=None):
        return add("ts", (out, a, s1, s2, op0, op1), both(out, a, "v"), [a, s1, s2], [out])

    def aff(out, a, scale, bias, eng="va"):
        return add("aff", (out, a, scale, bias), both(out, a, eng), [a, bias], [out])

    def scan(out, d0, d1, op0, op1, first=0.0):
        return add("scan", (out, d0, d1, op0, op1, first), {"v": vcost(out, [d0], 1)}, [d0, d1], [out])

    def ms(out, val):
        return add("ms", (out, val), {"v": vcost(out, [out], 0.5 if _two(out) else 1)}, [], [out])

    def act(out, in_, func, bias=0.0, scale=1.0, acc=None):
        return add("act", (out, in_, func, bias, scale, acc), both(out, in_, "a"), [in_], [out] + ([acc] if acc else []))

    def mms(groups):
        terms = [x for _, t in groups for x in t]
        return add("mm", groups, {"p": (0, sum(max(64, _n(b)) for _, b in terms), "")}, [x for ab in terms for x in ab], [o for o, _ in groups])

    def mm(out, terms):
        return mms([(out, terms)])

    def iota(out, pat, base, cm=0):
        return add("iota", (out, pat, base, cm), {"g": (130, 2 * _n(out), "")}, [], [out])

    def asel(out, in_, pat, op, base, cm):
        return add("asel", (out, in_, pat, op, base, cm), {"g": (170, 2 * _n(out), "")}, [in_], [out])

    def dma(q, buf, name, cols, sem, val, done=None):
        i = add("dma", (buf, name, cols, sem, done), {q: (1000.0 if q == "g" else 60.0, 0, "")},
                [] if done else [buf], [buf] if done else [])
        ops[i]["sem"] = (sem, val)
        ops[i]["done"] = done
        return i

    S = slice
    ALL = S(None)
    zr = lambda z, k: r("Z", z, S(15 - k, 143 - k))
    ONE, NEG, TWO, HALF, NHALF = (r("Id", j, ALL) for j in range(5))
    G32, G64, GN32, GN16 = (r("B8", j, ALL) for j in range(4))
    RC, R16, KP, K1, AC, WH = (r("col", j, S(0, 1)) for j in range(6))
    REP8, REP4, LAST, REP16, EXP = c("lst", 0, 8), c("lst", 0, 2), c("lst", 8, 14), c("lst", 16, 32), c("lst", 32, 40)
    XW, QW, QX, IX, DIAG = r("X", ALL), c("Qw", 0, 4096), r("Qw", ALL), r("Iw", ALL), c("MW", 0, 128)
    bank = [0]

    def next_bank():
        bank[0] += 1
        return "pb_%d" % bank[0]

    dma("s", r("ri", ALL), "rp", ALL, "lr", 16, 2300)
    dma("s", XW, "xf", ALL, "lx", 16, 5500)
    for j in range(4):
        dma("s", c("qi", 1024 * j, 1024 * j + 1024), "pa", S(1024 * j, 1024 * j + 1024), "lq%d" % j, 16, 7200 + 1700 * j)
    iota(r("pi", ALL), [[0, 16]], 0, 1)
    iota(r("ec", ALL), [[0, 16], [1, 16]], 0)
    ms(r("one", ALL), 1.0)
    ms(r("Z", 0, ALL), 0.0)
    ms(r("Z", 0, S(15, 144, 16)), 1.0)
    asel(ONE, r("one", ALL), [[-1, 128]], ALU.is_equal, 0, 1)
    asel(r("Z", 0, ALL), r("Z", 0, ALL), [[-1, 144]], ALU.is_ge, 15, 1)
    asel(r("Z", 0, ALL), r("Z", 0, ALL), [[1, 144]], ALU.is_ge, 0, -1)
    dma("g", r("wk", 0, S(0, 1)), "wt", ALL, "lw", 32, 2500)
    dma("g", r("wk", 1, S(0, 1)), "kap", ALL, "lw", 32, 2500)
    iota(c("tf", 0, 96), [[256, 8], [1, 12]], 1 - 2048)
    ts(c("pi", 8, 16), c("pi", 8, 16), 15, None, ALU.bitwise_and)
    ts(c("pi", 0, 8), c("pi", 0, 8), 7, None, ALU.bitwise_and)
    cp(c("r16", 0, 128), c("ri", 0, 128), 1.0, "a")
    cp(RC, c("pi", 8, 9))
    ts(R16, c("pi", 8, 9), 16.0, None, ALU.mult)
    ts(K1, c("pi", 8, 9), 1.0, None, ALU.add)
    ms(AC, -0.375)
    cp(REP8, c("pi", 0, 8))
    cp(REP16, c("ec", 0, 16))
    cp(EXP, c("ec", 0, 8))
    for m, f in ((NEG, -1.0), (TWO, 2.0), (HALF, 0.5), (NHALF, -0.5)):
        cp(m, ONE, f)
    cp(r("Z", 1, ALL), r("Z", 0, ALL), -1.0, "a")
    for m, f in ((G32, 32.0), (G64, 64.0), (GN32, -32.0), (GN16, -16.0), (r("TS", 0, S(0, 8)), 128.0), (r("TS", 0, S(8, 16)), 8.0)):
        cp(m, r("Z", 0, S(15, 143, 16)), f)
    ts(r("cD", ALL), c("tf", 0, 96), R16, None, ALU.add)
    ms(r("rsD", ALL), 1.0); ms(c("rsD", 0, 96, 12), 0.0)
    ms(r("Jc", ALL), 0.0); ms(c("Jc", 0, 8), 1.0); ms(c("Jc", 8, 16), 2.0); ms(c("Jc", 24, 32), -1.0)
    ts(c("MW", 0, 256), r("ec", ALL), RC, None, ALU.is_equal)
    for n in (256, 512, 1024):
        cp(c("MW", n, 2 * n), c("MW", 0, n), 1.0, "a")
    ts(r("TS", 1, S(0, 8)), c("ec", 0, 8), 16.0, RC, ALU.mult, ALU.add)
    cp(r("TS", 1, S(8, 16)), c("ec", 0, 8))
    ts(WH, r("wk", 0, S(0, 1)), 0.5, None, ALU.mult)
    cp(KP, r("wk", 1, S(0, 1)))
    ts(r("Z", 3, ALL), r("Z", 0, ALL), WH, None, ALU.mult)
    cp(r("Z", 4, ALL), r("Z", 3, ALL), 2.0, "a")
    iota(r("cU", ALL), [[0, 8], [-1, 12]], 12)
    cp(r("cU", ALL), r("cU", ALL), 2.0 ** 20, "a")
    ts(c("us", 0, 6), r("TS", 1, S(0, 6)), 1.0 / 12, -5.5 / 12, ALU.mult, ALU.add)
    ts(LAST, c("us", 0, 6), 12.0, 11.0, ALU.mult, ALU.add)
    ms(c("scD0", 0, 8), 0)
    inside = lambda out, in_: (asel(out, in_, [[-16, 8], [0, 16]], ALU.is_ge, 0, 1), asel(out, out, [[16, 8], [0, 16]], ALU.is_ge, 15, -1))
    inside(r("BO", ALL), r("one", ALL))
    iota(r("kapE", ALL), [[1, 16], [0, 8]], 0)
    ts(r("kr", ALL), r("kapE", ALL), RC, KP, ALU.is_equal, ALU.mult)
    mm(c("pq1", 0, 128), [(r("BO", ALL), r("kr", ALL))])
    cp(r("kapE", ALL), c("pq1", 0, 128), 1.0, "a")
    for h in range(2):
        ms(c("pq%d" % h, 145, 272, 18), 0.0)
    ms(r("dE", ALL), -1.0); ms(c("dE", 16, 144, 18), 16.0); ms(c("dE", 17, 144, 18), FAR)
    ms(r("rs16", ALL), 1.0); ms(c("rs16", 0, 128, 16), 0.0)
    ms(c("Iw", 4096, 4352), 0.0)

    def s_set(v, h, j):
        if v > 0:
            return
        if j == 1:
            for a in range(0, 4096, 512):
                iota(c("Iw", a, a + 512), [[1, 512]], a)
            return
        d0, d1, d2, d3 = (r("dd", j, ALL) for j in range(4))
        cp(r("Kc", ALL), r("BO", ALL), -(8192.0 + QSH), "a")
        ts(d0, c("ec", 0, 128), K1, -1.0, ALU.subtract, ALU.add)
        inside(d0, d0)
        ts(d1, d0, -1.0, 8192.0, ALU.is_le, ALU.mult)
        ts(d2, d0, -1.0, BIG - 8192.0, ALU.is_lt, ALU.mult)
        tt(r("Wa", ALL), d1, d2, ALU.add)
        ts(d1, d0, 1.0, BIG, ALU.is_gt, ALU.mult)
        ts(d2, d0, -1.0, 32.0, ALU.is_equal, ALU.mult)
        tt(r("Wb", ALL), d1, d2, ALU.add)
        ts(d3, d0, 1.0, 37.0, ALU.is_gt, ALU.mult)
        tt(r("Kw", ALL), d3, c("ec", 0, 128), ALU.mult)
        iota(r("nb", ALL), [[16, 16]], 4096)
        for h in range(2):
            ts(c("ct%d" % h, 0, 8), c("nb", 8 * h, 8 * h + 8), RC, None, ALU.add)
        ts(r("nb", ALL), r("nb", ALL), -4096.0, RC, ALU.add, ALU.add)
        ts(r("nb", ALL), r("nb", ALL), 16.0, None, ALU.mult)
        ts(r("Z", 2, ALL), r("Z", 0, ALL), K1, None, ALU.mult)

    def old_names(v, h, a=0, b=128):
        return c("r16", 256 * v + 128 * h + a, 256 * v + 128 * h + b)

    def cand(name, h, a, b):
        at = 256 * (name == "xc")
        return c(name + str(h), 128 * a + at, 128 * b + at)

    def nm(h, j):
        return r("nm%d" % h, j, ALL)

    def ni(h, j):
        return r("ni%d" % h, j, ALL)

    def s_cv(v, h, j):
        if v == 0:
            aff(c("Qw", 1024 * j, 1024 * j + 1024), c("qi", 1024 * j, 1024 * j + 1024), 1.0, -QSH)

    def s_xs(v, h, j):
        if h:
            cp(c("xw1", 512 * j, 512 * j + 512), ind(XW, old_names(v, h, 32 * j, 32 * j + 32)), 1.0, "va")
            return
        for t in (2 * j, 2 * j + 1):
            cp(r("xs0", t, ALL), ind(XW, old_names(v, h, 16 * t, 16 * t + 16)), 1.0, "va")

    def s_in(v, h, j):
        if v == 0:
            ops[cp(old_names(0, 1), c("ri", 128, 256), 1.0, "va")]["R"].append(r("xs0", ALL, ALL))

    def s_xw(v, h, j):
        out, in_ = r("xw%d" % h, ALL), r("xs%d" % h, ALL, ALL)
        i = add("move", (out, in_), {"s": (60.0, 0, "")}, [in_], [out])
        ops[i]["sem"], ops[i]["done"] = ("mv%d%d" % (v, h), 16), None

    def s_D(v, h, w):
        H = str(h)
        at = lambda k, t: c("xw1", k, 2048, 16) if h else r("xs0", t, S(k, 256, 16))
        dif = lambda k, t: [(ONE, at(k + 1, t)), (NEG, at(k, t))]
        keys = lambda a, b, t: mm(c("pq" + H, a, b), [(ONE, c("cD", a, b))] + [(zr(1, k), r("adD" + H, t, ALL, k)) for k in range(16)])
        pb = next_bank()
        if P["dsplit"][h]:
            tw = S(4 * w, 4 * w + 4)
            mms([(r(pb, S(l // 4, 8, 2), l % 4, ALL), dif(1 + l, tw)) for l in range(8)])
            act(r("adD" + H, tw, S(0, 8), ALL), r(pb, ALL), AF.Abs, scale=2048.0)
            pb = next_bank()
            mms([(r(pb, S(0, 4), l, ALL), dif(9 + l, tw)) for l in range(4)])
            act(r("adD" + H, tw, S(8, 12), ALL), r(pb, S(0, 4)), AF.Abs, scale=2048.0)
            keys(48 * w, 48 * w + 48, tw)
        else:
            mms([(r(pb, ALL, l, ALL), dif(4 * w + 1 + l, ALL)) for l in range(4)])
            act(r("adD" + H, ALL, S(4 * w, 4 * w + 4), ALL), r(pb, ALL), AF.Abs, scale=2048.0)
            if w == 2:
                keys(0, 96, ALL)

    def s_p(v, h, j):
        H = str(h)
        if j == 0:
            for out in ["scD" + H] + ["ends"] * (1 - h):
                scan(c(out, 8, 104), r("rsD", ALL), c("pq" + H, 0, 96), ALU.mult, ALU.min)
        else:
            ts(c("mq" + H, 0, 8), c("scD" + H, 19, 104, 12), 2047, None, ALU.bitwise_and)
            tt(r("off" + H, ALL), ind(c("mq" + H, 0, 8), REP4), r("Jc", ALL), ALU.add)

    def s_ws(v, h, j):
        mm(c("pq%d" % h, 400, 496), [(ONE, r("cU", ALL))] + [(zr(4, k), r("xs%d" % h, ALL, S(16 * k + 1, 16 * k + 13))) for k in range(16)])

    def s_u(v, h, j):
        H = str(h)
        u = c("ui", 8 * h, 8 * h + 8)
        if h == 0:
            tt(r("hold", ALL), ind(c("ends", 8, 104), LAST), c("scD0", 7, 103), ALU.is_equal)
            scan(r("us", ALL), r("hold", ALL), c("pq0", 400, 496), ALU.mult, ALU.max)
            ts(u, c("us", 11, 96, 12), 4095, None, ALU.bitwise_and)
        else:
            mm(c("pq1", 96, 104), [(zr(3, k), c("xc1", 256 + k, 384, 16)) for k in range(16)])
            aff(u, c("pq1", 96, 104), 1.0, 0.0)
            ts(u, u, 4095, None, ALU.bitwise_and)
        tt(c("sq" + H, 0, 8), u, u, ALU.mult)
        tt(r("ku" + H, ALL), ind(u, REP8), r("kapE", ALL), ALU.mult)
        aff(c("sq" + H, 8, 16), c("sq" + H, 0, 8), 1.0 / 32, AC)
        tt(r("cs" + H, ALL), ind(c("sq" + H, 8, 16), REP8), r("ku" + H, ALL), ALU.add)
        ts(c("ct" + H, 8, 136), r("cs" + H, ALL), 4095, None, ALU.bitwise_and)
        if P["co"][h] == "g":
            gcp(r("co" + H, ALL), c("ct" + H, 8, 136))
        else:
            aff(r("co" + H, ALL), c("ct" + H, 8, 136), 1.0, 0.0)

    def s_mk(v, h, j):
        H = str(h)
        cp(c("mk" + H, 0, 128), ind(r("MW", ALL), c("off" + H, 24, 32)), 1.0, "va")
        for n in (128, 256):
            if P["mk"][h] == "g":
                gcp(c("mk" + H, n, 2 * n), c("mk" + H, 0, n))
            else:
                cp(c("mk" + H, n, 2 * n), c("mk" + H, 0, n))

    def s_x12(v, h, j):
        cp(cand("xc", h, -2, 1 - h), ind(r("xw%d" % h, ALL), c("off%d" % h, 0, 24 - 8 * h)), 2.0, "a")

    def s_an(v, h, j):
        H = str(h)
        tt(c("anc" + H, 512 * j, 512 * j + 512), ind(QW, c("co" + H, 32 * j, 32 * j + 32)), r("mk" + H, ALL), ALU.mult)

    def s_b(v, h, a):
        H = str(h)
        lo, hi = (32 * x for x in P["b"][h][a])
        out = c("pq" + H, lo, hi)
        mm(out, [(zr(0, k), c("anc" + H, 16 * lo + k, 16 * hi, 16)) for k in range(16)])
        aff(c("bo" + H, lo, hi), out, 1.0, QSH)

    def s_pre(v, h, j):
        pb, mk = next_bank(), c("mk%d" % h, 0, 128)
        w = lambda j: r(pb, S(2 * j, 2 * j + 2), ALL, ALL)
        if h == 0:
            aff(c("Qw", 4096, 4352), old_names(v, 0, 0, 256), 1.0, -(16384.0 + QSH))
        mms([(w(0), [(r("Wa", ALL), mk)]), (w(1), [(r("Kw", ALL), mk), (r("Kc", ALL), mk)]), (w(2), [(r("Wb", ALL), mk)])])
        tt(nm(h, 0), w(0), old_names(v, h), ALU.max)
        tt(nm(h, 1), w(1), nm(h, 0), ALU.add)
        tt(nm(h, 2), w(2), nm(h, 0), ALU.min)

    def s_xc(v, h, j):
        m0, m1 = P["runs"][h][j]
        x = ind(XW, c("co%d" % h, 8 * m0 - 8, 8 * m1 - 8)) if j else ind(r("xw%d" % h, ALL), c("off%d" % h, 16, 24))
        cp(cand("xc", h, m0, m1), x, 2.0, "va")

    def s_sp(v, h, j):
        m0, m1 = P["runs"][h][j]
        xb = ind(XW, c("bo%d" % h, 8 * m0 - 8, 8 * m1 - 8)) if j else ind(r("xw%d" % h, ALL), c("off%d" % h, 24, 32))
        tt(cand("sp", h, m0, m1), xb, cand("xc", h, m0, m1), ALU.subtract)

    def s_px(v, h, j):
        if "v" in P["am"][h]:
            mms([(c("px", 128 * m, 128 * m + 128), [(NHALF, cand("xc", h, -2, -1))]) for m in range(4)])

    def s_E(v, h, j):
        m0, m1 = P["blocks"][h][j]
        x1, x2 = cand("xc", h, -2, -1), cand("xc", h, -1, 0)
        one = lambda name, m: cand(name, h, m, m + 1)
        part = lambda pb, a, b: r(pb, S(2 * (a - m0), 2 * (b - m0)), ALL, ALL)
        if j == 0:
            pb = next_bank()
            mms([(part(pb, 0, 1), [(HALF, x1), (ONE, one("sp", 0))]), (part(pb, 1, 2), [(HALF, x2), (HALF, one("xc", 0)), (TWO, one("sp", 0))])])
            act(cand("own", h, 0, 2), part(pb, 0, 2), AF.Abs)
            mm(c("pq%d" % h, 128, 272, 18), [(one("own", 0), G32), (one("own", 1), G32)] + [(x1, GN16)] * ("v" in P["am"][h]))
            return
        if P["am"][h][j] == "v":
            tt(cand("am", h, m0, m1), c("px", 0, 128 * (m1 - m0)), cand("sp", h, m0, m1), ALU.max)
            first = lambda m: [(one("am", m), G64), (one("sp", m), GN32)]
        else:
            pb = next_bank()
            mms([(part(pb, m, m + 1), [(HALF, x1), (ONE, one("sp", m))]) for m in range(m0, m1)])
            act(cand("am", h, m0, m1), part(pb, m0, m1), AF.Abs)
            first = lambda m: [(one("am", m), G32)] + [(x1, GN16)] * ("v" in P["am"][h])
        pb = next_bank()
        mms([(part(pb, m, m + 1), [(HALF, x2), (HALF, one("xc", m)), (TWO, one("sp", m))]) for m in range(m0, m1)])
        act(cand("ab", h, m0, m1), part(pb, m0, m1), AF.Abs)
        mms([(c("pq%d" % h, 128 + m, 272, 18), first(m) + [(one("ab", m), G32)]) for m in range(m0, m1)])

    def s_win(v, h, j):
        H = str(h)
        mq = c("won", 8 * h, 8 * h + 8)
        scan(r("sc" + H, ALL), c("pq" + H, 128, 272), r("dE", ALL), ALU.min, ALU.add, FAR)
        ts(mq, c("sc" + H, 16, 144, 18), 31, None, ALU.bitwise_and)
        tt(r("lw" + H, ALL), ind(mq, EXP), DIAG, ALU.mult)
        mm(c("pq" + H, 0, 16), [(r("lw" + H, ALL), r("TS", 0, ALL)), (ONE, r("TS", 1, ALL))])
        aff(c("wo" + H, 0, 16), c("pq" + H, 0, 16), 1.0, 0.0)

    def s_mid(v, h, j):
        H = str(h)
        tt(r("mid" + H, ALL), ind(cand("xc", h, 0, 17), c("wo" + H, 0, 8)), cand("xc", h, -2, -1), ALU.add)
        aff(r("mid" + H, ALL), r("mid" + H, ALL), 0.25, -0.25)

    def s_cw(v, h, j):
        H = str(h)
        tt(c("cm" + H, 0, 128), ind(r("ct" + H, ALL), c("wo" + H, 8, 16)), DIAG, ALU.mult)
        scan(c("cm" + H, 128, 256), r("rs16", ALL), c("cm" + H, 0, 128), ALU.mult, ALU.add)
        aff(c("wo" + H, 16, 24), c("cm" + H, 143, 256, 16), 1.0, 0.0)

    def s_nam(v, h, j):
        H = str(h)
        cw = c("wo" + H, 16, 24)
        tt(nm(h, 3), ind(QX, cw), nm(h, 1), ALU.min)
        aff(c("pq" + H, 272, 400), nm(h, 3), 32.0, 32 * QSH)
        tt(ni(h, 0), ind(IX, cw), nm(h, 2), ALU.mult)
        tt(ni(h, 1), c("pq" + H, 272, 400), ni(h, 0), ALU.add)
        ts(ni(h, 1), ni(h, 1), 5, 4095, ALU.arith_shift_right, ALU.bitwise_and)
        if v < NV - 1:
            sb = c("s16", 256 * v + 128 * h, 256 * v + 128 * h + 128)
            if P["s16"][h] == "g":
                gcp(sb, ni(h, 1))
            else:
                aff(sb, ni(h, 1), 1.0, 0.0)
            land, sem = old_names(v + 1, h), "ar%d%d" % (v + 1, h)
            i = add("send", (land, sb, sem), {"g": (300.0, 0, "")}, [sb], [land])
            ops[i]["sem"] = (sem, None)
            ops[i]["done"] = None
        else:
            gcp(c("yrf", 128 * h, 128 * h + 128), ni(h, 1))
            dma("s", c("yrf", 128 * h, 128 * h + 128), "yr", S(128 * h, 128 * h + 128), "or" + H, 16)

    def s_no(v, h, j):
        if v < NV - 1:
            ts(r("ne", ALL), r("ui", ALL), 15, None, ALU.bitwise_and)
            tt(r("no", ALL), r("ne", ALL), r("nb", ALL), ALU.add)
        else:
            out, ei = r(next_bank(), 0, 0, ALL), r("ei", ALL)
            mm(out, [(zr(3, t), c("xc%d" % (t // 8), 256 + 16 * (t % 8), 272 + 16 * (t % 8))) for t in range(16)])
            cp(ei, out)
            ts(ei, ei, 15, None, ALU.bitwise_and)
            tt(r("eq", 0, ALL), ind(ei, REP16), r("ec", ALL), ALU.is_equal)
            act(r("eq", 1, ALL), r("eq", 0, ALL), AF.Identity, bias=1.0, scale=-1.0)

    def s_stx(v, h, j):
        if v < NV - 1:
            cp(ind(XW, c("no", 8 * h, 8 * h + 8)), r("mid%d" % h, ALL))
        else:
            aff(r("nw", 1, S(128 * h, 128 * h + 128)), r("mid%d" % h, ALL), 1.0, 0.0)
            new_sums(h, 1)

    def s_s2(v, h, j):
        if v == NV - 1:
            aff(r("nw", 0, S(128 * h, 128 * h + 128)), ni(h, 1), 1.0, -QSH)
            new_sums(h, 0)

    def s_stq(v, h, j):
        if v < NV - 1:
            aff(r("nw", 0, ALL), c("s16", 256 * v, 256 * v + 256), 1.0, -QSH)
            cp(ind(QW, r("no", ALL)), r("nw", 0, ALL))

    def s_cnt(v, h, j):
        if v < NV - 1:
            out = r(next_bank(), 0, 0, ALL)
            act(r("sg", ALL), r("won", ALL), AF.Sign)
            mm(out, [(r("one", ALL), r("sg", ALL))])
            act(r("junk", ALL), out, AF.Identity, bias=-0.375 / 16, acc=AC)

    def new_sums(h, a):
        out, new, f = r(next_bank(), 0, 0, ALL), c("nsb", 16 * a, 16 * a + 16), r("fin", a, ALL)
        mm(out, [(zr(2, t), r("nw", a, S(16 * t, 16 * t + 16))) for t in range(8 * h, 8 * h + 8)])
        if h == 0:
            aff(new, out, 1.0, 136 * QSH if a == 0 else 0.0)
            return
        tt(new, out, new, ALU.add)
        tt(f, ind(new, REP16), r("eq", 0, ALL), ALU.mult)
        tt(f, c("pq0", 256 * a, 256 * a + 256), f, ALU.add)
        dma("s", f, ("yq", "yx")[a], ALL, ("oq", "ox")[a], 16)

    def s_qh(v, h, j):
        if v == NV - 1:
            for a in range(0, 4096, 256):
                gcp(c("Qh", a, a + 256), c("Qw", a, a + 256))

    def s_old(v, h, a):
        if v == NV - 1:
            pb = next_bank()
            for q in range(4):
                mm(r(pb, q, ALL, ALL), [(zr(2, t), c(("Qh", "X")[a], 256 * t + 64 * q, 256 * t + 64 * q + 64)) for t in range(16)])
            act(r("pre", a, ALL), r(pb, S(0, 4), ALL, ALL), AF.Identity, bias=136 * QSH if a == 0 else 0.0)

    def s_clr(v, h, a):
        if v == NV - 1:
            tt(c("pq0", 256 * a, 256 * a + 256), r("pre", a, ALL), r("eq", 1, ALL), ALU.mult)

    table = {"cv": s_cv, "xs": s_xs, "D": s_D, "p": s_p, "ws": s_ws, "xw": s_xw, "in": s_in, "u": s_u, "mk": s_mk, "x12": s_x12, "an": s_an, "b": s_b,
             "pre": s_pre, "xc": s_xc, "sp": s_sp, "px": s_px, "E": s_E, "win": s_win, "mid": s_mid, "cw": s_cw, "nam": s_nam,
             "no": s_no, "stx": s_stx, "s2": s_s2, "stq": s_stq, "cnt": s_cnt, "qh": s_qh, "old": s_old, "clr": s_clr, "set": s_set}
    steps = steps or ORDER
    names = [step.lstrip("-") for step in steps]
    held = {}
    for turn in range(NV + 2):
        for step, name in zip(steps, names):
            v = turn - (len(step) - len(name))
            if not 0 <= v < NV:
                continue
            if (name, v) not in held:
                key = max((k for k in table if name.startswith(k)), key=len)
                h, j = (int(x) for x in (name[len(key):] + "0")[:2])
                now[:] = [name, 2 * v + h]
                n = len(ops)
                table[key](v, h, j)
                held[name, v] = [names.count(name), ops[n:]]
                del ops[n:]
            left, calls = held[name, v]
            n = 1 if left > 1 else len(calls)
            ops.extend(calls[:n])
            held[name, v] = [left - 1, calls[n:]]
    return ops


def depend(ops):
    hist, deps = {}, []
    for i, op in enumerate(ops):
        d = {}
        acc = [(x, False) for x in op["R"]] + [(x, True) for x in op["W"]]
        op["B"] = sorted({x[0] for x, _ in acc if _psum(x)})
        for x, wr in acc:
            lo, hi, _ = _span(x)
            ps, m = _psum(x), _bits(x)
            for (j, a, b, w, m2) in hist.get(x[0], []):
                if a < hi and lo < b and (wr or w) and j != i and (m & m2 or not ps):
                    d[j] = d.get(j, False) or bool(m & m2)
        for x, wr in acc:
            lo, hi, _ = _span(x)
            h, m = hist.setdefault(x[0], []), _bits(x)
            if wr:
                h[:] = [e for e in h if e[4] & ~m]
            h.append((i, lo, hi, wr, m))
        deps.append(d)
    return deps


def _lag(op):
    return {"send": HOP, "dma": 2200.0, "move": 4500.0}.get(op["k"], 0.0)


def place(ops, deps, rank=None, eng=None):
    n = len(ops)
    rank = rank or range(n)
    eng = eng or [next(iter(op["c"])) for op in ops]
    succ, left = [[] for _ in ops], [len(d) for d in deps]
    for i, d in enumerate(deps):
        for j in d:
            succ[j].append(i)
    uses = {}
    for op in ops:
        for b in op["B"]:
            uses[b] = uses.get(b, 0) + 1
    lent, idle, last = {}, ["pb%d" % b for b in range(NB)], {}
    free, order = {e: 0.0 for e in "vapgs"}, {e: [] for e in "vapgs"}
    start, end = [0.0] * n, [0.0] * n
    ready = {i: 0.0 for i in range(n) if not left[i]}
    firm = {e: sorted((i for i in range(n) if eng[i] == e and ops[i]["t"] + e in FIRM),
                      key=lambda x: rank[x], reverse=True) for e in free}

    def after(j, e, raw):
        return end[j] + (LAT_X if eng[j] != e or "sem" in ops[j] else LAT_S if raw else 0.0)

    while ready:
        can = {}
        for i, s in ready.items():
            if firm[eng[i]] and rank[firm[eng[i]][-1]] < rank[i]:
                continue
            for b in ops[i]["B"]:
                b = lent.get(b) or (b if b[:2] != "pb" else idle[0] if idle else None)
                s = max(s, after(last[b], eng[i], False) if b in last else 0.0) if b else 1e18
            can[i] = max(s, free[eng[i]])
        first = min(can, key=can.get)
        e = eng[first]
        i = min((x for x in can if eng[x] == e and can[x] <= can[first] + SLACK), key=lambda x: rank[x])
        del ready[i]
        if i in firm[e][-1:]:
            firm[e].pop()
        op = ops[i]
        for b in op["B"]:
            if b[:2] == "pb" and b not in lent:
                lent[b] = idle.pop(0)
            real = lent.get(b, b)
            if real in last:
                deps[i].setdefault(last[real], False)
            last[real] = i
            uses[b] -= 1
            if b[:2] == "pb" and not uses[b]:
                idle.append(real)
        start[i] = can[i]
        free[e] = end[i] = can[i] + op["c"][e]
        if "sem" in op:
            end[i] = end[i] + op["done"] if op["k"] == "dma" and e == "g" else op["done"] or end[i] + _lag(op)
        order[e].append(i)
        for j in succ[i]:
            left[j] -= 1
            if not left[j]:
                ready[j] = max(after(x, eng[j], raw) for x, raw in deps[j].items())
    return eng, order, start, end, lent


def waits(ops, deps, eng, order, start):
    pos = {i: p for e in order for p, i in enumerate(order[e])}
    know = {e: {} for e in order}
    seen, need, marked = {}, {}, set()
    for i in sorted(range(len(ops)), key=lambda x: (start[x], pos[x])):
        e, w = eng[i], []
        kn = know[e]
        for j in sorted(deps[i], key=lambda x: -start[x]):
            key, val = (ops[j]["sem"][0], 0) if "sem" in ops[j] else (eng[j], pos[j])
            if key == e and not deps[i][j]:
                continue
            if kn.get(key, -1) >= val:
                continue
            w.append(j)
            marked.add(j)
            for k2, v2 in ([] if ops[j]["k"] == "send" else list(seen[j].items())) + [(key, val)]:
                kn[k2] = max(kn.get(k2, -1), v2)
        need[i] = w
        seen[i] = dict(kn)
    count, total = {}, {}
    for e in COUNTER:
        m = 0
        last = [i for i in order[e] if "sem" not in ops[i]][-1]
        marked.add(last)
        for i in order[e]:
            if i in marked and "sem" not in ops[i]:
                m += 1
                count[i] = m
        total[e] = m
    return need, count, total


_PLAN = {}


def plan():
    if not _PLAN:
        ops = build()
        deps = depend(ops)
        eng, order, start, end, lent = place(ops, deps)
        _PLAN["p"] = (ops, eng, order, lent) + waits(ops, deps, eng, order, start)
    return _PLAN["p"]


def rank_program(g, core, T, topo):
    rank = T.rank_of(core)
    if rank is None:
        return
    ops, eng, order, lent, need, count, total = plan()
    nxt = T.cores[(rank + 1) % len(T.cores)]
    prv = T.cores[(rank - 1) % len(T.cores)]
    rid, pid = topo.addr(nxt)[:2]
    mask = topo.mask(core, nxt)
    arrive = len(topo.engines(prv, core))
    Q = {"v": g.vector, "a": g.scalar, "p": g.tensor, "g": g, "s": g.sync}

    def ap(x):
        if not isinstance(x, tuple):
            return x
        a = T[lent.get(x[0], x[0])][(slice(None),) + tuple(x[1])]
        return a if x[2] is None else a.indirect(ap(x[2]))

    sends = 0
    for e in "sgvap":
        q = Q[e]
        for i in order[e]:
            op, a = ops[i], ops[i]["a"]
            for j in need[i]:
                if "sem" in ops[j]:
                    q.wait_ge(T.sem[ops[j]["sem"][0]], ops[j]["sem"][1] or arrive)
                else:
                    q.wait_ge(T.sem[COUNTER[eng[j]]], count[j])
            k = op["k"]
            if k == "cp" and e == "a":
                ins = q.activation(ap(a[0]), ap(a[1]), AF.Copy, scale=a[2])
            elif k == "cp" and a[2] == 1.0:
                ins = q.tensor_copy(ap(a[0]), ap(a[1]))
            elif k == "cp":
                ins = q.tensor_scalar(ap(a[0]), ap(a[1]), a[2], None, ALU.mult)
            elif k == "gcp":
                ins = q.affine_select(ap(a[0]), ap(a[1]), [[0, _n(a[0])]], ALU.is_ge, 0.0, 0, 0)
            elif k == "move":
                q.dma_start(ap(a[0]), ap(a[1])).then_inc(T.sem[op["sem"][0]], 16)
            elif k == "aff" and e == "a":
                ins = q.activation(ap(a[0]), ap(a[1]), AF.Identity, bias=ap(a[3]), scale=a[2])
            elif k == "aff" and a[2] == 1.0 and a[3] == 0.0:
                ins = q.tensor_copy(ap(a[0]), ap(a[1]))
            elif k == "aff":
                ins = q.tensor_scalar(ap(a[0]), ap(a[1]), a[2], ap(a[3]), ALU.mult, ALU.add)
            elif k == "tt":
                ins = q.tensor_tensor(ap(a[0]), ap(a[1]), ap(a[2]), a[3])
            elif k == "ts" and a[5] is None:
                ins = q.tensor_scalar(ap(a[0]), ap(a[1]), ap(a[2]), None, a[4])
            elif k == "ts":
                ins = q.tensor_scalar(ap(a[0]), ap(a[1]), ap(a[2]), ap(a[3]), a[4], a[5])
            elif k == "scan":
                ins = q.tensor_tensor_scan(ap(a[0]), ap(a[1]), ap(a[2]), a[5], a[3], a[4])
            elif k == "ms":
                ins = q.memset(ap(a[0]), a[1])
            elif k == "act" and a[5] is None:
                ins = q.activation(ap(a[0]), ap(a[1]), a[2], bias=a[3], scale=a[4])
            elif k == "act":
                ins = q.activation(ap(a[0]), ap(a[1]), a[2], bias=a[3], scale=a[4], accum_out=ap(a[5]))
            elif k == "mm":
                for out, terms in a:
                    for t, (l, rh) in enumerate(terms):
                        ins = q.matmul(ap(out), ap(l), ap(rh), t == 0, t == len(terms) - 1)
            elif k == "iota" and SCRATCH[a[0][0]][2] == I32:
                ins = q.iota(ap(a[0]), a[1], a[2], a[3])
            elif k == "iota":
                ins = q.iota(ap(a[0]), a[1], a[2], a[3], allow_small_or_imprecise_dtypes=True)
            elif k == "asel":
                ins = q.affine_select(ap(a[0]), ap(a[1]), a[2], a[3], 0.0, a[4], a[5])
            elif k == "dma" and e == "g":
                q.dma_start(ap(a[0]), T[a[1]][:], allow_slow_non_contiguous=True).then_inc(T.sem[a[3]], 16)
            elif k == "dma" and a[4]:
                q.dma_start(ap(a[0]), T[a[1]][:, a[2]]).then_inc(T.sem[a[3]], 16)
            elif k == "dma":
                q.dma_start(T[a[1]][:, a[2]], ap(a[0])).then_inc(T.sem[a[3]], 16)
            else:
                g.remote_dma(ap(a[0]), ap(a[1]), T.sem[a[2]], T.sem.sent, pid, rid, mask)
                sends += 1
            if i in count:
                ins.then_inc(T.sem[COUNTER[e]], 1)
        if e == "g":
            g.wait_ge(T.sem.sent, sends * len(topo.engines(core, nxt)))
            for e2 in "vapg":
                g.wait_ge(T.sem[COUNTER[e2]], total[e2])
            for name in OUTS:
                g.wait_ge(T.sem[name], 16)
